import numpy as np
import ml_dtypes


def mxq(x, axis, fmt="e4m3"):
    dtype, down = {"e4m3": (ml_dtypes.float8_e4m3fn, 7), "e5m2": (ml_dtypes.float8_e5m2, 14)}[fmt]
    v = np.moveaxis(np.asarray(x, np.float32).astype(ml_dtypes.bfloat16).astype(np.float64), axis, -1)
    blocks = v.reshape(v.shape[:-1] + (-1, 32))
    amax = np.abs(blocks).max(-1, keepdims=True)
    byte = np.maximum(np.where(amax > 0, np.frexp(amax)[1] - 1 + 127, 0) - down, 1)
    scale = np.exp2(byte - 127.0)
    codes = (blocks / scale).astype(np.float32).astype(dtype).astype(np.float64)
    return np.moveaxis((codes * scale).reshape(v.shape), -1, axis)


WIDE = False


def mx_kscale(k):
    if not WIDE:
        return np.ones(k)
    levels = np.array([10, -10, 5, -5, 0])
    if k % 512:
        return np.exp2(np.random.permutation(np.resize(levels, k // 32))).repeat(32)
    a = np.empty((k // 512, 16))
    for p in range(k // 512):
        a[p, :8] = np.random.permutation(np.resize(levels, 8))
        for g in range(8):
            far = levels[np.abs(levels - a[p, g]) >= 10]
            a[p, g + 8] = far[np.random.randint(len(far))]
    return np.exp2(a.ravel()).repeat(32)


BF16 = ml_dtypes.bfloat16


def bf(x):
    return np.asarray(x, np.float32).astype(BF16)


def f64(x):
    return np.asarray(x).astype(np.float64)

E4M3FN = np.array([(-1.0 if i & 128 else 1.0) * ((1.0 + (i & 7) / 8.0) * 2.0 ** (((i >> 3) & 15) - 7) if i & 120 else (i & 7) * 2.0 ** -9) for i in range(256)])


def e4m3fn_bytes(y):
    return np.clip(np.asarray(y, np.float64), -448.0, 448.0).astype(np.float32).astype(ml_dtypes.float8_e4m3fn).view(np.uint8)


def e4m3fn_values(b):
    return E4M3FN[b]


S, C = 2048, 512


def setup_inputs():
    t = mx_kscale(S)
    P0 = np.exp(2.0 * np.random.standard_normal((S, S)))
    P0 = P0 / P0.sum(axis=0, keepdims=True)
    P = P0 * t[:, None]
    P_scale = (np.abs(P).max(axis=1, keepdims=True) / 448.0).astype(np.float32)
    P_bytes = e4m3fn_bytes(P / f64(P_scale))
    V = 8.0 * np.random.standard_normal((S, C)) / t[:, None]
    R = 0.25 * np.random.standard_normal((S, C)) / t[:, None]
    discount = np.random.uniform(0.7, 0.99, (S, 1)) / t[:, None]
    return {"P_bytes": P_bytes, "P_scale": P_scale,
            "V": bf(V), "R": bf(R), "discount": bf(discount)}


def reference(P_bytes, P_scale, V, R, discount):
    r, g = f64(R), f64(discount)
    P = e4m3fn_values(P_bytes) * np.repeat(f64(P_scale), S, axis=1)
    p = mxq(P, 0, "e4m3")
    e1 = p.T @ mxq(f64(V), 0, "e4m3")
    v1 = r + g * e1
    e2 = p.T @ mxq(v1, 0, "e4m3")
    return r + g * e2

@@ -1,0 +1,229 @@
+from contextlib import ExitStack
+
+import concourse.mybir as mybir
+
+S, C = 2048, 512
+P = 128
+T = 4
+W = P * T
+G = S // W
+HALF = C // 2
+
+F32 = mybir.dt.float32
+BF16 = mybir.dt.bfloat16
+U32 = mybir.dt.uint32
+U8 = mybir.dt.uint8
+FP8 = mybir.dt.float8_e4m3fn
+FP8X4 = mybir.dt.float8_e4m3fn_x4
+MULT = mybir.AluOpType.mult
+ADD = mybir.AluOpType.add
+COPY = mybir.ActivationFunctionType.Copy
+
+FLOPS = 2 * 2 * S * S * C
+
+SCALAR_SLOTS = [1] + [4, 4, 3] + [4, 4, 4, 3] + [4, 4, 4, 3] + [4, 4, 4, 4]
+V_BY = "VVSV"
+V1_BY = "SSV"
+LAST_BY = "VVVSSSVS"
+
+
+def tile_two_sweep_policy_evaluation_d3_kernel(tc, P_bytes, P_scale, V, R, discount, out):
+    nc = tc.nc
+    copier = {"V": nc.vector.tensor_copy, "S": nc.scalar.copy}
+
+    with ExitStack() as ctx:
+        keep = ctx.enter_context(tc.tile_pool(name="keep", bufs=1))
+        chunks = ctx.enter_context(tc.tile_pool(name="chunks", bufs=5))
+        rows = ctx.enter_context(tc.tile_pool(name="rows", bufs=2))
+        results = ctx.enter_context(tc.tile_pool(name="results", bufs=10))
+        psum = ctx.enter_context(tc.psum_pool(name="psum", bufs=8))
+
+        scale_0 = keep.tile([P, T], F32, name="scale_0")
+        scale_rest = keep.tile([P, G - 1, T], F32, name="scale_rest")
+        disc = keep.tile([P, G, T], BF16, name="disc")
+        bytes_q = [keep.tile([P, G, T, W], U8, name=f"bytes_{q}", align_bytes=64) for q in range(2)]
+        bytes_23 = keep.tile([P, G, T, 2 * W], U8, name="bytes_23", align_bytes=64)
+        v_raw = keep.tile([P, G, T, C], BF16, name="v_raw", align_bytes=64)
+        r_sb = keep.tile([P, G, T, C], BF16, name="r_sb", align_bytes=64)
+        p_codes = keep.tile([P, G, G, W], U32, name="p_codes", align_bytes=64)
+        p_scales = keep.tile([P, G, G, W], U8, name="p_scales", align_bytes=64)
+        v_codes = [keep.tile([P, G, C], U32, name=f"v_codes_{s}", align_bytes=64) for s in range(2)]
+        v_scales = [keep.tile([P, G, C], U8, name=f"v_scales_{s}", align_bytes=64) for s in range(2)]
+
+        scale_view = P_scale.rearrange("(g p t) o -> p g (t o)", p=P, t=T)
+        p_view = P_bytes.rearrange("(g p t) i -> g p t i", p=P, t=T)
+        v_view = V.rearrange("(g p t) c -> g p t c", p=P, t=T)
+        r_view = R.rearrange("(g p t) c -> g p t c", p=P, t=T)
+        out_view = out.rearrange("(g p t) c -> g p t c", p=P, t=T)
+
+        nc.scalar.dma_start(out=scale_0[:], in_=scale_view[:, 0])
+        nc.sync.dma_start(out=bytes_q[0][:, 0], in_=p_view[0][:, :, 0:W])
+        nc.sync.dma_start(out=scale_rest[:], in_=scale_view[:, 1:])
+        nc.sync.dma_start(out=v_raw[:, 0], in_=v_view[0])
+        for g in range(1, G):
+            nc.sync.dma_start(out=bytes_q[0][:, g], in_=p_view[g][:, :, 0:W])
+            nc.sync.dma_start(out=v_raw[:, g], in_=v_view[g])
+        for g in range(G):
+            nc.sync.dma_start(out=bytes_q[1][:, g], in_=p_view[g][:, :, W : 2 * W])
+        nc.sync.dma_start(out=disc[:], in_=discount.rearrange("(g p t) o -> p g (t o)", p=P, t=T))
+        nc.sync.dma_start(out=r_sb[:, 0], in_=r_view[0])
+        for g in range(G):
+            nc.sync.dma_start(out=bytes_23[:, g], in_=p_view[g][:, :, 2 * W :])
+        for q in range(1, G):
+            nc.sync.dma_start(out=r_sb[:, q], in_=r_view[q])
+
+        wide = {}
+        mixed = {}
+        v_mixed = {}
+        v1_rows = {}
+        acc = {}
+
+        def widen(n):
+            q, g = divmod(n, G)
+            wide[n] = chunks.tile([P, T, W], BF16, name=f"wide_{n}", tag="wide", align_bytes=64)
+            for t in range(T):
+                src = bytes_q[q][:, g, t, :] if q < 2 else bytes_23[:, g, t, (q - 2) * W : (q - 1) * W]
+                scale = scale_0[:, t : t + 1] if g == 0 else scale_rest[:, g - 1, t : t + 1]
+                if t < SCALAR_SLOTS[n]:
+                    nc.scalar.activation(out=wide[n][:, t, :], in_=src.bitcast(FP8), func=COPY, scale=scale)
+                else:
+                    nc.vector.tensor_scalar(
+                        out=wide[n][:, t, :], in0=src.bitcast(FP8), scalar1=scale, scalar2=None, op0=MULT
+                    )
+
+        def interleave(n, b0, b1, copy):
+            if n not in mixed:
+                mixed[n] = chunks.tile([P, W * T], BF16, name=f"mixed_{n}", tag="mixed", align_bytes=64)
+            copy(
+                out=mixed[n][:].rearrange("p (b m e t) -> p m b e t", b=T, e=2, t=T)[:, :, b0:b1],
+                in_=wide[n][:].rearrange("p t (m e b) -> p m b e t", e=2, b=T)[:, :, b0:b1],
+            )
+
+        def quantise(n, b0, b1):
+            q, g = divmod(n, G)
+            cols = slice(b0 * P, b1 * P)
+            nc.vector.quantize_mx(
+                out=p_codes[:, q, g, cols].bitcast(FP8X4),
+                scales=p_scales[:, q, g, cols],
+                in_=mixed[n][:, b0 * P * T : b1 * P * T],
+            )
+
+        def interleave_v(sweep, g, c0, c1, copy):
+            if (sweep, g) not in v_mixed:
+                v_mixed[sweep, g] = rows.tile([P, C, T], BF16, name=f"v_mixed_{sweep}_{g}", tag="v_mixed", align_bytes=64)
+            src = v_raw[:, g] if sweep == 0 else v1_rows[g][:]
+            copy(out=v_mixed[sweep, g][:, c0:c1, :], in_=src[:, :, c0:c1].rearrange("p t c -> p c t"))
+
+        def quantise_v(sweep, g, c0, c1):
+            nc.vector.quantize_mx(
+                out=v_codes[sweep][:, g, c0:c1].bitcast(FP8X4),
+                scales=v_scales[sweep][:, g, c0:c1],
+                in_=v_mixed[sweep, g][:, c0:c1, :].rearrange("p c t -> p (c t)"),
+            )
+
+        def multiply(sweep, q, b, groups):
+            cols = slice(b * P, (b + 1) * P)
+            for g in groups:
+                if g == 0:
+                    acc[sweep, q, b] = psum.tile([P, C], F32, name=f"acc_{sweep}_{q}_{b}", tag="bank")
+                nc.tensor.matmul_mx(
+                    out=acc[sweep, q, b][:],
+                    lhsT=p_codes[:, q, g, cols].bitcast(FP8X4),
+                    lhsT_scale=p_scales[:, q, g, cols],
+                    rhs=v_codes[sweep][:, g, :].bitcast(FP8X4),
+                    rhs_scale=v_scales[sweep][:, g, :],
+                    start=(g == 0),
+                    stop=(g == G - 1),
+                )
+
+        def update(dst, sweep, q, b, c0, c1):
+            nc.vector.scalar_tensor_tensor(
+                out=dst[:, c0:c1],
+                in0=acc[sweep, q, b][:, c0:c1],
+                scalar=disc[:, q, b : b + 1],
+                in1=r_sb[:, q, b, c0:c1],
+                op0=MULT,
+                op1=ADD,
+            )
+
+        def update_v1(q, b, c0, c1):
+            if q not in v1_rows:
+                v1_rows[q] = rows.tile([P, T, C], BF16, name=f"v1_rows_{q}", tag="v1_rows", align_bytes=64)
+            update(v1_rows[q][:, b, :], 0, q, b, c0, c1)
+
+        def finish(q, b, pieces):
+            result = results.tile([P, C], F32, name=f"result_{q}_{b}", tag="result")
+            for k in range(pieces):
+                c0, c1 = k * C // pieces, (k + 1) * C // pieces
+                update(result, 1, q, b, c0, c1)
+                nc.sync.dma_start(out=out_view[q][:, b, c0:c1], in_=result[:, c0:c1])
+
+        widen(0)
+        interleave_v(0, 0, 0, C, copier[V_BY[0]])
+        widen(1)
+        interleave(0, 0, T, nc.vector.tensor_copy)
+        quantise_v(0, 0, 0, C)
+        interleave_v(0, 1, 0, C, copier[V_BY[1]])
+        widen(2)
+        last = (G - 1) * G
+        for n in range(last):
+            q, g = divmod(n, G)
+            if n + 1 < last:
+                interleave(n + 1, 0, T, nc.vector.tensor_copy)
+            quantise(n, 0, T)
+            if q >= 1 and g == 0:
+                for b in range(T):
+                    update_v1(q - 1, b, 0, C)
+            widen(n + 3)
+            if 1 <= n < G:
+                quantise_v(0, n, 0, C)
+                if n + 1 < G:
+                    interleave_v(0, n + 1, 0, C, copier[V_BY[n + 1]])
+            if q >= 1 and g == 1:
+                interleave_v(1, q - 1, 0, C, copier[V1_BY[q - 1]])
+            if q >= 1 and g == 2:
+                quantise_v(1, q - 1, 0, C)
+            for b in range(T):
+                multiply(0, q, b, [g])
+
+        interleave(last, 0, 2, copier[LAST_BY[0]])
+        widen(last + 3)
+        for k in range(2 * G):
+            h, g = divmod(k, G)
+            if k + 1 < 2 * G:
+                h_next, g_next = divmod(k + 1, G)
+                interleave(last + g_next, 2 * h_next, 2 * h_next + 2, copier[LAST_BY[k + 1]])
+            quantise(last + g, 2 * h, 2 * h + 2)
+            if k == 0:
+                for b in range(T):
+                    update_v1(G - 2, b, 0, C)
+            if k == 1:
+                interleave_v(1, G - 2, 0, C, copier[V1_BY[G - 2]])
+            if k == 2:
+                quantise_v(1, G - 2, 0, C)
+            if k == 5:
+                update_v1(G - 1, 0, 0, C)
+                update_v1(G - 1, 1, 0, C)
+            for b in (2 * h, 2 * h + 1):
+                multiply(0, G - 1, b, [g])
+            if h == 0:
+                multiply(1, 0, g, [0, 1])
+            if k in (4, 5):
+                multiply(1, 0, k - 4, [2])
+
+        for c0 in (0, HALF):
+            for b in (2, 3):
+                update_v1(G - 1, b, c0, c0 + HALF)
+        for b in (2, 3):
+            multiply(1, 0, b, [2])
+        for b in range(T):
+            multiply(1, 1, b, [0, 1, 2])
+        interleave_v(1, G - 1, 0, HALF, nc.scalar.copy)
+        interleave_v(1, G - 1, HALF, C, nc.vector.tensor_copy)
+        for c0 in (0, HALF):
+            quantise_v(1, G - 1, c0, c0 + HALF)
+
+        for q in range(G):
+            for b in range(T):
+                multiply(1, q, b, [G - 1] if q < 2 else range(G))
+                finish(q, b, 2 if (q, b) == (G - 1, T - 1) else 1)

@@ -95,8 +95,8 @@ def tile_two_sweep_policy_evaluation_d3_kernel(tc, P_bytes, P_scale, V, R, disco
             if n not in mixed:
                 mixed[n] = chunks.tile([P, W * T], BF16, name=f"mixed_{n}", tag="mixed", align_bytes=64)
             copy(
-                out=mixed[n][:].rearrange("p (b m e t) -> p m b e t", b=T, e=2, t=T)[:, :, b0:b1],
-                in_=wide[n][:].rearrange("p t (m e b) -> p m b e t", e=2, b=T)[:, :, b0:b1],
+                out=mixed[n][:].rearrange("p (b m t) -> p m t b", b=T, t=T)[:, :, :, b0:b1],
+                in_=wide[n][:].rearrange("p t (m b) -> p m t b", b=T)[:, :, :, b0:b1],
             )
 
         def quantise(n, b0, b1):
@@ -112,7 +112,10 @@ def tile_two_sweep_policy_evaluation_d3_kernel(tc, P_bytes, P_scale, V, R, disco
             if (sweep, g) not in v_mixed:
                 v_mixed[sweep, g] = rows.tile([P, C, T], BF16, name=f"v_mixed_{sweep}_{g}", tag="v_mixed", align_bytes=64)
             src = v_raw[:, g] if sweep == 0 else v1_rows[g][:]
-            copy(out=v_mixed[sweep, g][:, c0:c1, :], in_=src[:, :, c0:c1].rearrange("p t c -> p c t"))
+            copy(
+                out=v_mixed[sweep, g][:, c0:c1, :].rearrange("p (c i) t -> p c t i", i=4),
+                in_=src[:, :, c0:c1].rearrange("p t (c i) -> p c t i", i=4),
+            )
 
         def quantise_v(sweep, g, c0, c1):
             nc.vector.quantize_mx(

@@ -1,6 +1,7 @@
 from contextlib import ExitStack
 
 import concourse.mybir as mybir
+from concourse.masks import make_identity
 
 S, C = 2048, 512
 P = 128
@@ -21,10 +22,28 @@ COPY = mybir.ActivationFunctionType.Copy
 
 FLOPS = 2 * 2 * S * S * C
 
-SCALAR_SLOTS = [1] + [4, 4, 3] + [4, 4, 4, 3] + [4, 4, 4, 3] + [4, 4, 4, 4]
-V_BY = "VVSV"
-V1_BY = "SSV"
-LAST_BY = "VVVSSSVS"
+V_SLOTS = [3, 2, 1, 1] + [1, 1, 1, 1] + [1, 1, 1, 0] + [0, 0, 0, 0]
+LEAD = 3
+V_FIRST = False
+TURN_P = (7, 9, 11)
+TURN_V_AT = (0, 1, 2, 3)
+IL_V_AT = {}
+QV_AT = (1, 2, 3, 4)
+TURN_V1 = ()
+V1_S = ()
+IL_S = ()
+TURN_BANKS = (4, 5, 6, 7)
+EV_AFTER = 2
+EV_V = 3
+UPD = (1, 1, 0)
+V1_AT = (2, 2, 1)
+QV1_AT = (3, 7)
+MX_AT = {2: [0], 3: [1, 2], 4: [3], 6: [4, 5], 7: [6, 7], 10: [8, 9, 10], 11: [11]}
+EARLY_AT = {11: [(0, [0, 1]), (1, [0, 1]), (2, [0, 1]), (3, [0, 1])]}
+EXIT_AT = {}
+EXITS = 2
+ADD_FIRST = 1
+SPLIT = 256
 
 
 def tile_two_sweep_policy_evaluation_d3_kernel(tc, P_bytes, P_scale, V, R, discount, out):
@@ -34,13 +53,15 @@ def tile_two_sweep_policy_evaluation_d3_kernel(tc, P_bytes, P_scale, V, R, disco
     with ExitStack() as ctx:
         keep = ctx.enter_context(tc.tile_pool(name="keep", bufs=1))
         chunks = ctx.enter_context(tc.tile_pool(name="chunks", bufs=5))
-        rows = ctx.enter_context(tc.tile_pool(name="rows", bufs=2))
+        rows = ctx.enter_context(tc.tile_pool(name="rows", bufs=3))
         results = ctx.enter_context(tc.tile_pool(name="results", bufs=10))
-        psum = ctx.enter_context(tc.psum_pool(name="psum", bufs=8))
+        psum = ctx.enter_context(tc.psum_pool(name="psum", bufs=1))
+        ctx.enter_context(tc.manual_schedule())
 
         scale_0 = keep.tile([P, T], F32, name="scale_0")
         scale_rest = keep.tile([P, G - 1, T], F32, name="scale_rest")
         disc = keep.tile([P, G, T], BF16, name="disc")
+        disc32 = keep.tile([P, G, T], F32, name="disc32")
         bytes_q = [keep.tile([P, G, T, W], U8, name=f"bytes_{q}", align_bytes=64) for q in range(2)]
         bytes_23 = keep.tile([P, G, T, 2 * W], U8, name="bytes_23", align_bytes=64)
         v_raw = keep.tile([P, G, T, C], BF16, name="v_raw", align_bytes=64)
@@ -50,21 +71,29 @@ def tile_two_sweep_policy_evaluation_d3_kernel(tc, P_bytes, P_scale, V, R, disco
         v_codes = [keep.tile([P, G, C], U32, name=f"v_codes_{s}", align_bytes=64) for s in range(2)]
         v_scales = [keep.tile([P, G, C], U8, name=f"v_scales_{s}", align_bytes=64) for s in range(2)]
 
+        identity = keep.tile([P, P], BF16, name="identity")
+        make_identity(nc, identity[:])
+
         scale_view = P_scale.rearrange("(g p t) o -> p g (t o)", p=P, t=T)
         p_view = P_bytes.rearrange("(g p t) i -> g p t i", p=P, t=T)
         v_view = V.rearrange("(g p t) c -> g p t c", p=P, t=T)
         r_view = R.rearrange("(g p t) c -> g p t c", p=P, t=T)
         out_view = out.rearrange("(g p t) c -> g p t c", p=P, t=T)
 
+        def load_bytes(q, g):
+            nc.sync.dma_start(out=bytes_q[q][:, g], in_=p_view[g][:, :, q * W : (q + 1) * W])
+
         nc.scalar.dma_start(out=scale_0[:], in_=scale_view[:, 0])
-        nc.sync.dma_start(out=bytes_q[0][:, 0], in_=p_view[0][:, :, 0:W])
+        load_bytes(0, 0)
         nc.sync.dma_start(out=scale_rest[:], in_=scale_view[:, 1:])
+        load_bytes(0, 1)
         nc.sync.dma_start(out=v_raw[:, 0], in_=v_view[0])
+        load_bytes(0, 2)
+        load_bytes(0, 3)
         for g in range(1, G):
-            nc.sync.dma_start(out=bytes_q[0][:, g], in_=p_view[g][:, :, 0:W])
             nc.sync.dma_start(out=v_raw[:, g], in_=v_view[g])
-        for g in range(G):
-            nc.sync.dma_start(out=bytes_q[1][:, g], in_=p_view[g][:, :, W : 2 * W])
+            load_bytes(1, g - 1)
+        load_bytes(1, G - 1)
         nc.sync.dma_start(out=disc[:], in_=discount.rearrange("(g p t) o -> p g (t o)", p=P, t=T))
         nc.sync.dma_start(out=r_sb[:, 0], in_=r_view[0])
         for g in range(G):
@@ -76,15 +105,18 @@ def tile_two_sweep_policy_evaluation_d3_kernel(tc, P_bytes, P_scale, V, R, disco
         mixed = {}
         v_mixed = {}
         v1_rows = {}
+        turned = {}
+        parked = {}
         acc = {}
 
-        def widen(n):
+        def widen(n, slots, engine):
             q, g = divmod(n, G)
-            wide[n] = chunks.tile([P, T, W], BF16, name=f"wide_{n}", tag="wide", align_bytes=64)
-            for t in range(T):
+            if n not in wide:
+                wide[n] = chunks.tile([P, T, W], BF16, name=f"wide_{n}", tag="wide", align_bytes=64)
+            for t in slots:
                 src = bytes_q[q][:, g, t, :] if q < 2 else bytes_23[:, g, t, (q - 2) * W : (q - 1) * W]
                 scale = scale_0[:, t : t + 1] if g == 0 else scale_rest[:, g - 1, t : t + 1]
-                if t < SCALAR_SLOTS[n]:
+                if engine == "S":
                     nc.scalar.activation(out=wide[n][:, t, :], in_=src.bitcast(FP8), func=COPY, scale=scale)
                 else:
                     nc.vector.tensor_scalar(
@@ -97,6 +129,35 @@ def tile_two_sweep_policy_evaluation_d3_kernel(tc, P_bytes, P_scale, V, R, disco
             copy(
                 out=mixed[n][:].rearrange("p (b m t) -> p m t b", b=T, t=T)[:, :, :, b0:b1],
                 in_=wide[n][:].rearrange("p t (m b) -> p m t b", b=T)[:, :, :, b0:b1],
+            )
+
+        def turn(planes, h, name):
+            bank = psum.tile([P, 2 * W], BF16, name=f"turn_{name}_{h}", tag=f"bank_{TURN_BANKS[len(turned) % len(TURN_BANKS)]}")
+            turned[name, h] = bank
+            for j in range(2):
+                first = (2 * h + j) * P
+                nc.tensor.matmul(
+                    out=bank[:].rearrange("p (j c t) -> p j t c", j=2, t=T)[:, j],
+                    lhsT=identity[:],
+                    rhs=planes[:, :, first : first + P],
+                    start=True,
+                    stop=True,
+                )
+
+        def empty_p(n, h):
+            if n not in mixed:
+                mixed[n] = chunks.tile([P, W * T], BF16, name=f"mixed_{n}", tag="mixed", align_bytes=64)
+            nc.scalar.copy(
+                out=mixed[n][:].bitcast(F32).rearrange("p (b m w) -> p b m w", b=T, w=2)[:, :, h * 64 : (h + 1) * 64],
+                in_=turned[f"p{n}", h][:].bitcast(F32).rearrange("p (m b w) -> p b m w", b=T, w=2),
+            )
+
+        def empty_v(sweep, g, h):
+            if (sweep, g) not in v_mixed:
+                v_mixed[sweep, g] = rows.tile([P, C, T], BF16, name=f"v_mixed_{sweep}_{g}", tag="v_mixed", align_bytes=64)
+            nc.scalar.copy(
+                out=v_mixed[sweep, g][:].rearrange("p c t -> p (c t)").bitcast(F32)[:, h * W : (h + 1) * W],
+                in_=turned[f"v{sweep}{g}", h][:].bitcast(F32),
             )
 
         def quantise(n, b0, b1):
@@ -124,27 +185,28 @@ def tile_two_sweep_policy_evaluation_d3_kernel(tc, P_bytes, P_scale, V, R, disco
                 in_=v_mixed[sweep, g][:, c0:c1, :].rearrange("p c t -> p (c t)"),
             )
 
-        def multiply(sweep, q, b, groups):
+        def multiply(sweep, q, b, groups, bank=None, close=G - 1):
             cols = slice(b * P, (b + 1) * P)
             for g in groups:
-                if g == 0:
-                    acc[sweep, q, b] = psum.tile([P, C], F32, name=f"acc_{sweep}_{q}_{b}", tag="bank")
+                if bank is not None and g == groups[0]:
+                    acc[sweep, q, b] = psum.tile([P, C], F32, name=f"acc_{sweep}_{q}_{b}", tag=f"bank_{bank}")
                 nc.tensor.matmul_mx(
                     out=acc[sweep, q, b][:],
                     lhsT=p_codes[:, q, g, cols].bitcast(FP8X4),
                     lhsT_scale=p_scales[:, q, g, cols],
                     rhs=v_codes[sweep][:, g, :].bitcast(FP8X4),
                     rhs_scale=v_scales[sweep][:, g, :],
-                    start=(g == 0),
-                    stop=(g == G - 1),
+                    start=(bank is not None and g == groups[0]),
+                    stop=(g == close),
                 )
 
         def update(dst, sweep, q, b, c0, c1):
+            addend = parked[q, b] if sweep == 1 and parked.get((q, b), dst) is not dst else r_sb[:, q, b]
             nc.vector.scalar_tensor_tensor(
                 out=dst[:, c0:c1],
                 in0=acc[sweep, q, b][:, c0:c1],
                 scalar=disc[:, q, b : b + 1],
-                in1=r_sb[:, q, b, c0:c1],
+                in1=addend[:, c0:c1],
                 op0=MULT,
                 op1=ADD,
             )
@@ -154,6 +216,13 @@ def tile_two_sweep_policy_evaluation_d3_kernel(tc, P_bytes, P_scale, V, R, disco
                 v1_rows[q] = rows.tile([P, T, C], BF16, name=f"v1_rows_{q}", tag="v1_rows", align_bytes=64)
             update(v1_rows[q][:, b, :], 0, q, b, c0, c1)
 
+        def leave_early(q, b):
+            parked[q, b] = results.tile([P, C], F32, name=f"parked_{q}_{b}", tag="parked", bufs=4)
+            nc.scalar.activation(out=parked[q, b][:], in_=acc[1, q, b][:], func=COPY, scale=disc32[:, q, b : b + 1])
+
+        def add_reward(q, b):
+            nc.vector.tensor_tensor(out=parked[q, b][:], in0=parked[q, b][:], in1=r_sb[:, q, b], op=ADD)
+
         def finish(q, b, pieces):
             result = results.tile([P, C], F32, name=f"result_{q}_{b}", tag="result")
             for k in range(pieces):
@@ -161,72 +230,148 @@ def tile_two_sweep_policy_evaluation_d3_kernel(tc, P_bytes, P_scale, V, R, disco
                 update(result, 1, q, b, c0, c1)
                 nc.sync.dma_start(out=out_view[q][:, b, c0:c1], in_=result[:, c0:c1])
 
-        widen(0)
-        interleave_v(0, 0, 0, C, copier[V_BY[0]])
-        widen(1)
-        interleave(0, 0, T, nc.vector.tensor_copy)
-        quantise_v(0, 0, 0, C)
-        interleave_v(0, 1, 0, C, copier[V_BY[1]])
-        widen(2)
+        def s_slots(n):
+            return list(range(T - V_SLOTS[n])) if n < G * G else []
+
+        def v_slots(n):
+            return range(T - V_SLOTS[n], T) if n < G * G else []
+
+        def passes(n):
+            q, g = divmod(n, G)
+            for b in range(T):
+                multiply(0, q, b, [g], b if g == 0 else None)
+
+        end = G * G - 1
         last = (G - 1) * G
+        early = [divmod(e, T) for e in range(16)]
+        early_bank = [4, 5, 6, 7, 0, 1, 2, 3]
+        widen(0, s_slots(0), "S")
+        widen(0, v_slots(0), "V")
+        widen(1, s_slots(1), "S")
+        interleave(0, 0, T, nc.vector.tensor_copy)
+        widen(1, v_slots(1), "V")
+        if LEAD == 3:
+            widen(2, s_slots(2), "S")
+            widen(2, v_slots(2), "V")
         for n in range(last):
             q, g = divmod(n, G)
-            if n + 1 < last:
-                interleave(n + 1, 0, T, nc.vector.tensor_copy)
-            quantise(n, 0, T)
-            if q >= 1 and g == 0:
+            empties = []
+            if n in TURN_V_AT:
+                gv = TURN_V_AT.index(n)
+                for h in range(2):
+                    turn(v_raw[:, gv], h, f"v0{gv}")
+                empties = [lambda h, gv=gv: empty_v(0, gv, h)]
+            if n + 1 in TURN_P:
+                empties = [lambda h: empty_p(n + 1, h)]
+            sl = s_slots(n + LEAD)
+            if q >= 1 and g == V1_AT[q - 1] and q - 1 in V1_S:
+                interleave_v(1, q - 1, 0, C, nc.scalar.copy)
+            k = EV_V if n in TURN_V_AT else EV_AFTER
+            widen(n + LEAD, sl[:k], "S")
+            for empty in empties:
+                for h in range(2):
+                    empty(h)
+                    widen(n + LEAD, sl[k : k + 1], "S")
+                    k = k + 1
+            widen(n + LEAD, sl[k:], "S")
+            for e in EXIT_AT.get(n, []):
+                leave_early(*early[e])
+            if n == 8:
+                nc.vector.tensor_copy(out=disc32[:], in_=disc[:])
+            if V_FIRST:
+                widen(n + LEAD, v_slots(n + LEAD), "V")
+            if n + 1 not in TURN_P and n + 1 not in IL_S and n + 1 <= end:
+                interleave(n + 1, 0, T if n + 1 < last else 2, nc.vector.tensor_copy)
+            if n in IL_V_AT:
+                interleave_v(0, IL_V_AT[n], 0, C, nc.vector.tensor_copy)
+            if n < end:
+                quantise(n, 0, T)
+            else:
+                quantise(n, 0, 2)
+                quantise(n, 2, T)
+            if not V_FIRST:
+                widen(n + LEAD, v_slots(n + LEAD), "V")
+            if q >= 1 and g == V1_AT[q - 1] and q - 1 not in TURN_V1 and q - 1 not in V1_S:
+                interleave_v(1, q - 1, 0, C, nc.vector.tensor_copy)
+            if n in QV_AT:
+                quantise_v(0, QV_AT.index(n), 0, C)
+            if q >= 1 and g == UPD[q - 1]:
                 for b in range(T):
                     update_v1(q - 1, b, 0, C)
-            widen(n + 3)
-            if 1 <= n < G:
-                quantise_v(0, n, 0, C)
-                if n + 1 < G:
-                    interleave_v(0, n + 1, 0, C, copier[V_BY[n + 1]])
-            if q >= 1 and g == 1:
-                interleave_v(1, q - 1, 0, C, copier[V1_BY[q - 1]])
-            if q >= 1 and g == 2:
-                quantise_v(1, q - 1, 0, C)
-            for b in range(T):
-                multiply(0, q, b, [g])
+            if n - 4 in QV1_AT:
+                quantise_v(1, QV1_AT.index(n - 4), 0, C)
+            for m in MX_AT.get(n, []):
+                passes(m)
+            for c in TURN_P:
+                if n == max(c - 3, G - 1):
+                    for h in range(2):
+                        turn(wide[c], h, f"p{c}")
+            for e, gs in EARLY_AT.get(n, []):
+                multiply(1, *early[e], gs, early_bank[e % 8] if gs[0] == 0 else None, 1 if e < EXITS else G - 1)
 
-        interleave(last, 0, 2, copier[LAST_BY[0]])
-        widen(last + 3)
-        for k in range(2 * G):
-            h, g = divmod(k, G)
-            if k + 1 < 2 * G:
-                h_next, g_next = divmod(k + 1, G)
-                interleave(last + g_next, 2 * h_next, 2 * h_next + 2, copier[LAST_BY[k + 1]])
-            quantise(last + g, 2 * h, 2 * h + 2)
-            if k == 0:
-                for b in range(T):
-                    update_v1(G - 2, b, 0, C)
-            if k == 1:
-                interleave_v(1, G - 2, 0, C, copier[V1_BY[G - 2]])
-            if k == 2:
-                quantise_v(1, G - 2, 0, C)
-            if k == 5:
-                update_v1(G - 1, 0, 0, C)
-                update_v1(G - 1, 1, 0, C)
+        def early_passes(es, gs):
+            for e in es:
+                multiply(1, *early[e], gs, early_bank[e % 8] if gs[0] == 0 else None, 1 if e < EXITS else G - 1)
+
+        def half_passes(h, g):
             for b in (2 * h, 2 * h + 1):
-                multiply(0, G - 1, b, [g])
-            if h == 0:
-                multiply(1, 0, g, [0, 1])
-            if k in (4, 5):
-                multiply(1, 0, k - 4, [2])
+                multiply(0, G - 1, b, [g], b if g == 0 else None)
 
-        for c0 in (0, HALF):
-            for b in (2, 3):
-                update_v1(G - 1, b, c0, c0 + HALF)
-        for b in (2, 3):
-            multiply(1, 0, b, [2])
+        vcopy, scopy = nc.vector.tensor_copy, nc.scalar.copy
+        widen(end, s_slots(end), "S")
+        interleave(last + 1, 0, 2, vcopy)
+        quantise(last, 0, 2)
+        widen(end, v_slots(end), "V")
+        for e in range(EXITS):
+            leave_early(*early[e])
+        for g in range(G):
+            interleave(last + g, 2, T, scopy)
         for b in range(T):
-            multiply(1, 1, b, [0, 1, 2])
-        interleave_v(1, G - 1, 0, HALF, nc.scalar.copy)
-        interleave_v(1, G - 1, HALF, C, nc.vector.tensor_copy)
-        for c0 in (0, HALF):
-            quantise_v(1, G - 1, c0, c0 + HALF)
+            update_v1(G - 2, b, 0, C)
+        half_passes(0, 0)
+        early_passes(range(8, 8 + EXITS), [0, 1])
+        quantise(last + 1, 0, 2)
+        half_passes(0, 1)
+        interleave_v(1, G - 2, 0, C, vcopy)
+        interleave(last + 2, 0, 2, vcopy)
+        quantise_v(1, G - 2, 0, C)
+        interleave(last + 3, 0, 2, vcopy)
+        quantise(last + 2, 0, 2)
+        early_passes(list(range(EXITS, 4)), [2])
+        half_passes(0, 2)
+        quantise(last + 3, 0, 2)
+        half_passes(0, 3)
+        quantise(last, 2, T)
+        half_passes(1, 0)
+        quantise(last + 1, 2, T)
+        half_passes(1, 1)
+        early_passes(list(range(8, 8 + EXITS)), [2])
+        update_v1(G - 1, 0, 0, C)
+        update_v1(G - 1, 1, 0, C)
+        quantise(last + 2, 2, T)
+        half_passes(1, 2)
+        quantise(last + 3, 2, T)
+        half_passes(1, 3)
+        early_passes([4, 5], [0, 1, 2])
+        for e in range(ADD_FIRST):
+            add_reward(*early[e])
+        for c0, c1 in ((0, SPLIT), (SPLIT, C)):
+            for b in (2, 3):
+                update_v1(G - 1, b, c0, c1)
+        early_passes([6, 7], [0, 1, 2])
+        interleave_v(1, G - 1, 0, SPLIT, nc.scalar.copy)
+        interleave_v(1, G - 1, SPLIT, C, nc.vector.tensor_copy)
+        for c0, c1 in ((HALF, C), (0, HALF)):
+            quantise_v(1, G - 1, c0, c1)
 
-        for q in range(G):
-            for b in range(T):
-                multiply(1, q, b, [G - 1] if q < 2 else range(G))
-                finish(q, b, 2 if (q, b) == (G - 1, T - 1) else 1)
+        for e in range(ADD_FIRST, EXITS):
+            add_reward(*early[e])
+        held = list(range(EXITS, 4)) + list(range(8, 8 + EXITS)) + list(range(4, 8))
+        rest = list(range(EXITS)) + list(range(8 + EXITS, 16))
+        for e in held:
+            multiply(1, *early[e], [G - 1])
+        for e, f in zip(held, rest):
+            finish(*early[e], 1)
+            multiply(1, *early[f], [2, 3] if f < EXITS else list(range(G)), early_bank[e % 8])
+        for i, f in enumerate(rest):
+            finish(*early[f], 2 if i == 7 else 1)

@@ -42,8 +42,10 @@ MX_AT = {2: [0], 3: [1, 2], 4: [3], 6: [4, 5], 7: [6, 7], 10: [8, 9, 10], 11: [1
 EARLY_AT = {11: [(0, [0, 1]), (1, [0, 1]), (2, [0, 1]), (3, [0, 1])]}
 EXIT_AT = {}
 EXITS = 2
-ADD_FIRST = 1
+ADD_FIRST = 0
+ADD_V = 2
 SPLIT = 256
+LAST_PIECES = ((0, 256), (256, 512))
 
 
 def tile_two_sweep_policy_evaluation_d3_kernel(tc, P_bytes, P_scale, V, R, discount, out):
@@ -85,10 +87,10 @@ def tile_two_sweep_policy_evaluation_d3_kernel(tc, P_bytes, P_scale, V, R, disco
 
         nc.scalar.dma_start(out=scale_0[:], in_=scale_view[:, 0])
         load_bytes(0, 0)
-        nc.sync.dma_start(out=scale_rest[:], in_=scale_view[:, 1:])
+        nc.scalar.dma_start(out=scale_rest[:], in_=scale_view[:, 1:])
         load_bytes(0, 1)
-        nc.sync.dma_start(out=v_raw[:, 0], in_=v_view[0])
         load_bytes(0, 2)
+        nc.sync.dma_start(out=v_raw[:, 0], in_=v_view[0])
         load_bytes(0, 3)
         for g in range(1, G):
             nc.sync.dma_start(out=v_raw[:, g], in_=v_view[g])
@@ -127,8 +129,8 @@ def tile_two_sweep_policy_evaluation_d3_kernel(tc, P_bytes, P_scale, V, R, disco
             if n not in mixed:
                 mixed[n] = chunks.tile([P, W * T], BF16, name=f"mixed_{n}", tag="mixed", align_bytes=64)
             copy(
-                out=mixed[n][:].rearrange("p (b m t) -> p m t b", b=T, t=T)[:, :, :, b0:b1],
-                in_=wide[n][:].rearrange("p t (m b) -> p m t b", b=T)[:, :, :, b0:b1],
+                out=mixed[n][:].rearrange("p (b m e t) -> p m t e b", b=T, e=2, t=T)[:, :, :, :, b0:b1],
+                in_=wide[n][:].rearrange("p t (m e b) -> p m t e b", e=2, b=T)[:, :, :, :, b0:b1],
             )
 
         def turn(planes, h, name):
@@ -170,6 +172,8 @@ def tile_two_sweep_policy_evaluation_d3_kernel(tc, P_bytes, P_scale, V, R, disco
             )
 
         def interleave_v(sweep, g, c0, c1, copy):
+            if (sweep, g) == (1, G - 1) and (sweep, g) not in v_mixed:
+                v_mixed[sweep, g] = rows.tile([P, C, T], BF16, name="v_mixed_last", tag="v_mixed_last", bufs=1, align_bytes=64)
             if (sweep, g) not in v_mixed:
                 v_mixed[sweep, g] = rows.tile([P, C, T], BF16, name=f"v_mixed_{sweep}_{g}", tag="v_mixed", align_bytes=64)
             src = v_raw[:, g] if sweep == 0 else v1_rows[g][:]
@@ -200,6 +204,37 @@ def tile_two_sweep_policy_evaluation_d3_kernel(tc, P_bytes, P_scale, V, R, disco
                     stop=(g == close),
                 )
 
+        def last_tile(q, b, banks):
+            cols = slice(b * P, (b + 1) * P)
+            result = results.tile([P, C], F32, name=f"result_{q}_{b}", tag="result")
+            pieces = []
+            for bank, (c0, c1) in zip(banks, LAST_PIECES):
+                piece = psum.tile([P, c1 - c0], F32, name=f"piece_{c0}", tag=f"bank_{bank}")
+                pieces.append(piece)
+                for g in range(G):
+                    nc.tensor.matmul_mx(
+                        out=piece[:],
+                        lhsT=p_codes[:, q, g, cols].bitcast(FP8X4),
+                        lhsT_scale=p_scales[:, q, g, cols],
+                        rhs=v_codes[1][:, g, c0:c1].bitcast(FP8X4),
+                        rhs_scale=v_scales[1][:, g, c0:c1],
+                        start=(g == 0),
+                        stop=(g == G - 1),
+                    )
+            return result, pieces
+
+        def finish_last(q, b, result, pieces):
+            for piece, (c0, c1) in zip(pieces, LAST_PIECES):
+                nc.vector.scalar_tensor_tensor(
+                    out=result[:, c0:c1],
+                    in0=piece[:],
+                    scalar=disc[:, q, b : b + 1],
+                    in1=r_sb[:, q, b, c0:c1],
+                    op0=MULT,
+                    op1=ADD,
+                )
+                nc.sync.dma_start(out=out_view[q][:, b, c0:c1], in_=result[:, c0:c1])
+
         def update(dst, sweep, q, b, c0, c1):
             addend = parked[q, b] if sweep == 1 and parked.get((q, b), dst) is not dst else r_sb[:, q, b]
             nc.vector.scalar_tensor_tensor(
@@ -222,6 +257,12 @@ def tile_two_sweep_policy_evaluation_d3_kernel(tc, P_bytes, P_scale, V, R, disco
 
         def add_reward(q, b):
             nc.vector.tensor_tensor(out=parked[q, b][:], in0=parked[q, b][:], in1=r_sb[:, q, b], op=ADD)
+
+        def add_reward_late(tiles):
+            total = rows.tile([P, len(tiles), C], F32, name="parked_total", tag="v_mixed_last", bufs=1, align_bytes=64)
+            for i, (q, b) in enumerate(tiles):
+                nc.gpsimd.tensor_tensor(out=total[:, i], in0=parked[q, b][:], in1=r_sb[:, q, b], op=ADD)
+                parked[q, b] = total[:, i]
 
         def finish(q, b, pieces):
             result = results.tile([P, C], F32, name=f"result_{q}_{b}", tag="result")
@@ -337,21 +378,21 @@ def tile_two_sweep_policy_evaluation_d3_kernel(tc, P_bytes, P_scale, V, R, disco
         quantise_v(1, G - 2, 0, C)
         interleave(last + 3, 0, 2, vcopy)
         quantise(last + 2, 0, 2)
-        early_passes(list(range(EXITS, 4)), [2])
+        early_passes(list(range(EXITS, 4)) + [8], [2])
         half_passes(0, 2)
+        quantise(last, 2, T)
         quantise(last + 3, 0, 2)
         half_passes(0, 3)
-        quantise(last, 2, T)
         half_passes(1, 0)
         quantise(last + 1, 2, T)
         half_passes(1, 1)
-        early_passes(list(range(8, 8 + EXITS)), [2])
-        update_v1(G - 1, 0, 0, C)
-        update_v1(G - 1, 1, 0, C)
         quantise(last + 2, 2, T)
         half_passes(1, 2)
+        update_v1(G - 1, 0, 0, C)
         quantise(last + 3, 2, T)
         half_passes(1, 3)
+        update_v1(G - 1, 1, 0, C)
+        early_passes(list(range(9, 8 + EXITS)), [2])
         early_passes([4, 5], [0, 1, 2])
         for e in range(ADD_FIRST):
             add_reward(*early[e])
@@ -364,14 +405,21 @@ def tile_two_sweep_policy_evaluation_d3_kernel(tc, P_bytes, P_scale, V, R, disco
         for c0, c1 in ((HALF, C), (0, HALF)):
             quantise_v(1, G - 1, c0, c1)
 
-        for e in range(ADD_FIRST, EXITS):
+        for e in range(ADD_FIRST, ADD_V):
             add_reward(*early[e])
+        if ADD_V < EXITS:
+            add_reward_late([early[e] for e in range(ADD_V, EXITS)])
         held = list(range(EXITS, 4)) + list(range(8, 8 + EXITS)) + list(range(4, 8))
-        rest = list(range(EXITS)) + list(range(8 + EXITS, 16))
+        rest = list(range(ADD_V)) + list(range(8 + EXITS, 15)) + list(range(ADD_V, EXITS)) + [15]
         for e in held:
             multiply(1, *early[e], [G - 1])
-        for e, f in zip(held, rest):
+        for e, f in zip(held[:-1], rest[:-1]):
             finish(*early[e], 1)
             multiply(1, *early[f], [2, 3] if f < EXITS else list(range(G)), early_bank[e % 8])
-        for i, f in enumerate(rest):
-            finish(*early[f], 2 if i == 7 else 1)
+        finish(*early[held[-1]], 1)
+        finish(*early[rest[0]], 1)
+        finish(*early[rest[1]], 1)
+        tail = last_tile(*early[rest[-1]], [early_bank[e % 8] for e in (held[-1], held[0], held[1])])
+        for f in rest[2:-1]:
+            finish(*early[f], 1)
+        finish_last(*early[rest[-1]], *tail)

@@ -22,30 +22,11 @@ COPY = mybir.ActivationFunctionType.Copy
 
 FLOPS = 2 * 2 * S * S * C
 
-V_SLOTS = [3, 2, 1, 1] + [1, 1, 1, 1] + [1, 1, 1, 0] + [0, 0, 0, 0]
-LEAD = 3
-V_FIRST = False
 TURN_P = (7, 9, 11)
-TURN_V_AT = (0, 1, 2, 3)
-IL_V_AT = {}
-QV_AT = (1, 2, 3, 4)
-TURN_V1 = ()
-V1_S = ()
-IL_S = ()
-TURN_BANKS = (4, 5, 6, 7)
-EV_AFTER = 2
-EV_V = 3
-UPD = (1, 1, 0)
-V1_AT = (2, 2, 1)
-QV1_AT = (3, 7)
-MX_AT = {2: [0], 3: [1, 2], 4: [3], 6: [4, 5], 7: [6, 7], 10: [8, 9, 10], 11: [11]}
-EARLY_AT = {11: [(0, [0, 1]), (1, [0, 1]), (2, [0, 1]), (3, [0, 1])]}
-EXIT_AT = {}
-EXITS = 2
-ADD_FIRST = 0
-ADD_V = 2
-SPLIT = 256
-LAST_PIECES = ((0, 256), (256, 512))
+EXITS = {0: 1, 1: 1}
+WIDE_BUFS = 5
+MIXED_BUFS = 5
+V_SLOTS = [3, 2, 2, 1] + [1, 1, 1, 1] + [1, 1, 1, 1] + [0, 0, 0, 0]
 
 
 def tile_two_sweep_policy_evaluation_d3_kernel(tc, P_bytes, P_scale, V, R, discount, out):
@@ -110,59 +91,108 @@ def tile_two_sweep_policy_evaluation_d3_kernel(tc, P_bytes, P_scale, V, R, disco
         turned = {}
         parked = {}
         acc = {}
+        copier = {"V": nc.vector.tensor_copy, "S": nc.scalar.copy}
+        done = set()
+        waits = {}
 
-        def widen(n, slots, engine):
+        def note(facts):
+            for fact in facts:
+                done.add(fact)
+
+        def quarters(c0, c1):
+            return range(c0 // P, c1 // P)
+
+        def slot_free(tag, depth):
+            users = waits.setdefault(tag, [])
+            return len(users) < depth or users[len(users) - depth] <= done
+
+        def take(pool, shape, dtype, name, tag, depth, freed_by):
+            waits[tag].append(set(freed_by))
+            return pool.tile(shape, dtype, name=name, tag=tag, bufs=depth, align_bytes=64)
+
+        def widen(engine, n, t):
             q, g = divmod(n, G)
             if n not in wide:
-                wide[n] = chunks.tile([P, T, W], BF16, name=f"wide_{n}", tag="wide", align_bytes=64)
-            for t in slots:
-                src = bytes_q[q][:, g, t, :] if q < 2 else bytes_23[:, g, t, (q - 2) * W : (q - 1) * W]
-                scale = scale_0[:, t : t + 1] if g == 0 else scale_rest[:, g - 1, t : t + 1]
-                if engine == "S":
-                    nc.scalar.activation(out=wide[n][:, t, :], in_=src.bitcast(FP8), func=COPY, scale=scale)
-                else:
-                    nc.vector.tensor_scalar(
-                        out=wide[n][:, t, :], in0=src.bitcast(FP8), scalar1=scale, scalar2=None, op0=MULT
-                    )
+                if not slot_free("wide", WIDE_BUFS):
+                    return False
+                freed = [("turned", "p", n, h) for h in range(2)] if n in TURN_P else [("mixed", n, b) for b in range(T)]
+                wide[n] = take(chunks, [P, T, W], BF16, f"wide_{n}", "wide", WIDE_BUFS, freed)
+            src = bytes_q[q][:, g, t, :] if q < 2 else bytes_23[:, g, t, (q - 2) * W : (q - 1) * W]
+            scale = scale_0[:, t : t + 1] if g == 0 else scale_rest[:, g - 1, t : t + 1]
+            if engine == "S":
+                nc.scalar.activation(out=wide[n][:, t, :], in_=src.bitcast(FP8), func=COPY, scale=scale)
+            else:
+                nc.vector.tensor_scalar(out=wide[n][:, t, :], in0=src.bitcast(FP8), scalar1=scale, scalar2=None, op0=MULT)
+            done.add(("wide", n, t))
+            return True
 
-        def interleave(n, b0, b1, copy):
-            if n not in mixed:
-                mixed[n] = chunks.tile([P, W * T], BF16, name=f"mixed_{n}", tag="mixed", align_bytes=64)
-            copy(
-                out=mixed[n][:].rearrange("p (b m e t) -> p m t e b", b=T, e=2, t=T)[:, :, :, :, b0:b1],
-                in_=wide[n][:].rearrange("p t (m e b) -> p m t e b", e=2, b=T)[:, :, :, :, b0:b1],
+        def mixed_tile(n):
+            if n not in mixed and slot_free("mixed", MIXED_BUFS):
+                mixed[n] = take(chunks, [P, W * T], BF16, f"mixed_{n}", "mixed", MIXED_BUFS, [("codes", n, b) for b in range(T)])
+            return n in mixed
+
+        def v_mixed_tile(sweep, g):
+            if (sweep, g) not in v_mixed and slot_free("v_mixed", 3):
+                freed = [("v_codes", sweep, g, k) for k in range(T)]
+                v_mixed[sweep, g] = take(rows, [P, C, T], BF16, f"v_mixed_{sweep}_{g}", "v_mixed", 3, freed)
+            return (sweep, g) in v_mixed
+
+        def interleave(engine, n, b0, b1):
+            if not ({("wide", n, t) for t in range(T)} <= done and mixed_tile(n)):
+                return False
+            copier[engine](
+                out=mixed[n][:].rearrange("p (b m e t) -> p m b t e", b=T, e=2, t=T)[:, :, b0:b1],
+                in_=wide[n][:].rearrange("p t (m e b) -> p m b t e", e=2, b=T)[:, :, b0:b1],
             )
+            note(("mixed", n, b) for b in range(b0, b1))
+            return True
 
-        def turn(planes, h, name):
-            bank = psum.tile([P, 2 * W], BF16, name=f"turn_{name}_{h}", tag=f"bank_{TURN_BANKS[len(turned) % len(TURN_BANKS)]}")
-            turned[name, h] = bank
+        def turn(engine, kind, n, h, bank):
+            needs = {"p": {("wide", n, t) for t in range(T)}, "v": set(), "u": {("row", n, b, k) for b in range(T) for k in (2 * h, 2 * h + 1)}}[kind]
+            if not (needs <= done and slot_free(f"bank_{bank}", 1)):
+                return False
+            planes = wide[n] if kind == "p" else v_raw[:, n] if kind == "v" else v1_rows[n]
+            tiles = T if kind == "p" else 1
+            waits[f"bank_{bank}"].append({("emptied", kind, n, h)})
+            tile = psum.tile([P, 2 * W], BF16, name=f"turn_{kind}{n}_{h}", tag=f"bank_{bank}")
+            turned[kind, n, h] = tile
             for j in range(2):
                 first = (2 * h + j) * P
                 nc.tensor.matmul(
-                    out=bank[:].rearrange("p (j c t) -> p j t c", j=2, t=T)[:, j],
+                    out=tile[:].rearrange("p (b j m t) -> p j t m b", b=tiles, j=2, t=T)[:, j],
                     lhsT=identity[:],
-                    rhs=planes[:, :, first : first + P],
+                    rhs=planes[:, :, first : first + P].rearrange("p t (m b) -> p t m b", b=tiles),
                     start=True,
                     stop=True,
                 )
+            done.add(("turned", kind, n, h))
+            return True
 
-        def empty_p(n, h):
-            if n not in mixed:
-                mixed[n] = chunks.tile([P, W * T], BF16, name=f"mixed_{n}", tag="mixed", align_bytes=64)
-            nc.scalar.copy(
-                out=mixed[n][:].bitcast(F32).rearrange("p (b m w) -> p b m w", b=T, w=2)[:, :, h * 64 : (h + 1) * 64],
-                in_=turned[f"p{n}", h][:].bitcast(F32).rearrange("p (m b w) -> p b m w", b=T, w=2),
-            )
+        def empty(engine, kind, n, h):
+            if ("turned", kind, n, h) not in done:
+                return False
+            words = turned[kind, n, h][:].bitcast(F32)
+            if kind == "p":
+                if not mixed_tile(n):
+                    return False
+                copier[engine](
+                    out=mixed[n][:].bitcast(F32).rearrange("p (b x) -> p b x", b=T)[:, :, h * P : (h + 1) * P],
+                    in_=words.rearrange("p (b x) -> p b x", b=T),
+                )
+                if ("emptied", kind, n, 1 - h) in done:
+                    note(("mixed", n, b) for b in range(T))
+            else:
+                sweep = 0 if kind == "v" else 1
+                if not v_mixed_tile(sweep, n):
+                    return False
+                copier[engine](out=v_mixed[sweep, n][:].rearrange("p c t -> p (c t)").bitcast(F32)[:, h * W : (h + 1) * W], in_=words)
+                note(("v_mixed", sweep, n, k) for k in (2 * h, 2 * h + 1))
+            done.add(("emptied", kind, n, h))
+            return True
 
-        def empty_v(sweep, g, h):
-            if (sweep, g) not in v_mixed:
-                v_mixed[sweep, g] = rows.tile([P, C, T], BF16, name=f"v_mixed_{sweep}_{g}", tag="v_mixed", align_bytes=64)
-            nc.scalar.copy(
-                out=v_mixed[sweep, g][:].rearrange("p c t -> p (c t)").bitcast(F32)[:, h * W : (h + 1) * W],
-                in_=turned[f"v{sweep}{g}", h][:].bitcast(F32),
-            )
-
-        def quantise(n, b0, b1):
+        def quantise(engine, n, b0, b1):
+            if not {("mixed", n, b) for b in range(b0, b1)} <= done:
+                return False
             q, g = divmod(n, G)
             cols = slice(b0 * P, b1 * P)
             nc.vector.quantize_mx(
@@ -170,256 +200,190 @@ def tile_two_sweep_policy_evaluation_d3_kernel(tc, P_bytes, P_scale, V, R, disco
                 scales=p_scales[:, q, g, cols],
                 in_=mixed[n][:, b0 * P * T : b1 * P * T],
             )
+            note(("codes", n, b) for b in range(b0, b1))
+            return True
 
-        def interleave_v(sweep, g, c0, c1, copy):
-            if (sweep, g) == (1, G - 1) and (sweep, g) not in v_mixed:
-                v_mixed[sweep, g] = rows.tile([P, C, T], BF16, name="v_mixed_last", tag="v_mixed_last", bufs=1, align_bytes=64)
-            if (sweep, g) not in v_mixed:
-                v_mixed[sweep, g] = rows.tile([P, C, T], BF16, name=f"v_mixed_{sweep}_{g}", tag="v_mixed", align_bytes=64)
+        def interleave_v(engine, sweep, g, c0, c1):
+            needs = {("row", g, b, k) for b in range(T) for k in quarters(c0, c1)} if sweep == 1 else set()
+            if not (needs <= done and v_mixed_tile(sweep, g)):
+                return False
             src = v_raw[:, g] if sweep == 0 else v1_rows[g][:]
-            copy(
+            copier[engine](
                 out=v_mixed[sweep, g][:, c0:c1, :].rearrange("p (c i) t -> p c t i", i=4),
                 in_=src[:, :, c0:c1].rearrange("p t (c i) -> p c t i", i=4),
             )
+            note(("v_mixed", sweep, g, k) for k in quarters(c0, c1))
+            return True
 
-        def quantise_v(sweep, g, c0, c1):
+        def quantise_v(engine, sweep, g, c0, c1):
+            if not {("v_mixed", sweep, g, k) for k in quarters(c0, c1)} <= done:
+                return False
             nc.vector.quantize_mx(
                 out=v_codes[sweep][:, g, c0:c1].bitcast(FP8X4),
                 scales=v_scales[sweep][:, g, c0:c1],
                 in_=v_mixed[sweep, g][:, c0:c1, :].rearrange("p c t -> p (c t)"),
             )
+            note(("v_codes", sweep, g, k) for k in quarters(c0, c1))
+            return True
 
-        def multiply(sweep, q, b, groups, bank=None, close=G - 1):
+        def multiply(engine, sweep, tile, g, bank=None, close=False, c0=0, c1=C):
+            q, b = divmod(tile, T)
+            needs = {("codes", G * q + g, b)} | {("v_codes", sweep, g, k) for k in quarters(c0, c1)}
+            if not (needs <= done and (bank is None or slot_free(f"bank_{bank}", 1))):
+                return False
+            if bank is not None:
+                if sweep == 0:
+                    freed = {("row", q, b, k) for k in range(T)}
+                else:
+                    freed = {("parked", tile) if g == 0 and tile in EXITS else ("result", tile, c0)}
+                waits[f"bank_{bank}"].append(freed)
+                acc[sweep, tile, c0] = psum.tile([P, c1 - c0], F32, name=f"acc_{sweep}_{q}_{b}", tag=f"bank_{bank}")
             cols = slice(b * P, (b + 1) * P)
-            for g in groups:
-                if bank is not None and g == groups[0]:
-                    acc[sweep, q, b] = psum.tile([P, C], F32, name=f"acc_{sweep}_{q}_{b}", tag=f"bank_{bank}")
-                nc.tensor.matmul_mx(
-                    out=acc[sweep, q, b][:],
-                    lhsT=p_codes[:, q, g, cols].bitcast(FP8X4),
-                    lhsT_scale=p_scales[:, q, g, cols],
-                    rhs=v_codes[sweep][:, g, :].bitcast(FP8X4),
-                    rhs_scale=v_scales[sweep][:, g, :],
-                    start=(bank is not None and g == groups[0]),
-                    stop=(g == close),
-                )
-
-        def last_tile(q, b, banks):
-            cols = slice(b * P, (b + 1) * P)
-            result = results.tile([P, C], F32, name=f"result_{q}_{b}", tag="result")
-            pieces = []
-            for bank, (c0, c1) in zip(banks, LAST_PIECES):
-                piece = psum.tile([P, c1 - c0], F32, name=f"piece_{c0}", tag=f"bank_{bank}")
-                pieces.append(piece)
-                for g in range(G):
-                    nc.tensor.matmul_mx(
-                        out=piece[:],
-                        lhsT=p_codes[:, q, g, cols].bitcast(FP8X4),
-                        lhsT_scale=p_scales[:, q, g, cols],
-                        rhs=v_codes[1][:, g, c0:c1].bitcast(FP8X4),
-                        rhs_scale=v_scales[1][:, g, c0:c1],
-                        start=(g == 0),
-                        stop=(g == G - 1),
-                    )
-            return result, pieces
-
-        def finish_last(q, b, result, pieces):
-            for piece, (c0, c1) in zip(pieces, LAST_PIECES):
-                nc.vector.scalar_tensor_tensor(
-                    out=result[:, c0:c1],
-                    in0=piece[:],
-                    scalar=disc[:, q, b : b + 1],
-                    in1=r_sb[:, q, b, c0:c1],
-                    op0=MULT,
-                    op1=ADD,
-                )
-                nc.sync.dma_start(out=out_view[q][:, b, c0:c1], in_=result[:, c0:c1])
-
-        def update(dst, sweep, q, b, c0, c1):
-            addend = parked[q, b] if sweep == 1 and parked.get((q, b), dst) is not dst else r_sb[:, q, b]
-            nc.vector.scalar_tensor_tensor(
-                out=dst[:, c0:c1],
-                in0=acc[sweep, q, b][:, c0:c1],
-                scalar=disc[:, q, b : b + 1],
-                in1=addend[:, c0:c1],
-                op0=MULT,
-                op1=ADD,
+            nc.tensor.matmul_mx(
+                out=acc[sweep, tile, c0][:],
+                lhsT=p_codes[:, q, g, cols].bitcast(FP8X4),
+                lhsT_scale=p_scales[:, q, g, cols],
+                rhs=v_codes[sweep][:, g, c0:c1].bitcast(FP8X4),
+                rhs_scale=v_scales[sweep][:, g, c0:c1],
+                start=bank is not None,
+                stop=close,
             )
+            if close:
+                done.add(("sum", sweep, tile, g, c0))
+            return True
 
-        def update_v1(q, b, c0, c1):
+        def update(dst, sums, q, b, addend):
+            nc.vector.scalar_tensor_tensor(out=dst, in0=sums, scalar=disc[:, q, b : b + 1], in1=addend, op0=MULT, op1=ADD)
+
+        def update_v1(engine, q, b, c0, c1):
+            if ("sum", 0, T * q + b, G - 1, 0) not in done:
+                return False
             if q not in v1_rows:
-                v1_rows[q] = rows.tile([P, T, C], BF16, name=f"v1_rows_{q}", tag="v1_rows", align_bytes=64)
-            update(v1_rows[q][:, b, :], 0, q, b, c0, c1)
+                if not slot_free("v1_rows", 2):
+                    return False
+                v1_rows[q] = take(rows, [P, T, C], BF16, f"v1_rows_{q}", "v1_rows", 2, [("v_mixed", 1, q, k) for k in range(T)])
+            update(v1_rows[q][:, b, c0:c1], acc[0, T * q + b, 0][:, c0:c1], q, b, r_sb[:, q, b, c0:c1])
+            note(("row", q, b, k) for k in quarters(c0, c1))
+            return True
 
-        def leave_early(q, b):
-            parked[q, b] = results.tile([P, C], F32, name=f"parked_{q}_{b}", tag="parked", bufs=4)
-            nc.scalar.activation(out=parked[q, b][:], in_=acc[1, q, b][:], func=COPY, scale=disc32[:, q, b : b + 1])
+        def widen_discount(engine):
+            nc.vector.tensor_copy(out=disc32[:], in_=disc[:])
+            done.add(("disc32",))
+            return True
 
-        def add_reward(q, b):
-            nc.vector.tensor_tensor(out=parked[q, b][:], in0=parked[q, b][:], in1=r_sb[:, q, b], op=ADD)
-
-        def add_reward_late(tiles):
-            total = rows.tile([P, len(tiles), C], F32, name="parked_total", tag="v_mixed_last", bufs=1, align_bytes=64)
-            for i, (q, b) in enumerate(tiles):
-                nc.gpsimd.tensor_tensor(out=total[:, i], in0=parked[q, b][:], in1=r_sb[:, q, b], op=ADD)
-                parked[q, b] = total[:, i]
-
-        def finish(q, b, pieces):
-            result = results.tile([P, C], F32, name=f"result_{q}_{b}", tag="result")
-            for k in range(pieces):
-                c0, c1 = k * C // pieces, (k + 1) * C // pieces
-                update(result, 1, q, b, c0, c1)
-                nc.sync.dma_start(out=out_view[q][:, b, c0:c1], in_=result[:, c0:c1])
-
-        def s_slots(n):
-            return list(range(T - V_SLOTS[n])) if n < G * G else []
-
-        def v_slots(n):
-            return range(T - V_SLOTS[n], T) if n < G * G else []
-
-        def passes(n):
-            q, g = divmod(n, G)
-            for b in range(T):
-                multiply(0, q, b, [g], b if g == 0 else None)
-
-        end = G * G - 1
-        last = (G - 1) * G
-        early = [divmod(e, T) for e in range(16)]
-        early_bank = [4, 5, 6, 7, 0, 1, 2, 3]
-        widen(0, s_slots(0), "S")
-        widen(0, v_slots(0), "V")
-        widen(1, s_slots(1), "S")
-        interleave(0, 0, T, nc.vector.tensor_copy)
-        widen(1, v_slots(1), "V")
-        if LEAD == 3:
-            widen(2, s_slots(2), "S")
-            widen(2, v_slots(2), "V")
-        for n in range(last):
-            q, g = divmod(n, G)
-            empties = []
-            if n in TURN_V_AT:
-                gv = TURN_V_AT.index(n)
-                for h in range(2):
-                    turn(v_raw[:, gv], h, f"v0{gv}")
-                empties = [lambda h, gv=gv: empty_v(0, gv, h)]
-            if n + 1 in TURN_P:
-                empties = [lambda h: empty_p(n + 1, h)]
-            sl = s_slots(n + LEAD)
-            if q >= 1 and g == V1_AT[q - 1] and q - 1 in V1_S:
-                interleave_v(1, q - 1, 0, C, nc.scalar.copy)
-            k = EV_V if n in TURN_V_AT else EV_AFTER
-            widen(n + LEAD, sl[:k], "S")
-            for empty in empties:
-                for h in range(2):
-                    empty(h)
-                    widen(n + LEAD, sl[k : k + 1], "S")
-                    k = k + 1
-            widen(n + LEAD, sl[k:], "S")
-            for e in EXIT_AT.get(n, []):
-                leave_early(*early[e])
-            if n == 8:
-                nc.vector.tensor_copy(out=disc32[:], in_=disc[:])
-            if V_FIRST:
-                widen(n + LEAD, v_slots(n + LEAD), "V")
-            if n + 1 not in TURN_P and n + 1 not in IL_S and n + 1 <= end:
-                interleave(n + 1, 0, T if n + 1 < last else 2, nc.vector.tensor_copy)
-            if n in IL_V_AT:
-                interleave_v(0, IL_V_AT[n], 0, C, nc.vector.tensor_copy)
-            if n < end:
-                quantise(n, 0, T)
+        def park(engine, tile):
+            if not {("sum", 1, tile, EXITS[tile], 0), ("disc32",)} <= done:
+                return False
+            q, b = divmod(tile, T)
+            parked[tile] = results.tile([P, C], F32, name=f"parked_{q}_{b}", tag="parked", bufs=len(EXITS))
+            if engine == "V":
+                update(parked[tile][:], acc[1, tile, 0][:], q, b, r_sb[:, q, b])
+                done.add(("rewarded", tile))
             else:
-                quantise(n, 0, 2)
-                quantise(n, 2, T)
-            if not V_FIRST:
-                widen(n + LEAD, v_slots(n + LEAD), "V")
-            if q >= 1 and g == V1_AT[q - 1] and q - 1 not in TURN_V1 and q - 1 not in V1_S:
-                interleave_v(1, q - 1, 0, C, nc.vector.tensor_copy)
-            if n in QV_AT:
-                quantise_v(0, QV_AT.index(n), 0, C)
-            if q >= 1 and g == UPD[q - 1]:
-                for b in range(T):
-                    update_v1(q - 1, b, 0, C)
-            if n - 4 in QV1_AT:
-                quantise_v(1, QV1_AT.index(n - 4), 0, C)
-            for m in MX_AT.get(n, []):
-                passes(m)
-            for c in TURN_P:
-                if n == max(c - 3, G - 1):
-                    for h in range(2):
-                        turn(wide[c], h, f"p{c}")
-            for e, gs in EARLY_AT.get(n, []):
-                multiply(1, *early[e], gs, early_bank[e % 8] if gs[0] == 0 else None, 1 if e < EXITS else G - 1)
+                nc.scalar.activation(out=parked[tile][:], in_=acc[1, tile, 0][:], func=COPY, scale=disc32[:, q, b : b + 1])
+            done.add(("parked", tile))
+            return True
 
-        def early_passes(es, gs):
-            for e in es:
-                multiply(1, *early[e], gs, early_bank[e % 8] if gs[0] == 0 else None, 1 if e < EXITS else G - 1)
+        def add_reward(engine, tile):
+            if ("parked", tile) not in done:
+                return False
+            q, b = divmod(tile, T)
+            nc.vector.tensor_tensor(out=parked[tile][:], in0=parked[tile][:], in1=r_sb[:, q, b], op=ADD)
+            done.add(("rewarded", tile))
+            return True
 
-        def half_passes(h, g):
-            for b in (2 * h, 2 * h + 1):
-                multiply(0, G - 1, b, [g], b if g == 0 else None)
+        result = {}
 
-        vcopy, scopy = nc.vector.tensor_copy, nc.scalar.copy
-        widen(end, s_slots(end), "S")
-        interleave(last + 1, 0, 2, vcopy)
-        quantise(last, 0, 2)
-        widen(end, v_slots(end), "V")
-        for e in range(EXITS):
-            leave_early(*early[e])
+        def finish(engine, tile, c0=0, c1=C):
+            needs = {("sum", 1, tile, G - 1, c0)} | ({("rewarded", tile)} if tile in EXITS else set())
+            if not needs <= done:
+                return False
+            q, b = divmod(tile, T)
+            if tile not in result:
+                result[tile] = results.tile([P, C], F32, name=f"result_{q}_{b}", tag="result")
+            addend = parked[tile][:, c0:c1] if tile in EXITS else r_sb[:, q, b, c0:c1]
+            update(result[tile][:, c0:c1], acc[1, tile, c0][:], q, b, addend)
+            nc.sync.dma_start(out=out_view[q][:, b, c0:c1], in_=result[tile][:, c0:c1])
+            done.add(("result", tile, c0))
+            return True
+
+        def ws(n):
+            return [(widen, n, t) for t in range(T - V_SLOTS[n])]
+
+        def wv(n):
+            return [(widen, n, t) for t in range(T - V_SLOTS[n], T)]
+
+        def ev(kind, n):
+            return [(empty, kind, n, h) for h in range(2)]
+
+        def weave(n, c):
+            a, e = ws(n), ev("p", c)
+            return a[:2] + e[:1] + a[2:3] + e[1:] + a[3:]
+
+        def il(n, b0=0, b1=T):
+            return [(interleave, n, b0, b1)]
+
+        def qp(n, b0=0, b1=T):
+            return [(quantise, n, b0, b1)]
+
+        def upd(q, bs=range(T), c0=0, c1=C):
+            return [(update_v1, q, b, c0, c1) for b in bs]
+
+        def ilv(g, c0=0, c1=C):
+            return [(interleave_v, 1, g, c0, c1)]
+
+        def qv(sweep, g, c0=0, c1=C):
+            return [(quantise_v, sweep, g, c0, c1)]
+
+        def tn(kind, n, bank):
+            return [(turn, kind, n, h, bank + h) for h in range(2)]
+
+        def mx1(n, bs=range(T)):
+            q, g = divmod(n, G)
+            return [(multiply, 0, T * q + b, g, b if g == 0 else None, g == G - 1) for b in bs]
+
+        def mx2(tile, gs, bank=None, c0=0, c1=C):
+            return [(multiply, 1, tile, g, bank if g == gs[0] else None, g == G - 1 or g == EXITS.get(tile), c0, c1) for g in gs]
+
+        scalar = ws(0) + ws(1) + ws(2)
         for g in range(G):
-            interleave(last + g, 2, T, scopy)
-        for b in range(T):
-            update_v1(G - 2, b, 0, C)
-        half_passes(0, 0)
-        early_passes(range(8, 8 + EXITS), [0, 1])
-        quantise(last + 1, 0, 2)
-        half_passes(0, 1)
-        interleave_v(1, G - 2, 0, C, vcopy)
-        interleave(last + 2, 0, 2, vcopy)
-        quantise_v(1, G - 2, 0, C)
-        interleave(last + 3, 0, 2, vcopy)
-        quantise(last + 2, 0, 2)
-        early_passes(list(range(EXITS, 4)) + [8], [2])
-        half_passes(0, 2)
-        quantise(last, 2, T)
-        quantise(last + 3, 0, 2)
-        half_passes(0, 3)
-        half_passes(1, 0)
-        quantise(last + 1, 2, T)
-        half_passes(1, 1)
-        quantise(last + 2, 2, T)
-        half_passes(1, 2)
-        update_v1(G - 1, 0, 0, C)
-        quantise(last + 3, 2, T)
-        half_passes(1, 3)
-        update_v1(G - 1, 1, 0, C)
-        early_passes(list(range(9, 8 + EXITS)), [2])
-        early_passes([4, 5], [0, 1, 2])
-        for e in range(ADD_FIRST):
-            add_reward(*early[e])
-        for c0, c1 in ((0, SPLIT), (SPLIT, C)):
-            for b in (2, 3):
-                update_v1(G - 1, b, c0, c1)
-        early_passes([6, 7], [0, 1, 2])
-        interleave_v(1, G - 1, 0, SPLIT, nc.scalar.copy)
-        interleave_v(1, G - 1, SPLIT, C, nc.vector.tensor_copy)
-        for c0, c1 in ((HALF, C), (0, HALF)):
-            quantise_v(1, G - 1, c0, c1)
+            scalar = scalar + ws(3 + g) + ev("v", g)
+        scalar = scalar + ws(7) + ws(8) + weave(9, 7) + ws(10) + weave(11, 9) + ws(12) + weave(13, 11) + ws(14) + ws(15)
+        scalar = scalar + [(park, 0), (park, 1)] + il(12, 2) + il(13, 2) + il(14, 2) + il(15, 2) + ilv(3, 0, HALF)
 
-        for e in range(ADD_FIRST, ADD_V):
-            add_reward(*early[e])
-        if ADD_V < EXITS:
-            add_reward_late([early[e] for e in range(ADD_V, EXITS)])
-        held = list(range(EXITS, 4)) + list(range(8, 8 + EXITS)) + list(range(4, 8))
-        rest = list(range(ADD_V)) + list(range(8 + EXITS, 15)) + list(range(ADD_V, EXITS)) + [15]
-        for e in held:
-            multiply(1, *early[e], [G - 1])
-        for e, f in zip(held[:-1], rest[:-1]):
-            finish(*early[e], 1)
-            multiply(1, *early[f], [2, 3] if f < EXITS else list(range(G)), early_bank[e % 8])
-        finish(*early[held[-1]], 1)
-        finish(*early[rest[0]], 1)
-        finish(*early[rest[1]], 1)
-        tail = last_tile(*early[rest[-1]], [early_bank[e % 8] for e in (held[-1], held[0], held[1])])
-        for f in rest[2:-1]:
-            finish(*early[f], 1)
-        finish_last(*early[rest[-1]], *tail)
+        vector = wv(0) + il(0) + wv(1) + wv(2) + il(1) + qp(0) + wv(3)
+        for n in range(1, 5):
+            vector = vector + il(n + 1) + qp(n) + wv(n + 3) + qv(0, n - 1)
+        vector = vector + il(6) + qp(5) + wv(8) + upd(0) + qp(6) + wv(9) + ilv(0) + il(8) + qp(7) + wv(10) + qv(1, 0) + [(widen_discount,)]
+        vector = vector + qp(8) + wv(11) + il(10) + qp(9) + wv(12) + upd(1) + qp(10) + wv(13) + ilv(1) + il(12, 0, 2) + qp(11) + wv(14) + qv(1, 1)
+        vector = vector + il(13, 0, 2) + qp(12, 0, 2) + wv(15) + upd(2) + qp(13, 0, 2) + ilv(2) + il(14, 0, 2) + qv(1, 2) + il(15, 0, 2)
+        vector = vector + qp(14, 0, 2) + qp(12, 2) + qp(15, 0, 2) + qp(13, 2) + qp(14, 2) + upd(3, [0]) + qp(15, 2) + upd(3, [1])
+        vector = vector + upd(3, [2, 3], 0, HALF) + upd(3, [2, 3], HALF, C) + ilv(3, HALF, C) + qv(1, 3, HALF, C) + qv(1, 3, 0, HALF)
+        vector = vector + [(add_reward, 0), (add_reward, 1)]
+        order = [2, 3, 8, 9, 4, 5, 6, 7, 0, 1, 10, 11, 12, 13, 14]
+        vector = vector + [(finish, tile) for tile in order] + [(finish, 15, 0, HALF), (finish, 15, HALF, C)]
+
+        tensor = tn("v", 0, 4) + tn("v", 1, 6) + tn("v", 2, 4) + mx1(0) + tn("v", 3, 6) + mx1(1) + mx1(2) + mx1(3)
+        tensor = tensor + tn("p", 7, 4) + mx1(4) + mx1(5) + tn("p", 9, 6) + mx1(6) + mx1(7) + tn("p", 11, 4) + mx1(8) + mx1(9) + mx1(10) + mx1(11)
+        tensor = tensor + mx2(0, [0, 1], 4) + mx2(1, [0, 1], 5) + mx2(2, [0, 1], 6) + mx2(3, [0, 1], 7)
+        tensor = tensor + mx1(12, [0, 1]) + mx2(8, [0, 1], 4) + mx2(9, [0, 1], 5) + mx1(13, [0, 1]) + mx2(2, [2]) + mx2(3, [2]) + mx2(8, [2])
+        tensor = tensor + mx1(14, [0, 1]) + mx1(15, [0, 1]) + mx1(12, [2, 3]) + mx1(13, [2, 3]) + mx1(14, [2, 3]) + mx1(15, [2, 3]) + mx2(9, [2])
+        for tile in range(4, 8):
+            tensor = tensor + mx2(tile, [0, 1, 2], tile - 4)
+        for tile in order[:8]:
+            tensor = tensor + mx2(tile, [3])
+        banks = [6, 7, 4, 5, 0, 1, 2, 3]
+        for tile, bank in zip(order[8:], banks):
+            tensor = tensor + mx2(tile, [2, 3] if tile in EXITS else [0, 1, 2, 3], bank)
+        tensor = tensor + mx2(15, [0, 1, 2, 3], 3, 0, HALF) + mx2(15, [0, 1, 2, 3], 6, HALF, C)
+
+
+        queues = {"S": scalar, "V": vector, "T": tensor}
+        at = {engine: 0 for engine in queues}
+        while any(at[engine] < len(queues[engine]) for engine in queues):
+            moved = False
+            for engine, steps in queues.items():
+                while at[engine] < len(steps) and steps[at[engine]][0](engine, *steps[at[engine]][1:]):
+                    at[engine] = at[engine] + 1
+                    moved = True
+            assert moved, [steps[at[engine]][1:] for engine, steps in queues.items() if at[engine] < len(steps)]

@@ -49,10 +49,13 @@ def tile_two_sweep_policy_evaluation_d3_kernel(tc, P_bytes, P_scale, V, R, disco
         bytes_23 = keep.tile([P, G, T, 2 * W], U8, name="bytes_23", align_bytes=64)
         v_raw = keep.tile([P, G, T, C], BF16, name="v_raw", align_bytes=64)
         r_sb = keep.tile([P, G, T, C], BF16, name="r_sb", align_bytes=64)
-        p_codes = keep.tile([P, G, G, W], U32, name="p_codes", align_bytes=64)
-        p_scales = keep.tile([P, G, G, W], U8, name="p_scales", align_bytes=64)
-        v_codes = [keep.tile([P, G, C], U32, name=f"v_codes_{s}", align_bytes=64) for s in range(2)]
-        v_scales = [keep.tile([P, G, C], U8, name=f"v_scales_{s}", align_bytes=64) for s in range(2)]
+        p_codes = keep.tile([P, G, G, W], U32, name="p_codes", align_bytes=256)
+        p_scale_bytes = keep.tile([P, 64 + G * G * W], U8, name="p_scales", align_bytes=256)
+        p_scales = p_scale_bytes[:, 64:].rearrange("p (q g w) -> p q g w", q=G, g=G)
+        v_words = [keep.tile([P, 32 + G * C], U32, name=f"v_codes_{s}", align_bytes=256) for s in range(2)]
+        v_codes = [words[:, 32:].rearrange("p (g c) -> p g c", g=G) for words in v_words]
+        v_scale_bytes = [keep.tile([P, 192 + G * C], U8, name=f"v_scales_{s}", align_bytes=256) for s in range(2)]
+        v_scales = [plane[:, 192:].rearrange("p (g c) -> p g c", g=G) for plane in v_scale_bytes]
 
         identity = keep.tile([P, P], BF16, name="identity")
         make_identity(nc, identity[:])
@@ -348,34 +351,34 @@ def tile_two_sweep_policy_evaluation_d3_kernel(tc, P_bytes, P_scale, V, R, disco
         scalar = ws(0) + ws(1) + ws(2)
         for g in range(G):
             scalar = scalar + ws(3 + g) + ev("v", g)
-        scalar = scalar + ws(7) + ws(8) + weave(9, 7) + ws(10) + weave(11, 9) + ws(12) + weave(13, 11) + ws(14) + ws(15)
-        scalar = scalar + [(park, 0), (park, 1)] + il(12, 2) + il(13, 2) + il(14, 2) + il(15, 2) + ilv(3, 0, HALF)
+        scalar = scalar + ws(7) + ws(8) + weave(9, 7) + ws(10) + weave(11, 9) + ws(12) + weave(13, 11) + ws(14) + ws(15)[:1] + [(park, 0)] + ws(15)[1:2] + [(park, 1)] + ws(15)[2:]
+        scalar = scalar + [step for b in (2, 3) for n in range(12, 16) for step in il(n, b, b + 1)] + ilv(3, 0, HALF)
 
         vector = wv(0) + il(0) + wv(1) + wv(2) + il(1) + qp(0) + wv(3)
         for n in range(1, 5):
             vector = vector + il(n + 1) + qp(n) + wv(n + 3) + qv(0, n - 1)
         vector = vector + il(6) + qp(5) + wv(8) + upd(0) + qp(6) + wv(9) + ilv(0) + il(8) + qp(7) + wv(10) + qv(1, 0) + [(widen_discount,)]
-        vector = vector + qp(8) + wv(11) + il(10) + qp(9) + wv(12) + upd(1) + qp(10) + wv(13) + ilv(1) + il(12, 0, 2) + qp(11) + wv(14) + qv(1, 1)
-        vector = vector + il(13, 0, 2) + qp(12, 0, 2) + wv(15) + upd(2) + qp(13, 0, 2) + ilv(2) + il(14, 0, 2) + qv(1, 2) + il(15, 0, 2)
-        vector = vector + qp(14, 0, 2) + qp(12, 2) + qp(15, 0, 2) + qp(13, 2) + qp(14, 2) + upd(3, [0]) + qp(15, 2) + upd(3, [1])
-        vector = vector + upd(3, [2, 3], 0, HALF) + upd(3, [2, 3], HALF, C) + ilv(3, HALF, C) + qv(1, 3, HALF, C) + qv(1, 3, 0, HALF)
-        vector = vector + [(add_reward, 0), (add_reward, 1)]
+        vector = vector + qp(8) + wv(11) + il(10) + qp(9) + wv(12) + upd(1) + qp(10) + wv(13) + ilv(1) + qp(11) + wv(14) + qv(1, 1) + il(12, 0, 2)
+        vector = vector + upd(2) + qp(12, 0, 2) + ilv(2) + il(13, 0, 2) + qv(1, 2) + il(14, 0, 2) + qp(13, 0, 2) + wv(15) + il(15, 0, 2) + qp(14, 0, 2)
+        vector = vector + qp(12, 2, 3) + qp(13, 2, 3) + qp(15, 0, 2) + qp(14, 2, 3) + qp(15, 2, 3) + qp(12, 3) + qp(13, 3) + upd(3, [0]) + qp(14, 3) + upd(3, [1]) + qp(15, 3) + upd(3, [2]) + [(add_reward, 0)]
+        vector = vector + upd(3, [3], 0, HALF) + upd(3, [3], HALF, C) + ilv(3, HALF, C) + qv(1, 3, HALF, C) + qv(1, 3, 0, HALF) + [(add_reward, 1)]
         order = [2, 3, 8, 9, 4, 5, 6, 7, 0, 1, 10, 11, 12, 13, 14]
         vector = vector + [(finish, tile) for tile in order] + [(finish, 15, 0, HALF), (finish, 15, HALF, C)]
 
         tensor = tn("v", 0, 4) + tn("v", 1, 6) + tn("v", 2, 4) + mx1(0) + tn("v", 3, 6) + mx1(1) + mx1(2) + mx1(3)
         tensor = tensor + tn("p", 7, 4) + mx1(4) + mx1(5) + tn("p", 9, 6) + mx1(6) + mx1(7) + tn("p", 11, 4) + mx1(8) + mx1(9) + mx1(10) + mx1(11)
-        tensor = tensor + mx2(0, [0, 1], 4) + mx2(1, [0, 1], 5) + mx2(2, [0, 1], 6) + mx2(3, [0, 1], 7)
-        tensor = tensor + mx1(12, [0, 1]) + mx2(8, [0, 1], 4) + mx2(9, [0, 1], 5) + mx1(13, [0, 1]) + mx2(2, [2]) + mx2(3, [2]) + mx2(8, [2])
-        tensor = tensor + mx1(14, [0, 1]) + mx1(15, [0, 1]) + mx1(12, [2, 3]) + mx1(13, [2, 3]) + mx1(14, [2, 3]) + mx1(15, [2, 3]) + mx2(9, [2])
-        for tile in range(4, 8):
+        tensor = tensor + mx2(0, [0, 1], 6) + mx2(1, [0, 1], 7) + mx2(2, [0, 1], 4) + mx2(3, [0, 1], 5)
+        tensor = tensor + mx2(8, [0, 1], 6) + mx1(12, [0, 1]) + mx2(9, [0, 1], 7) + mx2(2, [2]) + mx2(3, [2]) + mx2(8, [2]) + mx2(9, [2])
+        tensor = tensor + mx1(13, [0, 1]) + mx1(14, [0, 1]) + mx1(15, [0, 1]) + mx1(12, [2]) + mx1(13, [2]) + mx1(14, [2]) + mx1(15, [2])
+        tensor = tensor + mx1(12, [3]) + mx1(13, [3]) + mx1(14, [3]) + mx1(15, [3]) + mx2(4, [0, 1, 2], 0)
+        for tile in range(5, 8):
             tensor = tensor + mx2(tile, [0, 1, 2], tile - 4)
         for tile in order[:8]:
             tensor = tensor + mx2(tile, [3])
-        banks = [6, 7, 4, 5, 0, 1, 2, 3]
+        banks = [4, 5, 6, 7, 0, 1, 2, 3]
         for tile, bank in zip(order[8:], banks):
-            tensor = tensor + mx2(tile, [2, 3] if tile in EXITS else [0, 1, 2, 3], bank)
-        tensor = tensor + mx2(15, [0, 1, 2, 3], 3, 0, HALF) + mx2(15, [0, 1, 2, 3], 6, HALF, C)
+            tensor = tensor + mx2(tile, list(range(EXITS[tile] + 1, G)) if tile in EXITS else [0, 1, 2, 3], bank)
+        tensor = tensor + mx2(15, [0, 1, 2, 3], banks[7], 0, HALF) + mx2(15, [0, 1, 2, 3], banks[0], HALF, C)
 
 
         queues = {"S": scalar, "V": vector, "T": tensor}

@@ -22,11 +22,15 @@ COPY = mybir.ActivationFunctionType.Copy
 
 FLOPS = 2 * 2 * S * S * C
 
-TURN_P = (7, 9, 11)
-EXITS = {0: 1, 1: 1}
+TURN_P = (7, 9)
+EXITS = {0: 1, 1: 1, 2: 1, 3: 1}
 WIDE_BUFS = 5
 MIXED_BUFS = 5
-V_SLOTS = [3, 2, 2, 1] + [1, 1, 1, 1] + [1, 1, 1, 1] + [0, 0, 0, 0]
+V_SLOTS = [3, 2, 2, 1] + [1, 1, 1, 1] + [1, 1, 1, 0] + [0, 0, 1, 0]
+PAIRED = ()
+HELD = None
+TWO_QUEUES = False
+AHEAD = 5
 
 
 def tile_two_sweep_policy_evaluation_d3_kernel(tc, P_bytes, P_scale, V, R, discount, out):
@@ -49,13 +53,10 @@ def tile_two_sweep_policy_evaluation_d3_kernel(tc, P_bytes, P_scale, V, R, disco
         bytes_23 = keep.tile([P, G, T, 2 * W], U8, name="bytes_23", align_bytes=64)
         v_raw = keep.tile([P, G, T, C], BF16, name="v_raw", align_bytes=64)
         r_sb = keep.tile([P, G, T, C], BF16, name="r_sb", align_bytes=64)
-        p_codes = keep.tile([P, G, G, W], U32, name="p_codes", align_bytes=256)
-        p_scale_bytes = keep.tile([P, 64 + G * G * W], U8, name="p_scales", align_bytes=256)
-        p_scales = p_scale_bytes[:, 64:].rearrange("p (q g w) -> p q g w", q=G, g=G)
-        v_words = [keep.tile([P, 32 + G * C], U32, name=f"v_codes_{s}", align_bytes=256) for s in range(2)]
-        v_codes = [words[:, 32:].rearrange("p (g c) -> p g c", g=G) for words in v_words]
-        v_scale_bytes = [keep.tile([P, 192 + G * C], U8, name=f"v_scales_{s}", align_bytes=256) for s in range(2)]
-        v_scales = [plane[:, 192:].rearrange("p (g c) -> p g c", g=G) for plane in v_scale_bytes]
+        p_codes = keep.tile([P, G, G, W], U32, name="p_codes", align_bytes=64)
+        p_scales = keep.tile([P, G, G, W], U8, name="p_scales", align_bytes=64)
+        v_codes = [keep.tile([P, G, C], U32, name=f"v_codes_{s}", align_bytes=64) for s in range(2)]
+        v_scales = [keep.tile([P, G, C], U8, name=f"v_scales_{s}", align_bytes=64) for s in range(2)]
 
         identity = keep.tile([P, P], BF16, name="identity")
         make_identity(nc, identity[:])
@@ -130,11 +131,19 @@ def tile_two_sweep_policy_evaluation_d3_kernel(tc, P_bytes, P_scale, V, R, disco
             return True
 
         def mixed_tile(n):
+            if n == HELD and n not in mixed and slot_free("held", 1):
+                mixed[n] = take(chunks, [P, W * T], BF16, f"mixed_{n}", "held", 1, [("codes", n, b) for b in range(T)])
             if n not in mixed and slot_free("mixed", MIXED_BUFS):
                 mixed[n] = take(chunks, [P, W * T], BF16, f"mixed_{n}", "mixed", MIXED_BUFS, [("codes", n, b) for b in range(T)])
             return n in mixed
 
         def v_mixed_tile(sweep, g):
+            if (sweep, g) == (1, G - 1) and (sweep, g) not in v_mixed and slot_free("last", 1):
+                v_mixed[sweep, g] = take(rows, [P, C, T], BF16, "v_mixed_last", "last", 1, [("v_codes", sweep, g, k) for k in range(T)])
+            if (sweep, g) == (1, 0) and HELD is not None:
+                if (sweep, g) not in v_mixed and HELD in mixed and slot_free("held", 1):
+                    v_mixed[sweep, g] = take(chunks, [P, C, T], BF16, "v_mixed_1_0", "held", 1, [])
+                return (sweep, g) in v_mixed
             if (sweep, g) not in v_mixed and slot_free("v_mixed", 3):
                 freed = [("v_codes", sweep, g, k) for k in range(T)]
                 v_mixed[sweep, g] = take(rows, [P, C, T], BF16, f"v_mixed_{sweep}_{g}", "v_mixed", 3, freed)
@@ -211,6 +220,17 @@ def tile_two_sweep_policy_evaluation_d3_kernel(tc, P_bytes, P_scale, V, R, disco
             if not (needs <= done and v_mixed_tile(sweep, g)):
                 return False
             src = v_raw[:, g] if sweep == 0 else v1_rows[g][:]
+            if engine == "G":
+                nc.gpsimd.tensor_scalar(
+                    out=v_mixed[sweep, g][:, c0:c1, :],
+                    in0=src[:, :, c0:c1].rearrange("p t c -> p c t"),
+                    scalar1=1.0,
+                    scalar2=0.0,
+                    op0=MULT,
+                    op1=ADD,
+                )
+                note(("v_mixed", sweep, g, k) for k in quarters(c0, c1))
+                return True
             copier[engine](
                 out=v_mixed[sweep, g][:, c0:c1, :].rearrange("p (c i) t -> p c t i", i=4),
                 in_=src[:, :, c0:c1].rearrange("p t (c i) -> p c t i", i=4),
@@ -291,22 +311,37 @@ def tile_two_sweep_policy_evaluation_d3_kernel(tc, P_bytes, P_scale, V, R, disco
             if ("parked", tile) not in done:
                 return False
             q, b = divmod(tile, T)
+            if engine == "G":
+                if "late" not in turned:
+                    if not ((1, G - 1) in v_mixed and slot_free("last", 1)):
+                        return False
+                    turned["late"] = take(rows, [P, len(EXITS), C], F32, "late", "last", 1, [])
+                nc.gpsimd.tensor_tensor(out=turned["late"][:, tile], in0=parked[tile][:], in1=r_sb[:, q, b], op=ADD)
+                parked[tile] = turned["late"][:, tile]
+                done.add(("rewarded", tile))
+                return True
             nc.vector.tensor_tensor(out=parked[tile][:], in0=parked[tile][:], in1=r_sb[:, q, b], op=ADD)
             done.add(("rewarded", tile))
             return True
 
         result = {}
+        stored = []
 
         def finish(engine, tile, c0=0, c1=C):
             needs = {("sum", 1, tile, G - 1, c0)} | ({("rewarded", tile)} if tile in EXITS else set())
             if not needs <= done:
                 return False
             q, b = divmod(tile, T)
-            if tile not in result:
-                result[tile] = results.tile([P, C], F32, name=f"result_{q}_{b}", tag="result")
+            pair = tile // 2
+            if pair not in result:
+                result[pair] = results.tile([P, 2, C], F32, name=f"result_{q}_{b}", tag="result", bufs=5)
             addend = parked[tile][:, c0:c1] if tile in EXITS else r_sb[:, q, b, c0:c1]
-            update(result[tile][:, c0:c1], acc[1, tile, c0][:], q, b, addend)
-            nc.sync.dma_start(out=out_view[q][:, b, c0:c1], in_=result[tile][:, c0:c1])
+            update(result[pair][:, b % 2, c0:c1], acc[1, tile, c0][:], q, b, addend)
+            if pair not in PAIRED:
+                (nc.scalar if TWO_QUEUES and len(stored) % 2 else nc.sync).dma_start(out=out_view[q][:, b, c0:c1], in_=result[pair][:, b % 2, c0:c1])
+            elif b % 2 == 1:
+                nc.sync.dma_start(out=out_view[q][:, b - 1 : b + 1], in_=result[pair][:])
+            stored.append(tile)
             done.add(("result", tile, c0))
             return True
 
@@ -351,37 +386,40 @@ def tile_two_sweep_policy_evaluation_d3_kernel(tc, P_bytes, P_scale, V, R, disco
         scalar = ws(0) + ws(1) + ws(2)
         for g in range(G):
             scalar = scalar + ws(3 + g) + ev("v", g)
-        scalar = scalar + ws(7) + ws(8) + weave(9, 7) + ws(10) + weave(11, 9) + ws(12) + weave(13, 11) + ws(14) + ws(15)[:1] + [(park, 0)] + ws(15)[1:2] + [(park, 1)] + ws(15)[2:]
-        scalar = scalar + [step for b in (2, 3) for n in range(12, 16) for step in il(n, b, b + 1)] + ilv(3, 0, HALF)
+        scalar = scalar + ws(7) + ws(8) + weave(9, 7) + ws(10) + weave(11, 9) + ws(12) + ws(13) + ws(14) + ws(15) + [(park, 0), (park, 1)]
+        scalar = scalar + il(12, 2, 3) + [(park, 2), (park, 3)] + il(13, 2, 3) + il(14, 2, 3) + il(15, 2, 3) + [step for n in range(12, 16) for step in il(n, 3)] + ilv(2) + ilv(3, 0, HALF)
 
         vector = wv(0) + il(0) + wv(1) + wv(2) + il(1) + qp(0) + wv(3)
         for n in range(1, 5):
             vector = vector + il(n + 1) + qp(n) + wv(n + 3) + qv(0, n - 1)
         vector = vector + il(6) + qp(5) + wv(8) + upd(0) + qp(6) + wv(9) + ilv(0) + il(8) + qp(7) + wv(10) + qv(1, 0) + [(widen_discount,)]
-        vector = vector + qp(8) + wv(11) + il(10) + qp(9) + wv(12) + upd(1) + qp(10) + wv(13) + ilv(1) + qp(11) + wv(14) + qv(1, 1) + il(12, 0, 2)
-        vector = vector + upd(2) + qp(12, 0, 2) + ilv(2) + il(13, 0, 2) + qv(1, 2) + il(14, 0, 2) + qp(13, 0, 2) + wv(15) + il(15, 0, 2) + qp(14, 0, 2)
-        vector = vector + qp(12, 2, 3) + qp(13, 2, 3) + qp(15, 0, 2) + qp(14, 2, 3) + qp(15, 2, 3) + qp(12, 3) + qp(13, 3) + upd(3, [0]) + qp(14, 3) + upd(3, [1]) + qp(15, 3) + upd(3, [2]) + [(add_reward, 0)]
-        vector = vector + upd(3, [3], 0, HALF) + upd(3, [3], HALF, C) + ilv(3, HALF, C) + qv(1, 3, HALF, C) + qv(1, 3, 0, HALF) + [(add_reward, 1)]
-        order = [2, 3, 8, 9, 4, 5, 6, 7, 0, 1, 10, 11, 12, 13, 14]
+        vector = vector + qp(8) + wv(11) + il(10) + wv(12) + upd(1) + qp(9) + ilv(1) + qp(10) + il(11) + qv(1, 1) + wv(13) + qp(11) + wv(14) + il(12, 0, 2)
+        vector = vector + wv(15) + upd(2) + qp(12, 0, 2) + il(13, 0, 2) + il(14, 0, 2) + qp(13, 0, 2) + il(15, 0, 2) + qp(14, 0, 2)
+        vector = vector + qp(12, 2, 3) + qp(13, 2, 3) + qp(15, 0, 2) + qp(14, 2, 3) + qp(15, 2, 3) + qp(12, 3) + upd(3, [0]) + qp(13, 3) + qp(14, 3) + upd(3, [1]) + qp(15, 3) + upd(3, [2])
+        vector = vector + [(add_reward, 0)] + upd(3, [3], 0, HALF) + upd(3, [3], HALF, C) + qv(1, 2) + ilv(3, HALF, C) + qv(1, 3, HALF, C) + qv(1, 3, 0, HALF)
+        order = [8, 9, 10, 11, 4, 5, 6, 7, 0, 12, 1, 13, 2, 14, 3]
         vector = vector + [(finish, tile) for tile in order] + [(finish, 15, 0, HALF), (finish, 15, HALF, C)]
 
+        gpsimd = [(add_reward, tile) for tile in (1, 2, 3)]
         tensor = tn("v", 0, 4) + tn("v", 1, 6) + tn("v", 2, 4) + mx1(0) + tn("v", 3, 6) + mx1(1) + mx1(2) + mx1(3)
-        tensor = tensor + tn("p", 7, 4) + mx1(4) + mx1(5) + tn("p", 9, 6) + mx1(6) + mx1(7) + tn("p", 11, 4) + mx1(8) + mx1(9) + mx1(10) + mx1(11)
-        tensor = tensor + mx2(0, [0, 1], 6) + mx2(1, [0, 1], 7) + mx2(2, [0, 1], 4) + mx2(3, [0, 1], 5)
-        tensor = tensor + mx2(8, [0, 1], 6) + mx1(12, [0, 1]) + mx2(9, [0, 1], 7) + mx2(2, [2]) + mx2(3, [2]) + mx2(8, [2]) + mx2(9, [2])
+        tensor = tensor + tn("p", 7, 4) + mx1(4) + mx1(5) + tn("p", 9, 6) + mx1(6) + mx1(7) + mx2(0, [0], 4) + mx2(1, [0], 5) + mx2(2, [0], 6) + mx2(3, [0], 7) + mx1(8) + mx1(9) + mx1(10)
+        tensor = tensor + mx2(0, [1]) + mx2(1, [1]) + mx1(11) + mx2(2, [1]) + mx2(3, [1])
+        tensor = tensor + mx2(8, [0, 1], 4) + mx2(9, [0, 1], 5) + mx2(10, [0, 1], 6) + mx1(12, [0, 1]) + mx2(11, [0, 1], 7)
         tensor = tensor + mx1(13, [0, 1]) + mx1(14, [0, 1]) + mx1(15, [0, 1]) + mx1(12, [2]) + mx1(13, [2]) + mx1(14, [2]) + mx1(15, [2])
-        tensor = tensor + mx1(12, [3]) + mx1(13, [3]) + mx1(14, [3]) + mx1(15, [3]) + mx2(4, [0, 1, 2], 0)
-        for tile in range(5, 8):
-            tensor = tensor + mx2(tile, [0, 1, 2], tile - 4)
-        for tile in order[:8]:
-            tensor = tensor + mx2(tile, [3])
+        tensor = tensor + mx1(12, [3]) + mx1(13, [3]) + mx1(14, [3]) + mx1(15, [3])
+        for tile in range(4, 8):
+            tensor = tensor + mx2(tile, [0, 1], tile - 4)
+        for tile in order[:AHEAD]:
+            tensor = tensor + mx2(tile, [2])
+        for k, tile in enumerate(order[:8]):
+            tensor = tensor + mx2(tile, [3]) + [step for later in order[AHEAD + k : 8][:1] for step in mx2(later, [2])]
         banks = [4, 5, 6, 7, 0, 1, 2, 3]
         for tile, bank in zip(order[8:], banks):
             tensor = tensor + mx2(tile, list(range(EXITS[tile] + 1, G)) if tile in EXITS else [0, 1, 2, 3], bank)
         tensor = tensor + mx2(15, [0, 1, 2, 3], banks[7], 0, HALF) + mx2(15, [0, 1, 2, 3], banks[0], HALF, C)
 
 
-        queues = {"S": scalar, "V": vector, "T": tensor}
+        queues = {"S": scalar, "V": vector, "T": tensor, "G": gpsimd}
         at = {engine: 0 for engine in queues}
         while any(at[engine] < len(queues[engine]) for engine in queues):
             moved = False

@@ -25,12 +25,11 @@ FLOPS = 2 * 2 * S * S * C
 TURN_P = (7, 9)
 EXITS = {0: 1, 1: 1, 2: 1, 3: 1}
 WIDE_BUFS = 5
-MIXED_BUFS = 5
-V_SLOTS = [3, 2, 2, 1] + [1, 1, 1, 1] + [1, 1, 1, 0] + [0, 0, 1, 0]
-PAIRED = ()
-HELD = None
-TWO_QUEUES = False
+MIXED_BUFS = 4
+V_SLOTS = [3, 0, 0, 0] + [1, 0, 0, 0] + [0, 1, 0, 1] + [0, 0, 0, 0]
 AHEAD = 5
+RESULT_BUFS = 8
+HELD = 9
 
 
 def tile_two_sweep_policy_evaluation_d3_kernel(tc, P_bytes, P_scale, V, R, discount, out):
@@ -41,7 +40,7 @@ def tile_two_sweep_policy_evaluation_d3_kernel(tc, P_bytes, P_scale, V, R, disco
         keep = ctx.enter_context(tc.tile_pool(name="keep", bufs=1))
         chunks = ctx.enter_context(tc.tile_pool(name="chunks", bufs=5))
         rows = ctx.enter_context(tc.tile_pool(name="rows", bufs=3))
-        results = ctx.enter_context(tc.tile_pool(name="results", bufs=10))
+        results = ctx.enter_context(tc.tile_pool(name="results", bufs=8))
         psum = ctx.enter_context(tc.psum_pool(name="psum", bufs=1))
         ctx.enter_context(tc.manual_schedule())
 
@@ -49,8 +48,9 @@ def tile_two_sweep_policy_evaluation_d3_kernel(tc, P_bytes, P_scale, V, R, disco
         scale_rest = keep.tile([P, G - 1, T], F32, name="scale_rest")
         disc = keep.tile([P, G, T], BF16, name="disc")
         disc32 = keep.tile([P, G, T], F32, name="disc32")
-        bytes_q = [keep.tile([P, G, T, W], U8, name=f"bytes_{q}", align_bytes=64) for q in range(2)]
-        bytes_23 = keep.tile([P, G, T, 2 * W], U8, name="bytes_23", align_bytes=64)
+        first_bytes = [keep.tile([P, T, W], U8, name=f"first_bytes_{q}", align_bytes=64) for q in range(2)]
+        pair_bytes = keep.tile([P, G - 1, T, 2 * W], U8, name="bytes_01", align_bytes=64)
+        p_bytes = [None, keep.tile([P, G, T, 2 * W], U8, name="bytes_23", align_bytes=64)]
         v_raw = keep.tile([P, G, T, C], BF16, name="v_raw", align_bytes=64)
         r_sb = keep.tile([P, G, T, C], BF16, name="r_sb", align_bytes=64)
         p_codes = keep.tile([P, G, G, W], U32, name="p_codes", align_bytes=64)
@@ -67,24 +67,27 @@ def tile_two_sweep_policy_evaluation_d3_kernel(tc, P_bytes, P_scale, V, R, disco
         r_view = R.rearrange("(g p t) c -> g p t c", p=P, t=T)
         out_view = out.rearrange("(g p t) c -> g p t c", p=P, t=T)
 
-        def load_bytes(q, g):
-            nc.sync.dma_start(out=bytes_q[q][:, g], in_=p_view[g][:, :, q * W : (q + 1) * W])
+        def load_first(q):
+            nc.sync.dma_start(out=first_bytes[q][:], in_=p_view[0][:, :, q * W : (q + 1) * W])
+
+        def load_pair(g):
+            nc.sync.dma_start(out=pair_bytes[:, g - 1], in_=p_view[g][:, :, : 2 * W])
 
         nc.scalar.dma_start(out=scale_0[:], in_=scale_view[:, 0])
-        load_bytes(0, 0)
+        load_first(0)
         nc.scalar.dma_start(out=scale_rest[:], in_=scale_view[:, 1:])
-        load_bytes(0, 1)
-        load_bytes(0, 2)
+        load_first(1)
+        load_pair(1)
         nc.sync.dma_start(out=v_raw[:, 0], in_=v_view[0])
-        load_bytes(0, 3)
-        for g in range(1, G):
-            nc.sync.dma_start(out=v_raw[:, g], in_=v_view[g])
-            load_bytes(1, g - 1)
-        load_bytes(1, G - 1)
+        load_pair(2)
+        nc.sync.dma_start(out=v_raw[:, 1], in_=v_view[1])
+        load_pair(3)
+        nc.sync.dma_start(out=v_raw[:, 2], in_=v_view[2])
+        nc.sync.dma_start(out=v_raw[:, 3], in_=v_view[3])
         nc.sync.dma_start(out=disc[:], in_=discount.rearrange("(g p t) o -> p g (t o)", p=P, t=T))
         nc.sync.dma_start(out=r_sb[:, 0], in_=r_view[0])
         for g in range(G):
-            nc.sync.dma_start(out=bytes_23[:, g], in_=p_view[g][:, :, 2 * W :])
+            nc.sync.dma_start(out=p_bytes[1][:, g], in_=p_view[g][:, :, 2 * W :])
         for q in range(1, G):
             nc.sync.dma_start(out=r_sb[:, q], in_=r_view[q])
 
@@ -93,6 +96,7 @@ def tile_two_sweep_policy_evaluation_d3_kernel(tc, P_bytes, P_scale, V, R, disco
         v_mixed = {}
         v1_rows = {}
         turned = {}
+        both = {}
         parked = {}
         acc = {}
         copier = {"V": nc.vector.tensor_copy, "S": nc.scalar.copy}
@@ -114,20 +118,27 @@ def tile_two_sweep_policy_evaluation_d3_kernel(tc, P_bytes, P_scale, V, R, disco
             waits[tag].append(set(freed_by))
             return pool.tile(shape, dtype, name=name, tag=tag, bufs=depth, align_bytes=64)
 
-        def widen(engine, n, t):
+        def readers(n):
+            return [("turned", "p", n, h) for h in range(2)] if n in TURN_P else [("mixed", n, b) for b in range(T)]
+
+        def widen(engine, n, t, count=1):
             q, g = divmod(n, G)
             if n not in wide:
                 if not slot_free("wide", WIDE_BUFS):
                     return False
-                freed = [("turned", "p", n, h) for h in range(2)] if n in TURN_P else [("mixed", n, b) for b in range(T)]
-                wide[n] = take(chunks, [P, T, W], BF16, f"wide_{n}", "wide", WIDE_BUFS, freed)
-            src = bytes_q[q][:, g, t, :] if q < 2 else bytes_23[:, g, t, (q - 2) * W : (q - 1) * W]
+                if q < 2 and g > 0:
+                    both[g] = take(chunks, [P, T, 2 * W], BF16, f"wide_{g}", "wide", WIDE_BUFS, readers(g) + readers(g + G))
+                    wide[g], wide[g + G] = both[g][:, :, :W], both[g][:, :, W:]
+                else:
+                    wide[n] = take(chunks, [P, T, W], BF16, f"wide_{n}", "wide", WIDE_BUFS, readers(n))[:]
+            src = first_bytes[q][:, t] if q < 2 and g == 0 else pair_bytes[:, g - 1, t] if q < 2 else p_bytes[1][:, g, t, (q - 2) * W : (q - 1) * W]
+            dst = both[g][:, t, :] if count == 2 else wide[n][:, t, :]
             scale = scale_0[:, t : t + 1] if g == 0 else scale_rest[:, g - 1, t : t + 1]
             if engine == "S":
-                nc.scalar.activation(out=wide[n][:, t, :], in_=src.bitcast(FP8), func=COPY, scale=scale)
+                nc.scalar.activation(out=dst, in_=src.bitcast(FP8), func=COPY, scale=scale)
             else:
-                nc.vector.tensor_scalar(out=wide[n][:, t, :], in0=src.bitcast(FP8), scalar1=scale, scalar2=None, op0=MULT)
-            done.add(("wide", n, t))
+                nc.vector.tensor_scalar(out=dst, in0=src.bitcast(FP8), scalar1=scale, scalar2=None, op0=MULT)
+            note(("wide", n + G * k, t) for k in range(count))
             return True
 
         def mixed_tile(n):
@@ -154,7 +165,7 @@ def tile_two_sweep_policy_evaluation_d3_kernel(tc, P_bytes, P_scale, V, R, disco
                 return False
             copier[engine](
                 out=mixed[n][:].rearrange("p (b m e t) -> p m b t e", b=T, e=2, t=T)[:, :, b0:b1],
-                in_=wide[n][:].rearrange("p t (m e b) -> p m b t e", e=2, b=T)[:, :, b0:b1],
+                in_=wide[n].rearrange("p t (m e b) -> p m b t e", e=2, b=T)[:, :, b0:b1],
             )
             note(("mixed", n, b) for b in range(b0, b1))
             return True
@@ -171,7 +182,7 @@ def tile_two_sweep_policy_evaluation_d3_kernel(tc, P_bytes, P_scale, V, R, disco
             for j in range(2):
                 first = (2 * h + j) * P
                 nc.tensor.matmul(
-                    out=tile[:].rearrange("p (b j m t) -> p j t m b", b=tiles, j=2, t=T)[:, j],
+                    out=tile[:].rearrange("p (j b m t) -> p j t m b", j=2, b=tiles, t=T)[:, j],
                     lhsT=identity[:],
                     rhs=planes[:, :, first : first + P].rearrange("p t (m b) -> p t m b", b=tiles),
                     start=True,
@@ -188,8 +199,8 @@ def tile_two_sweep_policy_evaluation_d3_kernel(tc, P_bytes, P_scale, V, R, disco
                 if not mixed_tile(n):
                     return False
                 copier[engine](
-                    out=mixed[n][:].bitcast(F32).rearrange("p (b x) -> p b x", b=T)[:, :, h * P : (h + 1) * P],
-                    in_=words.rearrange("p (b x) -> p b x", b=T),
+                    out=mixed[n][:].bitcast(F32).rearrange("p (b h j x) -> p h b j x", b=T, h=2, j=2)[:, h],
+                    in_=words.rearrange("p (j b x) -> p b j x", j=2, b=T),
                 )
                 if ("emptied", kind, n, 1 - h) in done:
                     note(("mixed", n, b) for b in range(T))
@@ -315,9 +326,9 @@ def tile_two_sweep_policy_evaluation_d3_kernel(tc, P_bytes, P_scale, V, R, disco
                 if "late" not in turned:
                     if not ((1, G - 1) in v_mixed and slot_free("last", 1)):
                         return False
-                    turned["late"] = take(rows, [P, len(EXITS), C], F32, "late", "last", 1, [])
-                nc.gpsimd.tensor_tensor(out=turned["late"][:, tile], in0=parked[tile][:], in1=r_sb[:, q, b], op=ADD)
-                parked[tile] = turned["late"][:, tile]
+                    turned["late"] = take(rows, [P, len(EXITS) - 1, C], F32, "late", "last", 1, [])
+                nc.gpsimd.tensor_tensor(out=turned["late"][:, tile - 1], in0=parked[tile][:], in1=r_sb[:, q, b], op=ADD)
+                parked[tile] = turned["late"][:, tile - 1]
                 done.add(("rewarded", tile))
                 return True
             nc.vector.tensor_tensor(out=parked[tile][:], in0=parked[tile][:], in1=r_sb[:, q, b], op=ADD)
@@ -332,16 +343,11 @@ def tile_two_sweep_policy_evaluation_d3_kernel(tc, P_bytes, P_scale, V, R, disco
             if not needs <= done:
                 return False
             q, b = divmod(tile, T)
-            pair = tile // 2
-            if pair not in result:
-                result[pair] = results.tile([P, 2, C], F32, name=f"result_{q}_{b}", tag="result", bufs=5)
+            if tile not in result:
+                result[tile] = results.tile([P, C], F32, name=f"result_{q}_{b}", tag="result", bufs=RESULT_BUFS)
             addend = parked[tile][:, c0:c1] if tile in EXITS else r_sb[:, q, b, c0:c1]
-            update(result[pair][:, b % 2, c0:c1], acc[1, tile, c0][:], q, b, addend)
-            if pair not in PAIRED:
-                (nc.scalar if TWO_QUEUES and len(stored) % 2 else nc.sync).dma_start(out=out_view[q][:, b, c0:c1], in_=result[pair][:, b % 2, c0:c1])
-            elif b % 2 == 1:
-                nc.sync.dma_start(out=out_view[q][:, b - 1 : b + 1], in_=result[pair][:])
-            stored.append(tile)
+            update(result[tile][:, c0:c1], acc[1, tile, c0][:], q, b, addend)
+            nc.sync.dma_start(out=out_view[q][:, b, c0:c1], in_=result[tile][:, c0:c1])
             done.add(("result", tile, c0))
             return True
 
@@ -378,42 +384,41 @@ def tile_two_sweep_policy_evaluation_d3_kernel(tc, P_bytes, P_scale, V, R, disco
 
         def mx1(n, bs=range(T)):
             q, g = divmod(n, G)
-            return [(multiply, 0, T * q + b, g, b if g == 0 else None, g == G - 1) for b in bs]
+            return [(multiply, 0, T * q + b, g, b + T * (q // 2) if g == 0 else None, g == G - 1) for b in bs]
 
         def mx2(tile, gs, bank=None, c0=0, c1=C):
             return [(multiply, 1, tile, g, bank if g == gs[0] else None, g == G - 1 or g == EXITS.get(tile), c0, c1) for g in gs]
 
-        scalar = ws(0) + ws(1) + ws(2)
-        for g in range(G):
-            scalar = scalar + ws(3 + g) + ev("v", g)
-        scalar = scalar + ws(7) + ws(8) + weave(9, 7) + ws(10) + weave(11, 9) + ws(12) + ws(13) + ws(14) + ws(15) + [(park, 0), (park, 1)]
-        scalar = scalar + il(12, 2, 3) + [(park, 2), (park, 3)] + il(13, 2, 3) + il(14, 2, 3) + il(15, 2, 3) + [step for n in range(12, 16) for step in il(n, 3)] + ilv(2) + ilv(3, 0, HALF)
+        def w2(g, slots):
+            return [(widen, g, t, 2) for t in slots]
 
-        vector = wv(0) + il(0) + wv(1) + wv(2) + il(1) + qp(0) + wv(3)
-        for n in range(1, 5):
-            vector = vector + il(n + 1) + qp(n) + wv(n + 3) + qv(0, n - 1)
-        vector = vector + il(6) + qp(5) + wv(8) + upd(0) + qp(6) + wv(9) + ilv(0) + il(8) + qp(7) + wv(10) + qv(1, 0) + [(widen_discount,)]
-        vector = vector + qp(8) + wv(11) + il(10) + wv(12) + upd(1) + qp(9) + ilv(1) + qp(10) + il(11) + qv(1, 1) + wv(13) + qp(11) + wv(14) + il(12, 0, 2)
+        scalar = ws(0) + ws(4) + w2(1, [0, 1]) + w2(2, [0]) + ev("v", 0) + w2(2, [1]) + ev("v", 1) + w2(3, [0, 1]) + ev("v", 2) + w2(3, [2]) + ev("v", 3)
+        scalar = scalar + ws(8) + ev("p", 7)[:1] + ws(9)[:1] + ev("p", 7)[1:] + ws(9)[1:] + ws(10) + ws(11) + ev("p", 9)[:1] + ws(12)[:1] + ev("p", 9)[1:] + ws(12)[1:] + ws(13) + ws(14) + ws(15)
+        scalar = scalar + il(12, 2, 3) + [(park, 0), (park, 1)] + il(13, 2, 3) + [(park, 2), (park, 3)] + il(14, 2, 3) + il(15, 2, 3) + [step for n in range(12, 16) for step in il(n, 3)] + ilv(2) + ilv(3, 0, HALF)
+
+        vector = wv(0) + wv(4) + il(0) + w2(1, [2, 3]) + qp(0) + il(4) + il(1) + w2(2, [2, 3]) + qp(4) + qv(0, 0) + w2(3, [3]) + il(2) + qp(1) + il(5) + qv(0, 1)
+        vector = vector + qp(2) + il(6) + qp(5) + qv(0, 2) + il(3) + qp(6) + wv(8) + qp(3) + qv(0, 3) + wv(9) + il(8) + qp(7) + upd(0) + wv(10) + [(widen_discount,)]
+        vector = vector + wv(11) + qp(8) + il(10) + wv(12) + il(11) + qp(10) + qp(9) + upd(1) + ilv(0, HALF, C) + qp(11) + ilv(1) + qv(1, 0) + il(12, 0, 2) + qv(1, 1) + wv(13) + wv(14)
         vector = vector + wv(15) + upd(2) + qp(12, 0, 2) + il(13, 0, 2) + il(14, 0, 2) + qp(13, 0, 2) + il(15, 0, 2) + qp(14, 0, 2)
         vector = vector + qp(12, 2, 3) + qp(13, 2, 3) + qp(15, 0, 2) + qp(14, 2, 3) + qp(15, 2, 3) + qp(12, 3) + upd(3, [0]) + qp(13, 3) + qp(14, 3) + upd(3, [1]) + qp(15, 3) + upd(3, [2])
         vector = vector + [(add_reward, 0)] + upd(3, [3], 0, HALF) + upd(3, [3], HALF, C) + qv(1, 2) + ilv(3, HALF, C) + qv(1, 3, HALF, C) + qv(1, 3, 0, HALF)
         order = [8, 9, 10, 11, 4, 5, 6, 7, 0, 12, 1, 13, 2, 14, 3]
         vector = vector + [(finish, tile) for tile in order] + [(finish, 15, 0, HALF), (finish, 15, HALF, C)]
 
-        gpsimd = [(add_reward, tile) for tile in (1, 2, 3)]
-        tensor = tn("v", 0, 4) + tn("v", 1, 6) + tn("v", 2, 4) + mx1(0) + tn("v", 3, 6) + mx1(1) + mx1(2) + mx1(3)
-        tensor = tensor + tn("p", 7, 4) + mx1(4) + mx1(5) + tn("p", 9, 6) + mx1(6) + mx1(7) + mx2(0, [0], 4) + mx2(1, [0], 5) + mx2(2, [0], 6) + mx2(3, [0], 7) + mx1(8) + mx1(9) + mx1(10)
-        tensor = tensor + mx2(0, [1]) + mx2(1, [1]) + mx1(11) + mx2(2, [1]) + mx2(3, [1])
-        tensor = tensor + mx2(8, [0, 1], 4) + mx2(9, [0, 1], 5) + mx2(10, [0, 1], 6) + mx1(12, [0, 1]) + mx2(11, [0, 1], 7)
+        gpsimd = ilv(0, 0, HALF) + [(add_reward, tile) for tile in (1, 2, 3)]
+        tensor = tn("v", 0, 4) + tn("v", 1, 6) + tn("v", 2, 4) + mx1(0) + tn("v", 3, 6) + mx1(1) + tn("p", 7, 4) + mx1(2) + mx1(3)
+        tensor = tensor + tn("p", 9, 6) + mx1(4) + mx1(5) + mx1(6) + mx1(7) + mx1(8) + mx1(9) + mx1(10) + mx1(11)
+        tensor = tensor + mx2(0, [0], 0) + mx2(1, [0], 1) + mx2(2, [0], 2) + mx2(3, [0], 3) + mx2(0, [1]) + mx2(1, [1]) + mx2(2, [1]) + mx2(3, [1])
+        tensor = tensor + mx2(8, [0, 1], 0) + mx2(9, [0, 1], 1) + mx1(12, [0, 1]) + mx2(10, [0, 1], 2) + mx2(11, [0, 1], 3)
         tensor = tensor + mx1(13, [0, 1]) + mx1(14, [0, 1]) + mx1(15, [0, 1]) + mx1(12, [2]) + mx1(13, [2]) + mx1(14, [2]) + mx1(15, [2])
         tensor = tensor + mx1(12, [3]) + mx1(13, [3]) + mx1(14, [3]) + mx1(15, [3])
         for tile in range(4, 8):
-            tensor = tensor + mx2(tile, [0, 1], tile - 4)
+            tensor = tensor + mx2(tile, [0, 1], tile)
         for tile in order[:AHEAD]:
             tensor = tensor + mx2(tile, [2])
         for k, tile in enumerate(order[:8]):
             tensor = tensor + mx2(tile, [3]) + [step for later in order[AHEAD + k : 8][:1] for step in mx2(later, [2])]
-        banks = [4, 5, 6, 7, 0, 1, 2, 3]
+        banks = list(range(8))
         for tile, bank in zip(order[8:], banks):
             tensor = tensor + mx2(tile, list(range(EXITS[tile] + 1, G)) if tile in EXITS else [0, 1, 2, 3], bank)
         tensor = tensor + mx2(15, [0, 1, 2, 3], banks[7], 0, HALF) + mx2(15, [0, 1, 2, 3], banks[0], HALF, C)

@@ -22,25 +22,22 @@ COPY = mybir.ActivationFunctionType.Copy
 
 FLOPS = 2 * 2 * S * S * C
 
-TURN_P = (7, 9)
+TURN_P = (4, 7)
+SCALAR_TILES = (11, 14)
+TILED = 2
 EXITS = {0: 1, 1: 1, 2: 1, 3: 1}
-WIDE_BUFS = 5
+WIDE_BUFS = 3
 MIXED_BUFS = 4
-V_SLOTS = [3, 0, 0, 0] + [1, 0, 0, 0] + [0, 1, 0, 1] + [0, 0, 0, 0]
-AHEAD = 5
-RESULT_BUFS = 8
-HELD = 9
+MIXED_S_BUFS = 2
+V_MIXED_BUFS = 3
 
 
 def tile_two_sweep_policy_evaluation_d3_kernel(tc, P_bytes, P_scale, V, R, discount, out):
     nc = tc.nc
-    copier = {"V": nc.vector.tensor_copy, "S": nc.scalar.copy}
 
     with ExitStack() as ctx:
         keep = ctx.enter_context(tc.tile_pool(name="keep", bufs=1))
-        chunks = ctx.enter_context(tc.tile_pool(name="chunks", bufs=5))
-        rows = ctx.enter_context(tc.tile_pool(name="rows", bufs=3))
-        results = ctx.enter_context(tc.tile_pool(name="results", bufs=8))
+        stream = ctx.enter_context(tc.tile_pool(name="stream", bufs=1))
         psum = ctx.enter_context(tc.psum_pool(name="psum", bufs=1))
         ctx.enter_context(tc.manual_schedule())
 
@@ -50,11 +47,11 @@ def tile_two_sweep_policy_evaluation_d3_kernel(tc, P_bytes, P_scale, V, R, disco
         disc32 = keep.tile([P, G, T], F32, name="disc32")
         first_bytes = [keep.tile([P, T, W], U8, name=f"first_bytes_{q}", align_bytes=64) for q in range(2)]
         pair_bytes = keep.tile([P, G - 1, T, 2 * W], U8, name="bytes_01", align_bytes=64)
-        p_bytes = [None, keep.tile([P, G, T, 2 * W], U8, name="bytes_23", align_bytes=64)]
+        late_bytes = keep.tile([P, G, T, 2 * W], U8, name="bytes_23", align_bytes=64)
         v_raw = keep.tile([P, G, T, C], BF16, name="v_raw", align_bytes=64)
         r_sb = keep.tile([P, G, T, C], BF16, name="r_sb", align_bytes=64)
-        p_codes = keep.tile([P, G, G, W], U32, name="p_codes", align_bytes=64)
-        p_scales = keep.tile([P, G, G, W], U8, name="p_scales", align_bytes=64)
+        p_codes = keep.tile([P, G * G, W], U32, name="p_codes", align_bytes=64)
+        p_scales = keep.tile([P, G * G, W], U8, name="p_scales", align_bytes=64)
         v_codes = [keep.tile([P, G, C], U32, name=f"v_codes_{s}", align_bytes=64) for s in range(2)]
         v_scales = [keep.tile([P, G, C], U8, name=f"v_scales_{s}", align_bytes=64) for s in range(2)]
 
@@ -73,32 +70,44 @@ def tile_two_sweep_policy_evaluation_d3_kernel(tc, P_bytes, P_scale, V, R, disco
         def load_pair(g):
             nc.sync.dma_start(out=pair_bytes[:, g - 1], in_=p_view[g][:, :, : 2 * W])
 
+        def load_late(g):
+            nc.sync.dma_start(out=late_bytes[:, g], in_=p_view[g][:, :, 2 * W :])
+
+        def load_v(g):
+            nc.sync.dma_start(out=v_raw[:, g], in_=v_view[g])
+
+        def load_r(q):
+            nc.sync.dma_start(out=r_sb[:, q], in_=r_view[q])
+
         nc.scalar.dma_start(out=scale_0[:], in_=scale_view[:, 0])
         load_first(0)
         nc.scalar.dma_start(out=scale_rest[:], in_=scale_view[:, 1:])
         load_first(1)
         load_pair(1)
-        nc.sync.dma_start(out=v_raw[:, 0], in_=v_view[0])
         load_pair(2)
-        nc.sync.dma_start(out=v_raw[:, 1], in_=v_view[1])
+        load_v(0)
+        load_v(1)
         load_pair(3)
-        nc.sync.dma_start(out=v_raw[:, 2], in_=v_view[2])
-        nc.sync.dma_start(out=v_raw[:, 3], in_=v_view[3])
+        load_v(2)
+        load_late(0)
+        load_v(3)
+        load_late(1)
         nc.sync.dma_start(out=disc[:], in_=discount.rearrange("(g p t) o -> p g (t o)", p=P, t=T))
-        nc.sync.dma_start(out=r_sb[:, 0], in_=r_view[0])
-        for g in range(G):
-            nc.sync.dma_start(out=p_bytes[1][:, g], in_=p_view[g][:, :, 2 * W :])
+        load_late(2)
+        load_r(0)
+        load_late(3)
         for q in range(1, G):
-            nc.sync.dma_start(out=r_sb[:, q], in_=r_view[q])
+            load_r(q)
 
         wide = {}
+        slots = {}
         mixed = {}
         v_mixed = {}
         v1_rows = {}
         turned = {}
-        both = {}
         parked = {}
         acc = {}
+        results = {}
         copier = {"V": nc.vector.tensor_copy, "S": nc.scalar.copy}
         done = set()
         waits = {}
@@ -114,67 +123,79 @@ def tile_two_sweep_policy_evaluation_d3_kernel(tc, P_bytes, P_scale, V, R, disco
             users = waits.setdefault(tag, [])
             return len(users) < depth or users[len(users) - depth] <= done
 
-        def take(pool, shape, dtype, name, tag, depth, freed_by):
+        def take(shape, dtype, name, tag, depth, freed_by):
             waits[tag].append(set(freed_by))
-            return pool.tile(shape, dtype, name=name, tag=tag, bufs=depth, align_bytes=64)
+            return stream.tile(shape, dtype, name=name, tag=tag, bufs=depth, align_bytes=64)
 
         def readers(n):
-            return [("turned", "p", n, h) for h in range(2)] if n in TURN_P else [("mixed", n, b) for b in range(T)]
+            return [("turned", "p", n, h) for h in range(2)] if n in TURN_P else [("mixed", n, k) for k in range(T)]
 
-        def widen(engine, n, t, count=1):
-            q, g = divmod(n, G)
-            if n not in wide:
+        def wide_slot(key):
+            if key not in slots:
                 if not slot_free("wide", WIDE_BUFS):
                     return False
-                if q < 2 and g > 0:
-                    both[g] = take(chunks, [P, T, 2 * W], BF16, f"wide_{g}", "wide", WIDE_BUFS, readers(g) + readers(g + G))
-                    wide[g], wide[g + G] = both[g][:, :, :W], both[g][:, :, W:]
-                else:
-                    wide[n] = take(chunks, [P, T, W], BF16, f"wide_{n}", "wide", WIDE_BUFS, readers(n))[:]
-            src = first_bytes[q][:, t] if q < 2 and g == 0 else pair_bytes[:, g - 1, t] if q < 2 else p_bytes[1][:, g, t, (q - 2) * W : (q - 1) * W]
-            dst = both[g][:, t, :] if count == 2 else wide[n][:, t, :]
+                units = [2 * key, 2 * key + 1, 2 * key + G, 2 * key + G + 1] if key < 2 else range(T * key, T * key + T)
+                slots[key] = take([P, G * T * W], BF16, f"wide_{key}", "wide", WIDE_BUFS, [fact for n in units for fact in readers(n)])
+            return True
+
+        def planes_of(q, g):
+            if q >= 2:
+                return slots[q][:].rearrange("p (g t i) -> p g t i", g=G, t=T)[:, g]
+            if g == 0:
+                return slots[0][:, q * T * W : (q + 1) * T * W].rearrange("p (t i) -> p t i", t=T)
+            half = slots[g // 2][:, (g % 2) * 2 * T * W : (g % 2 + 1) * 2 * T * W]
+            return half.rearrange("p (t q i) -> p q t i", t=T, q=2)[:, q]
+
+        def widen(engine, q, g, t, count=1):
+            if not wide_slot(q if q >= 2 else g // 2):
+                return False
+            if count == 2:
+                first = ((g % 2) * T + t) * 2 * W
+                src, dst = pair_bytes[:, g - 1, t], slots[g // 2][:, first : first + 2 * W]
+            else:
+                src = first_bytes[q][:, t] if q < 2 else late_bytes[:, g, t, (q - 2) * W : (q - 1) * W]
+                dst = planes_of(q, g)[:, t]
             scale = scale_0[:, t : t + 1] if g == 0 else scale_rest[:, g - 1, t : t + 1]
             if engine == "S":
                 nc.scalar.activation(out=dst, in_=src.bitcast(FP8), func=COPY, scale=scale)
             else:
                 nc.vector.tensor_scalar(out=dst, in0=src.bitcast(FP8), scalar1=scale, scalar2=None, op0=MULT)
-            note(("wide", n + G * k, t) for k in range(count))
+            note(("wide", q + k, g, t) for k in range(count))
             return True
 
         def mixed_tile(n):
-            if n == HELD and n not in mixed and slot_free("held", 1):
-                mixed[n] = take(chunks, [P, W * T], BF16, f"mixed_{n}", "held", 1, [("codes", n, b) for b in range(T)])
-            if n not in mixed and slot_free("mixed", MIXED_BUFS):
-                mixed[n] = take(chunks, [P, W * T], BF16, f"mixed_{n}", "mixed", MIXED_BUFS, [("codes", n, b) for b in range(T)])
+            tag, depth = ("mixed_s", MIXED_S_BUFS) if n in TURN_P + SCALAR_TILES else ("mixed", MIXED_BUFS)
+            if n not in mixed and slot_free(tag, depth):
+                mixed[n] = take([P, W * T], BF16, f"mixed_{n}", tag, depth, [("codes", n, k) for k in range(T)])
             return n in mixed
 
         def v_mixed_tile(sweep, g):
-            if (sweep, g) == (1, G - 1) and (sweep, g) not in v_mixed and slot_free("last", 1):
-                v_mixed[sweep, g] = take(rows, [P, C, T], BF16, "v_mixed_last", "last", 1, [("v_codes", sweep, g, k) for k in range(T)])
-            if (sweep, g) == (1, 0) and HELD is not None:
-                if (sweep, g) not in v_mixed and HELD in mixed and slot_free("held", 1):
-                    v_mixed[sweep, g] = take(chunks, [P, C, T], BF16, "v_mixed_1_0", "held", 1, [])
-                return (sweep, g) in v_mixed
-            if (sweep, g) not in v_mixed and slot_free("v_mixed", 3):
-                freed = [("v_codes", sweep, g, k) for k in range(T)]
-                v_mixed[sweep, g] = take(rows, [P, C, T], BF16, f"v_mixed_{sweep}_{g}", "v_mixed", 3, freed)
+            tag, depth = ("last", 1) if (sweep, g) == (1, G - 1) else ("v_mixed", V_MIXED_BUFS)
+            if (sweep, g) not in v_mixed and slot_free(tag, depth):
+                v_mixed[sweep, g] = take([P, C, T], BF16, f"v_mixed_{sweep}_{g}", tag, depth, [("v_codes", sweep, g, k) for k in range(T)])
             return (sweep, g) in v_mixed
 
-        def interleave(engine, n, b0, b1):
-            if not ({("wide", n, t) for t in range(T)} <= done and mixed_tile(n)):
+        def interleave(engine, n, k0, k1):
+            q, r = divmod(n, G)
+            groups = [r] if q < TILED else range(k0, k1)
+            if not ({("wide", q, g, t) for g in groups for t in range(T)} <= done and mixed_tile(n)):
                 return False
-            copier[engine](
-                out=mixed[n][:].rearrange("p (b m e t) -> p m b t e", b=T, e=2, t=T)[:, :, b0:b1],
-                in_=wide[n].rearrange("p t (m e b) -> p m b t e", e=2, b=T)[:, :, b0:b1],
-            )
-            note(("mixed", n, b) for b in range(b0, b1))
+            if q < TILED:
+                dst = mixed[n][:].rearrange("p (b m e t) -> p m b t e", b=T, e=2, t=T)[:, :, k0:k1]
+                src = planes_of(q, r).rearrange("p t (m e b) -> p m b t e", e=2, b=T)[:, :, k0:k1]
+            else:
+                dst = mixed[n][:].rearrange("p (g m e t) -> p g m t e", g=G, e=2, t=T)[:, k0:k1]
+                src = slots[q][:].rearrange("p (g t m e b) -> p b g m t e", g=G, t=T, e=2, b=T)[:, r, k0:k1]
+            copier[engine](out=dst, in_=src)
+            note(("mixed", n, k) for k in range(k0, k1))
             return True
 
         def turn(engine, kind, n, h, bank):
-            needs = {"p": {("wide", n, t) for t in range(T)}, "v": set(), "u": {("row", n, b, k) for b in range(T) for k in (2 * h, 2 * h + 1)}}[kind]
+            q, g = divmod(n, G)
+            needs = {"p": {("wide", q, g, t) for t in range(T)}, "v": set(), "u": {("row", n, b, k) for b in range(T) for k in (2 * h, 2 * h + 1)}}[kind]
             if not (needs <= done and slot_free(f"bank_{bank}", 1)):
                 return False
-            planes = wide[n] if kind == "p" else v_raw[:, n] if kind == "v" else v1_rows[n]
+            planes = planes_of(q, g) if kind == "p" else v_raw[:, n] if kind == "v" else v1_rows[n][:]
             tiles = T if kind == "p" else 1
             waits[f"bank_{bank}"].append({("emptied", kind, n, h)})
             tile = psum.tile([P, 2 * W], BF16, name=f"turn_{kind}{n}_{h}", tag=f"bank_{bank}")
@@ -213,40 +234,38 @@ def tile_two_sweep_policy_evaluation_d3_kernel(tc, P_bytes, P_scale, V, R, disco
             done.add(("emptied", kind, n, h))
             return True
 
-        def quantise(engine, n, b0, b1):
-            if not {("mixed", n, b) for b in range(b0, b1)} <= done:
+        def quantise(engine, n, k0, k1):
+            if not {("mixed", n, k) for k in range(k0, k1)} <= done:
                 return False
-            q, g = divmod(n, G)
-            cols = slice(b0 * P, b1 * P)
+            cols = slice(k0 * P, k1 * P)
             nc.vector.quantize_mx(
-                out=p_codes[:, q, g, cols].bitcast(FP8X4),
-                scales=p_scales[:, q, g, cols],
-                in_=mixed[n][:, b0 * P * T : b1 * P * T],
+                out=p_codes[:, n, cols].bitcast(FP8X4),
+                scales=p_scales[:, n, cols],
+                in_=mixed[n][:, k0 * P * T : k1 * P * T],
             )
-            note(("codes", n, b) for b in range(b0, b1))
+            note(("codes", n, k) for k in range(k0, k1))
             return True
 
-        def interleave_v(engine, sweep, g, c0, c1):
-            needs = {("row", g, b, k) for b in range(T) for k in quarters(c0, c1)} if sweep == 1 else set()
-            if not (needs <= done and v_mixed_tile(sweep, g)):
+        def interleave_v(engine, g, c0, c1):
+            needs = {("row", g, b, k) for b in range(T) for k in quarters(c0, c1)}
+            if not (needs <= done and v_mixed_tile(1, g)):
                 return False
-            src = v_raw[:, g] if sweep == 0 else v1_rows[g][:]
+            src = v1_rows[g][:]
             if engine == "G":
                 nc.gpsimd.tensor_scalar(
-                    out=v_mixed[sweep, g][:, c0:c1, :],
+                    out=v_mixed[1, g][:, c0:c1, :],
                     in0=src[:, :, c0:c1].rearrange("p t c -> p c t"),
                     scalar1=1.0,
                     scalar2=0.0,
                     op0=MULT,
                     op1=ADD,
                 )
-                note(("v_mixed", sweep, g, k) for k in quarters(c0, c1))
-                return True
-            copier[engine](
-                out=v_mixed[sweep, g][:, c0:c1, :].rearrange("p (c i) t -> p c t i", i=4),
-                in_=src[:, :, c0:c1].rearrange("p t (c i) -> p c t i", i=4),
-            )
-            note(("v_mixed", sweep, g, k) for k in quarters(c0, c1))
+            else:
+                copier[engine](
+                    out=v_mixed[1, g][:, c0:c1, :].rearrange("p (c i) t -> p c t i", i=4),
+                    in_=src[:, :, c0:c1].rearrange("p t (c i) -> p c t i", i=4),
+                )
+            note(("v_mixed", 1, g, k) for k in quarters(c0, c1))
             return True
 
         def quantise_v(engine, sweep, g, c0, c1):
@@ -262,21 +281,22 @@ def tile_two_sweep_policy_evaluation_d3_kernel(tc, P_bytes, P_scale, V, R, disco
 
         def multiply(engine, sweep, tile, g, bank=None, close=False, c0=0, c1=C):
             q, b = divmod(tile, T)
-            needs = {("codes", G * q + g, b)} | {("v_codes", sweep, g, k) for k in quarters(c0, c1)}
+            n, k = (G * q + g, b) if q < TILED else (tile, g)
+            needs = {("codes", n, k)} | {("v_codes", sweep, g, j) for j in quarters(c0, c1)}
             if not (needs <= done and (bank is None or slot_free(f"bank_{bank}", 1))):
                 return False
             if bank is not None:
                 if sweep == 0:
-                    freed = {("row", q, b, k) for k in range(T)}
+                    freed = {("row", q, b, j) for j in range(T)}
                 else:
                     freed = {("parked", tile) if g == 0 and tile in EXITS else ("result", tile, c0)}
                 waits[f"bank_{bank}"].append(freed)
-                acc[sweep, tile, c0] = psum.tile([P, c1 - c0], F32, name=f"acc_{sweep}_{q}_{b}", tag=f"bank_{bank}")
-            cols = slice(b * P, (b + 1) * P)
+                acc[sweep, tile, c0] = psum.tile([P, c1 - c0], F32, name=f"acc_{sweep}_{tile}", tag=f"bank_{bank}")
+            cols = slice(k * P, (k + 1) * P)
             nc.tensor.matmul_mx(
                 out=acc[sweep, tile, c0][:],
-                lhsT=p_codes[:, q, g, cols].bitcast(FP8X4),
-                lhsT_scale=p_scales[:, q, g, cols],
+                lhsT=p_codes[:, n, cols].bitcast(FP8X4),
+                lhsT_scale=p_scales[:, n, cols],
                 rhs=v_codes[sweep][:, g, c0:c1].bitcast(FP8X4),
                 rhs_scale=v_scales[sweep][:, g, c0:c1],
                 start=bank is not None,
@@ -289,14 +309,15 @@ def tile_two_sweep_policy_evaluation_d3_kernel(tc, P_bytes, P_scale, V, R, disco
         def update(dst, sums, q, b, addend):
             nc.vector.scalar_tensor_tensor(out=dst, in0=sums, scalar=disc[:, q, b : b + 1], in1=addend, op0=MULT, op1=ADD)
 
-        def update_v1(engine, q, b, c0, c1):
-            if ("sum", 0, T * q + b, G - 1, 0) not in done:
+        def update_v1(engine, tile, c0, c1):
+            q, b = divmod(tile, T)
+            if ("sum", 0, tile, G - 1, 0) not in done:
                 return False
             if q not in v1_rows:
                 if not slot_free("v1_rows", 2):
                     return False
-                v1_rows[q] = take(rows, [P, T, C], BF16, f"v1_rows_{q}", "v1_rows", 2, [("v_mixed", 1, q, k) for k in range(T)])
-            update(v1_rows[q][:, b, c0:c1], acc[0, T * q + b, 0][:, c0:c1], q, b, r_sb[:, q, b, c0:c1])
+                v1_rows[q] = take([P, T, C], BF16, f"v1_rows_{q}", "v1_rows", 2, [("v_mixed", 1, q, k) for k in range(T)])
+            update(v1_rows[q][:, b, c0:c1], acc[0, tile, 0][:, c0:c1], q, b, r_sb[:, q, b, c0:c1])
             note(("row", q, b, k) for k in quarters(c0, c1))
             return True
 
@@ -309,12 +330,12 @@ def tile_two_sweep_policy_evaluation_d3_kernel(tc, P_bytes, P_scale, V, R, disco
             if not {("sum", 1, tile, EXITS[tile], 0), ("disc32",)} <= done:
                 return False
             q, b = divmod(tile, T)
-            parked[tile] = results.tile([P, C], F32, name=f"parked_{q}_{b}", tag="parked", bufs=len(EXITS))
+            parked[tile] = stream.tile([P, C], F32, name=f"parked_{tile}", tag="parked", bufs=len(EXITS))[:]
             if engine == "V":
-                update(parked[tile][:], acc[1, tile, 0][:], q, b, r_sb[:, q, b])
+                update(parked[tile], acc[1, tile, 0][:], q, b, r_sb[:, q, b])
                 done.add(("rewarded", tile))
             else:
-                nc.scalar.activation(out=parked[tile][:], in_=acc[1, tile, 0][:], func=COPY, scale=disc32[:, q, b : b + 1])
+                nc.scalar.activation(out=parked[tile], in_=acc[1, tile, 0][:], func=COPY, scale=disc32[:, q, b : b + 1])
             done.add(("parked", tile))
             return True
 
@@ -322,59 +343,57 @@ def tile_two_sweep_policy_evaluation_d3_kernel(tc, P_bytes, P_scale, V, R, disco
             if ("parked", tile) not in done:
                 return False
             q, b = divmod(tile, T)
-            if engine == "G":
-                if "late" not in turned:
-                    if not ((1, G - 1) in v_mixed and slot_free("last", 1)):
-                        return False
-                    turned["late"] = take(rows, [P, len(EXITS) - 1, C], F32, "late", "last", 1, [])
-                nc.gpsimd.tensor_tensor(out=turned["late"][:, tile - 1], in0=parked[tile][:], in1=r_sb[:, q, b], op=ADD)
-                parked[tile] = turned["late"][:, tile - 1]
-                done.add(("rewarded", tile))
-                return True
-            nc.vector.tensor_tensor(out=parked[tile][:], in0=parked[tile][:], in1=r_sb[:, q, b], op=ADD)
+            if "late" not in turned:
+                if not ((1, G - 1) in v_mixed and slot_free("last", 1)):
+                    return False
+                turned["late"] = take([P, len(EXITS), C], F32, "late", "last", 1, [])
+            dst = turned["late"][:, list(EXITS).index(tile)]
+            nc.gpsimd.tensor_tensor(out=dst, in0=parked[tile], in1=r_sb[:, q, b], op=ADD)
+            parked[tile] = dst
             done.add(("rewarded", tile))
             return True
 
-        result = {}
-        stored = []
+        finished = []
 
         def finish(engine, tile, c0=0, c1=C):
             needs = {("sum", 1, tile, G - 1, c0)} | ({("rewarded", tile)} if tile in EXITS else set())
             if not needs <= done:
                 return False
             q, b = divmod(tile, T)
-            if tile not in result:
-                result[tile] = results.tile([P, C], F32, name=f"result_{q}_{b}", tag="result", bufs=RESULT_BUFS)
+            if tile not in finished:
+                finished.append(tile)
+            half, place = divmod(finished.index(tile), 2 * T)
+            if half not in results:
+                if not slot_free("wide", WIDE_BUFS):
+                    return False
+                results[half] = take([P, 2 * T, C], F32, f"results_{half}", "wide", WIDE_BUFS, [])
+            dst = results[half][:, place, c0:c1]
             addend = parked[tile][:, c0:c1] if tile in EXITS else r_sb[:, q, b, c0:c1]
-            update(result[tile][:, c0:c1], acc[1, tile, c0][:], q, b, addend)
-            nc.sync.dma_start(out=out_view[q][:, b, c0:c1], in_=result[tile][:, c0:c1])
+            update(dst, acc[1, tile, c0][:], q, b, addend)
+            nc.sync.dma_start(out=out_view[q][:, b, c0:c1], in_=dst)
             done.add(("result", tile, c0))
             return True
 
-        def ws(n):
-            return [(widen, n, t) for t in range(T - V_SLOTS[n])]
+        def w1(q, g, ts=range(T)):
+            return [(widen, q, g, t) for t in ts]
 
-        def wv(n):
-            return [(widen, n, t) for t in range(T - V_SLOTS[n], T)]
+        def w2(g, ts):
+            return [(widen, 0, g, t, 2) for t in ts]
 
-        def ev(kind, n):
-            return [(empty, kind, n, h) for h in range(2)]
+        def ev(kind, n, hs=range(2)):
+            return [(empty, kind, n, h) for h in hs]
 
-        def weave(n, c):
-            a, e = ws(n), ev("p", c)
-            return a[:2] + e[:1] + a[2:3] + e[1:] + a[3:]
+        def il(n, k0=0, k1=T):
+            return [(interleave, n, k0, k1)]
 
-        def il(n, b0=0, b1=T):
-            return [(interleave, n, b0, b1)]
+        def qp(n, k0=0, k1=T):
+            return [(quantise, n, k0, k1)]
 
-        def qp(n, b0=0, b1=T):
-            return [(quantise, n, b0, b1)]
-
-        def upd(q, bs=range(T), c0=0, c1=C):
-            return [(update_v1, q, b, c0, c1) for b in bs]
+        def upd(tiles, c0=0, c1=C):
+            return [(update_v1, tile, c0, c1) for tile in tiles]
 
         def ilv(g, c0=0, c1=C):
-            return [(interleave_v, 1, g, c0, c1)]
+            return [(interleave_v, g, c0, c1)]
 
         def qv(sweep, g, c0=0, c1=C):
             return [(quantise_v, sweep, g, c0, c1)]
@@ -382,47 +401,39 @@ def tile_two_sweep_policy_evaluation_d3_kernel(tc, P_bytes, P_scale, V, R, disco
         def tn(kind, n, bank):
             return [(turn, kind, n, h, bank + h) for h in range(2)]
 
-        def mx1(n, bs=range(T)):
-            q, g = divmod(n, G)
-            return [(multiply, 0, T * q + b, g, b + T * (q // 2) if g == 0 else None, g == G - 1) for b in bs]
+        def mx1(tiles, gs, bank=None):
+            return [(multiply, 0, tile, g, bank + j if g == 0 else None, g == G - 1) for g in gs for j, tile in enumerate(tiles)]
 
         def mx2(tile, gs, bank=None, c0=0, c1=C):
             return [(multiply, 1, tile, g, bank if g == gs[0] else None, g == G - 1 or g == EXITS.get(tile), c0, c1) for g in gs]
 
-        def w2(g, slots):
-            return [(widen, g, t, 2) for t in slots]
+        scalar = w1(0, 0, [0]) + w1(1, 0, [0, 1]) + w2(1, [0, 1]) + w2(2, [0]) + ev("p", 4) + w2(2, [1]) + ev("v", 0) + w2(3, [0]) + ev("v", 1) + w1(2, 0, [0, 1]) + ev("v", 2) + w1(2, 0, [2, 3]) + ev("v", 3)
+        scalar = scalar + w1(2, 1, [0, 1]) + ev("p", 7) + w1(2, 1, [2, 3]) + w1(2, 2) + w1(2, 3, [0]) + w1(3, 0) + w1(3, 1) + il(11) + w1(3, 2, [0, 1]) + ev("u", 1) + w1(3, 2, [2, 3]) + w1(3, 3)
+        scalar = scalar + [(park, 0), (park, 1)] + il(14) + [(park, 2)] + ilv(2) + il(15, 2, 4) + [(park, 3)] + ilv(3, 3 * P, C)
 
-        scalar = ws(0) + ws(4) + w2(1, [0, 1]) + w2(2, [0]) + ev("v", 0) + w2(2, [1]) + ev("v", 1) + w2(3, [0, 1]) + ev("v", 2) + w2(3, [2]) + ev("v", 3)
-        scalar = scalar + ws(8) + ev("p", 7)[:1] + ws(9)[:1] + ev("p", 7)[1:] + ws(9)[1:] + ws(10) + ws(11) + ev("p", 9)[:1] + ws(12)[:1] + ev("p", 9)[1:] + ws(12)[1:] + ws(13) + ws(14) + ws(15)
-        scalar = scalar + il(12, 2, 3) + [(park, 0), (park, 1)] + il(13, 2, 3) + [(park, 2), (park, 3)] + il(14, 2, 3) + il(15, 2, 3) + [step for n in range(12, 16) for step in il(n, 3)] + ilv(2) + ilv(3, 0, HALF)
-
-        vector = wv(0) + wv(4) + il(0) + w2(1, [2, 3]) + qp(0) + il(4) + il(1) + w2(2, [2, 3]) + qp(4) + qv(0, 0) + w2(3, [3]) + il(2) + qp(1) + il(5) + qv(0, 1)
-        vector = vector + qp(2) + il(6) + qp(5) + qv(0, 2) + il(3) + qp(6) + wv(8) + qp(3) + qv(0, 3) + wv(9) + il(8) + qp(7) + upd(0) + wv(10) + [(widen_discount,)]
-        vector = vector + wv(11) + qp(8) + il(10) + wv(12) + il(11) + qp(10) + qp(9) + upd(1) + ilv(0, HALF, C) + qp(11) + ilv(1) + qv(1, 0) + il(12, 0, 2) + qv(1, 1) + wv(13) + wv(14)
-        vector = vector + wv(15) + upd(2) + qp(12, 0, 2) + il(13, 0, 2) + il(14, 0, 2) + qp(13, 0, 2) + il(15, 0, 2) + qp(14, 0, 2)
-        vector = vector + qp(12, 2, 3) + qp(13, 2, 3) + qp(15, 0, 2) + qp(14, 2, 3) + qp(15, 2, 3) + qp(12, 3) + upd(3, [0]) + qp(13, 3) + qp(14, 3) + upd(3, [1]) + qp(15, 3) + upd(3, [2])
-        vector = vector + [(add_reward, 0)] + upd(3, [3], 0, HALF) + upd(3, [3], HALF, C) + qv(1, 2) + ilv(3, HALF, C) + qv(1, 3, HALF, C) + qv(1, 3, 0, HALF)
-        order = [8, 9, 10, 11, 4, 5, 6, 7, 0, 12, 1, 13, 2, 14, 3]
+        vector = w1(0, 0, [1, 2, 3]) + w1(1, 0, [2, 3]) + il(0) + w2(1, [2, 3]) + qp(0) + w2(2, [2]) + il(1) + w2(2, [3]) + il(5) + qp(1) + qp(4) + w2(3, [1, 2, 3]) + qv(0, 0) + il(2) + qp(5) + qv(0, 1)
+        vector = vector + il(3) + qp(2) + qv(0, 2) + il(6) + qp(3) + qv(0, 3) + qp(6) + w1(2, 3, [1, 2, 3]) + [(widen_discount,)] + qp(7) + upd(range(2))
+        vector = vector + il(8) + upd([2]) + qp(8) + upd(range(3, 8)) + il(9) + ilv(0, HALF, C) + qp(9) + qv(1, 0) + il(10) + upd([8]) + qp(10) + qv(1, 1) + qp(11) + upd([9, 10])
+        vector = vector + il(12) + upd([11]) + qp(12) + il(13) + qp(14) + upd([12]) + qp(13) + il(15, 0, 2) + upd([14]) + qp(15, 0, 2) + qv(1, 2) + qp(15, 2, 4) + upd([13])
+        vector = vector + upd([15], 0, HALF) + upd([15], HALF, C) + ilv(3, 0, HALF) + ilv(3, HALF, 3 * P) + qv(1, 3, 0, HALF) + qv(1, 3, HALF, C)
+        order = [4, 5, 6, 7, 8, 9, 10, 11, 0, 12, 1, 13, 2, 14, 3]
         vector = vector + [(finish, tile) for tile in order] + [(finish, 15, 0, HALF), (finish, 15, HALF, C)]
 
-        gpsimd = ilv(0, 0, HALF) + [(add_reward, tile) for tile in (1, 2, 3)]
-        tensor = tn("v", 0, 4) + tn("v", 1, 6) + tn("v", 2, 4) + mx1(0) + tn("v", 3, 6) + mx1(1) + tn("p", 7, 4) + mx1(2) + mx1(3)
-        tensor = tensor + tn("p", 9, 6) + mx1(4) + mx1(5) + mx1(6) + mx1(7) + mx1(8) + mx1(9) + mx1(10) + mx1(11)
-        tensor = tensor + mx2(0, [0], 0) + mx2(1, [0], 1) + mx2(2, [0], 2) + mx2(3, [0], 3) + mx2(0, [1]) + mx2(1, [1]) + mx2(2, [1]) + mx2(3, [1])
-        tensor = tensor + mx2(8, [0, 1], 0) + mx2(9, [0, 1], 1) + mx1(12, [0, 1]) + mx2(10, [0, 1], 2) + mx2(11, [0, 1], 3)
-        tensor = tensor + mx1(13, [0, 1]) + mx1(14, [0, 1]) + mx1(15, [0, 1]) + mx1(12, [2]) + mx1(13, [2]) + mx1(14, [2]) + mx1(15, [2])
-        tensor = tensor + mx1(12, [3]) + mx1(13, [3]) + mx1(14, [3]) + mx1(15, [3])
-        for tile in range(4, 8):
-            tensor = tensor + mx2(tile, [0, 1], tile)
-        for tile in order[:AHEAD]:
-            tensor = tensor + mx2(tile, [2])
-        for k, tile in enumerate(order[:8]):
-            tensor = tensor + mx2(tile, [3]) + [step for later in order[AHEAD + k : 8][:1] for step in mx2(later, [2])]
-        banks = list(range(8))
-        for tile, bank in zip(order[8:], banks):
-            tensor = tensor + mx2(tile, list(range(EXITS[tile] + 1, G)) if tile in EXITS else [0, 1, 2, 3], bank)
-        tensor = tensor + mx2(15, [0, 1, 2, 3], banks[7], 0, HALF) + mx2(15, [0, 1, 2, 3], banks[0], HALF, C)
+        gpsimd = ilv(0, 0, HALF) + [(add_reward, tile) for tile in EXITS]
 
+        every = list(range(G))
+        tensor = tn("p", 4, 4) + tn("v", 0, 6) + tn("v", 1, 4) + tn("v", 2, 6) + tn("v", 3, 4) + tn("p", 7, 6) + mx1(range(4), every, 0)
+        tensor = tensor + mx1(range(4, 8), every, 4) + mx1([8], every, 0) + tn("u", 1, 4) + mx1([9], every, 1)
+        held = {0: 2, 1: 3, 2: 6, 3: 7, 4: 4, 5: 5}
+        tensor = tensor + [step for tile, bank in held.items() for step in mx2(tile, [0], bank)] + mx1([10], every, 0) + mx2(0, [1]) + mx2(1, [1]) + mx1([11], every, 1)
+        tensor = tensor + mx2(2, [1]) + mx2(3, [1]) + mx2(4, [1]) + mx2(5, [1]) + mx2(6, [0, 1], 2) + mx1([12], every, 0) + mx2(7, [0, 1], 3) + mx1([14], every, 1) + mx2(8, [0, 1], 6)
+        tensor = tensor + mx1([13], every, 0) + mx1([15], [0, 1], 1) + mx2(4, [2]) + mx2(5, [2]) + mx1([15], [2, 3]) + mx2(6, [2]) + mx2(7, [2]) + mx2(8, [2]) + mx2(9, [0, 1, 2], 7)
+        tensor = tensor + mx2(10, [0, 1, 2], 0) + mx2(11, [0, 1, 2], 1)
+        for tile in order[:8]:
+            tensor = tensor + mx2(tile, [3])
+        for tile, bank in zip(order[8:], [4, 5, 2, 3, 6, 7, 0]):
+            tensor = tensor + mx2(tile, [2, 3] if tile in EXITS else every, bank)
+        tensor = tensor + mx2(15, every, 1, 0, HALF) + mx2(15, every, 4, HALF, C)
 
         queues = {"S": scalar, "V": vector, "T": tensor, "G": gpsimd}
         at = {engine: 0 for engine in queues}
@@ -432,4 +443,4 @@ def tile_two_sweep_policy_evaluation_d3_kernel(tc, P_bytes, P_scale, V, R, disco
                 while at[engine] < len(steps) and steps[at[engine]][0](engine, *steps[at[engine]][1:]):
                     at[engine] = at[engine] + 1
                     moved = True
-            assert moved, [steps[at[engine]][1:] for engine, steps in queues.items() if at[engine] < len(steps)]
+            assert moved, [steps[at[engine]] for engine, steps in queues.items() if at[engine] < len(steps)]

@@ -23,13 +23,17 @@ COPY = mybir.ActivationFunctionType.Copy
 FLOPS = 2 * 2 * S * S * C
 
 TURN_P = (4, 7)
-SCALAR_TILES = (11, 14)
-TILED = 2
+SCALAR_TILES = ()
+TILED = 4
 EXITS = {0: 1, 1: 1, 2: 1, 3: 1}
 WIDE_BUFS = 3
 MIXED_BUFS = 4
 MIXED_S_BUFS = 2
 V_MIXED_BUFS = 3
+PLANE_STEP = W + 32
+PAIR_STEP = 2 * W + 32
+GROUP_STEP = T * PLANE_STEP + 8
+AHEAD = 4
 
 
 def tile_two_sweep_policy_evaluation_d3_kernel(tc, P_bytes, P_scale, V, R, discount, out):
@@ -135,23 +139,29 @@ def tile_two_sweep_policy_evaluation_d3_kernel(tc, P_bytes, P_scale, V, R, disco
                 if not slot_free("wide", WIDE_BUFS):
                     return False
                 units = [2 * key, 2 * key + 1, 2 * key + G, 2 * key + G + 1] if key < 2 else range(T * key, T * key + T)
-                slots[key] = take([P, G * T * W], BF16, f"wide_{key}", "wide", WIDE_BUFS, [fact for n in units for fact in readers(n)])
+                slots[key] = take([P, G * GROUP_STEP], BF16, f"wide_{key}", "wide", WIDE_BUFS, [fact for n in units for fact in readers(n)])
             return True
+
+        def late_planes(q):
+            rows = slots[q][:].rearrange("p (g x) -> p g x", g=G)[:, :, : T * PLANE_STEP]
+            return rows.rearrange("p g (t i) -> p g t i", t=T)[:, :, :, :W]
+
+        def pair_planes(g):
+            first = (g % 2) * 2 * T * PLANE_STEP
+            return slots[g // 2][:, first : first + T * PAIR_STEP].rearrange("p (t i) -> p t i", t=T)[:, :, : 2 * W]
 
         def planes_of(q, g):
             if q >= 2:
-                return slots[q][:].rearrange("p (g t i) -> p g t i", g=G, t=T)[:, g]
+                return late_planes(q)[:, g]
             if g == 0:
-                return slots[0][:, q * T * W : (q + 1) * T * W].rearrange("p (t i) -> p t i", t=T)
-            half = slots[g // 2][:, (g % 2) * 2 * T * W : (g % 2 + 1) * 2 * T * W]
-            return half.rearrange("p (t q i) -> p q t i", t=T, q=2)[:, q]
+                return slots[0][:, q * T * PLANE_STEP : (q + 1) * T * PLANE_STEP].rearrange("p (t i) -> p t i", t=T)[:, :, :W]
+            return pair_planes(g)[:, :, q * W : (q + 1) * W]
 
         def widen(engine, q, g, t, count=1):
             if not wide_slot(q if q >= 2 else g // 2):
                 return False
             if count == 2:
-                first = ((g % 2) * T + t) * 2 * W
-                src, dst = pair_bytes[:, g - 1, t], slots[g // 2][:, first : first + 2 * W]
+                src, dst = pair_bytes[:, g - 1, t], pair_planes(g)[:, t]
             else:
                 src = first_bytes[q][:, t] if q < 2 else late_bytes[:, g, t, (q - 2) * W : (q - 1) * W]
                 dst = planes_of(q, g)[:, t]
@@ -185,7 +195,7 @@ def tile_two_sweep_policy_evaluation_d3_kernel(tc, P_bytes, P_scale, V, R, disco
                 src = planes_of(q, r).rearrange("p t (m e b) -> p m b t e", e=2, b=T)[:, :, k0:k1]
             else:
                 dst = mixed[n][:].rearrange("p (g m e t) -> p g m t e", g=G, e=2, t=T)[:, k0:k1]
-                src = slots[q][:].rearrange("p (g t m e b) -> p b g m t e", g=G, t=T, e=2, b=T)[:, r, k0:k1]
+                src = late_planes(q).rearrange("p g t (m e b) -> p b g m t e", e=2, b=T)[:, r, k0:k1]
             copier[engine](out=dst, in_=src)
             note(("mixed", n, k) for k in range(k0, k1))
             return True
@@ -407,33 +417,34 @@ def tile_two_sweep_policy_evaluation_d3_kernel(tc, P_bytes, P_scale, V, R, disco
         def mx2(tile, gs, bank=None, c0=0, c1=C):
             return [(multiply, 1, tile, g, bank if g == gs[0] else None, g == G - 1 or g == EXITS.get(tile), c0, c1) for g in gs]
 
-        scalar = w1(0, 0, [0]) + w1(1, 0, [0, 1]) + w2(1, [0, 1]) + w2(2, [0]) + ev("p", 4) + w2(2, [1]) + ev("v", 0) + w2(3, [0]) + ev("v", 1) + w1(2, 0, [0, 1]) + ev("v", 2) + w1(2, 0, [2, 3]) + ev("v", 3)
-        scalar = scalar + w1(2, 1, [0, 1]) + ev("p", 7) + w1(2, 1, [2, 3]) + w1(2, 2) + w1(2, 3, [0]) + w1(3, 0) + w1(3, 1) + il(11) + w1(3, 2, [0, 1]) + ev("u", 1) + w1(3, 2, [2, 3]) + w1(3, 3)
-        scalar = scalar + [(park, 0), (park, 1)] + il(14) + [(park, 2)] + ilv(2) + il(15, 2, 4) + [(park, 3)] + ilv(3, 3 * P, C)
+        scalar = w1(0, 0, [0]) + w1(1, 0, [0, 1]) + w2(1, [0, 1]) + w2(2, [0]) + ev("p", 4) + w2(2, [1]) + ev("v", 0) + w2(3, [0]) + ev("v", 1) + w2(3, [1]) + w1(2, 0, [0]) + ev("v", 2) + w1(2, 0, [1, 2]) + ev("v", 3)
+        scalar = scalar + w1(2, 0, [3]) + w1(2, 1, [0]) + ev("p", 7) + w1(2, 1, [1, 2, 3]) + w1(2, 2) + w1(2, 3) + w1(3, 0) + w1(3, 1) + w1(3, 2, [0]) + ev("u", 1) + w1(3, 2, [1, 2, 3]) + w1(3, 3, [0]) + [(park, 0), (park, 1), (park, 2)] + il(12, 2, 3) + [(park, 3)]
+        scalar = scalar + [step for n in range(13, 16) for step in il(n, 2, 3)] + [step for n in range(12, 16) for step in il(n, 3)] + ilv(2) + ilv(3, 3 * P, C)
 
-        vector = w1(0, 0, [1, 2, 3]) + w1(1, 0, [2, 3]) + il(0) + w2(1, [2, 3]) + qp(0) + w2(2, [2]) + il(1) + w2(2, [3]) + il(5) + qp(1) + qp(4) + w2(3, [1, 2, 3]) + qv(0, 0) + il(2) + qp(5) + qv(0, 1)
-        vector = vector + il(3) + qp(2) + qv(0, 2) + il(6) + qp(3) + qv(0, 3) + qp(6) + w1(2, 3, [1, 2, 3]) + [(widen_discount,)] + qp(7) + upd(range(2))
-        vector = vector + il(8) + upd([2]) + qp(8) + upd(range(3, 8)) + il(9) + ilv(0, HALF, C) + qp(9) + qv(1, 0) + il(10) + upd([8]) + qp(10) + qv(1, 1) + qp(11) + upd([9, 10])
-        vector = vector + il(12) + upd([11]) + qp(12) + il(13) + qp(14) + upd([12]) + qp(13) + il(15, 0, 2) + upd([14]) + qp(15, 0, 2) + qv(1, 2) + qp(15, 2, 4) + upd([13])
-        vector = vector + upd([15], 0, HALF) + upd([15], HALF, C) + ilv(3, 0, HALF) + ilv(3, HALF, 3 * P) + qv(1, 3, 0, HALF) + qv(1, 3, HALF, C)
-        order = [4, 5, 6, 7, 8, 9, 10, 11, 0, 12, 1, 13, 2, 14, 3]
+        vector = w1(0, 0, [1, 2, 3]) + w1(1, 0, [2, 3]) + il(0) + w2(1, [2, 3]) + qp(0) + w2(2, [2]) + il(1) + w2(2, [3]) + il(5) + qp(1) + qp(4) + w2(3, [3]) + qv(0, 0) + il(2) + qp(5) + w2(3, [2]) + qv(0, 1)
+        vector = vector + il(3) + qp(2) + qv(0, 2) + il(6) + qp(3) + qv(0, 3) + il(8) + qp(6) + qp(7) + [(widen_discount,)] + upd(range(2))
+        vector = vector + il(9) + qp(8) + upd([2]) + qp(9) + upd(range(3, 8)) + ilv(0, HALF, C) + il(10) + qv(1, 0) + qp(10) + il(11) + qv(1, 1) + w1(3, 3, [2]) + qp(11) + w1(3, 3, [1, 3]) + il(12, 0, 2)
+        vector = vector + upd([8, 9]) + qp(12, 0, 2) + il(13, 0, 2) + il(14, 0, 2) + qp(13, 0, 2) + qp(12, 2, 3) + upd([10]) + qp(14, 0, 2) + il(15, 0, 2) + qp(13, 2, 3) + upd([11])
+        vector = vector + qp(15, 0, 2) + qp(14, 2, 3) + qp(15, 2, 3) + qp(12, 3) + qp(13, 3) + qp(14, 3) + upd([12]) + qp(15, 3) + upd([13, 14])
+        vector = vector + upd([15], 0, HALF) + upd([15], HALF, C) + qv(1, 2) + ilv(3, 0, HALF) + ilv(3, HALF, 3 * P) + qv(1, 3, 0, HALF) + qv(1, 3, HALF, C)
+        order = [8, 9, 10, 11, 4, 5, 6, 7, 0, 12, 1, 13, 2, 14, 3]
         vector = vector + [(finish, tile) for tile in order] + [(finish, 15, 0, HALF), (finish, 15, HALF, C)]
 
         gpsimd = ilv(0, 0, HALF) + [(add_reward, tile) for tile in EXITS]
 
         every = list(range(G))
         tensor = tn("p", 4, 4) + tn("v", 0, 6) + tn("v", 1, 4) + tn("v", 2, 6) + tn("v", 3, 4) + tn("p", 7, 6) + mx1(range(4), every, 0)
-        tensor = tensor + mx1(range(4, 8), every, 4) + mx1([8], every, 0) + tn("u", 1, 4) + mx1([9], every, 1)
-        held = {0: 2, 1: 3, 2: 6, 3: 7, 4: 4, 5: 5}
-        tensor = tensor + [step for tile, bank in held.items() for step in mx2(tile, [0], bank)] + mx1([10], every, 0) + mx2(0, [1]) + mx2(1, [1]) + mx1([11], every, 1)
-        tensor = tensor + mx2(2, [1]) + mx2(3, [1]) + mx2(4, [1]) + mx2(5, [1]) + mx2(6, [0, 1], 2) + mx1([12], every, 0) + mx2(7, [0, 1], 3) + mx1([14], every, 1) + mx2(8, [0, 1], 6)
-        tensor = tensor + mx1([13], every, 0) + mx1([15], [0, 1], 1) + mx2(4, [2]) + mx2(5, [2]) + mx1([15], [2, 3]) + mx2(6, [2]) + mx2(7, [2]) + mx2(8, [2]) + mx2(9, [0, 1, 2], 7)
-        tensor = tensor + mx2(10, [0, 1, 2], 0) + mx2(11, [0, 1, 2], 1)
-        for tile in order[:8]:
-            tensor = tensor + mx2(tile, [3])
-        for tile, bank in zip(order[8:], [4, 5, 2, 3, 6, 7, 0]):
+        tensor = tensor + mx1(range(4, 8), every, 4) + mx1(range(8, 12), [0, 1], 0) + tn("u", 1, 4) + mx2(0, [0], 6) + mx2(1, [0], 7) + mx1(range(8, 12), [2])
+        tensor = tensor + mx2(2, [0], 4) + mx2(3, [0], 5) + mx2(0, [1]) + mx2(1, [1]) + mx2(2, [1]) + mx1([8, 9], [3]) + mx2(3, [1]) + mx1([10, 11], [3])
+        tensor = tensor + mx2(8, [0, 1], 6) + mx2(9, [0, 1], 7) + mx2(10, [0, 1], 4) + mx1([12, 13], [0], 0) + mx2(11, [0, 1], 5)
+        tensor = tensor + mx1([12, 13], [1, 2]) + mx1([14], [0, 1], 2) + mx1([12, 13], [3]) + mx1([14], [2, 3]) + mx1([15], every, 3) + mx2(4, [0, 1], 0) + mx2(5, [0, 1], 1) + mx2(6, [0, 1], 2) + mx2(8, [2]) + mx2(7, [0, 1], 3)
+        for tile in order[1:AHEAD]:
+            tensor = tensor + mx2(tile, [2])
+        for k, tile in enumerate(order[:8]):
+            tensor = tensor + mx2(tile, [3]) + [step for later in order[AHEAD + k : 8][:1] for step in mx2(later, [2])]
+        for tile, bank in zip(order[8:], [6, 7, 4, 5, 0, 1, 2]):
             tensor = tensor + mx2(tile, [2, 3] if tile in EXITS else every, bank)
-        tensor = tensor + mx2(15, every, 1, 0, HALF) + mx2(15, every, 4, HALF, C)
+        tensor = tensor + mx2(15, every, 3, 0, HALF) + mx2(15, every, 6, HALF, C)
 
         queues = {"S": scalar, "V": vector, "T": tensor, "G": gpsimd}
         at = {engine: 0 for engine in queues}

@@ -86,6 +86,10 @@ def tile_two_sweep_policy_evaluation_d3_kernel(tc, P_bytes, P_scale, V, R, disco
         nc.scalar.dma_start(out=scale_0[:], in_=scale_view[:, 0])
         load_first(0)
         nc.scalar.dma_start(out=scale_rest[:], in_=scale_view[:, 1:])
+        warm_in = keep.tile([P, 1], F32, name="warm_in")
+        warm_out = keep.tile([P, 1], F32, name="warm_out")
+        nc.vector.memset(warm_in[:], 0.0)
+        nc.scalar.activation(out=warm_out[:], in_=warm_in[:], func=COPY)
         load_first(1)
         load_pair(1)
         load_pair(2)
@@ -103,6 +107,7 @@ def tile_two_sweep_policy_evaluation_d3_kernel(tc, P_bytes, P_scale, V, R, disco
         for q in range(1, G):
             load_r(q)
 
+        first_planes = [stream.tile([P, T, PLANE_STEP], BF16, name=f"first_planes_{q}", tag="small", bufs=2, align_bytes=64) for q in range(2)]
         wide = {}
         slots = {}
         mixed = {}
@@ -138,7 +143,7 @@ def tile_two_sweep_policy_evaluation_d3_kernel(tc, P_bytes, P_scale, V, R, disco
             if key not in slots:
                 if not slot_free("wide", WIDE_BUFS):
                     return False
-                units = [2 * key, 2 * key + 1, 2 * key + G, 2 * key + G + 1] if key < 2 else range(T * key, T * key + T)
+                units = [n for n in (2 * key, 2 * key + 1, 2 * key + G, 2 * key + G + 1) if n % G] if key < 2 else range(T * key, T * key + T)
                 slots[key] = take([P, G * GROUP_STEP], BF16, f"wide_{key}", "wide", WIDE_BUFS, [fact for n in units for fact in readers(n)])
             return True
 
@@ -154,11 +159,11 @@ def tile_two_sweep_policy_evaluation_d3_kernel(tc, P_bytes, P_scale, V, R, disco
             if q >= 2:
                 return late_planes(q)[:, g]
             if g == 0:
-                return slots[0][:, q * T * PLANE_STEP : (q + 1) * T * PLANE_STEP].rearrange("p (t i) -> p t i", t=T)[:, :, :W]
+                return first_planes[q][:, :, :W]
             return pair_planes(g)[:, :, q * W : (q + 1) * W]
 
         def widen(engine, q, g, t, count=1):
-            if not wide_slot(q if q >= 2 else g // 2):
+            if not ((q < 2 and g == 0) or wide_slot(q if q >= 2 else g // 2)):
                 return False
             if count == 2:
                 src, dst = pair_bytes[:, g - 1, t], pair_planes(g)[:, t]
@@ -340,7 +345,9 @@ def tile_two_sweep_policy_evaluation_d3_kernel(tc, P_bytes, P_scale, V, R, disco
             if not {("sum", 1, tile, EXITS[tile], 0), ("disc32",)} <= done:
                 return False
             q, b = divmod(tile, T)
-            parked[tile] = stream.tile([P, C], F32, name=f"parked_{tile}", tag="parked", bufs=len(EXITS))[:]
+            if tile % 2 == 0:
+                parked["pair"] = stream.tile([P, 2, C], F32, name=f"parked_{tile}", tag="small", bufs=2, align_bytes=64)
+            parked[tile] = parked["pair"][:, tile % 2]
             if engine == "V":
                 update(parked[tile], acc[1, tile, 0][:], q, b, r_sb[:, q, b])
                 done.add(("rewarded", tile))

@@ -23,17 +23,14 @@ COPY = mybir.ActivationFunctionType.Copy
 FLOPS = 2 * 2 * S * S * C
 
 TURN_P = (4, 7)
-SCALAR_TILES = ()
-TILED = 4
+SCALAR_TILES = (14, 15)
 EXITS = {0: 1, 1: 1, 2: 1, 3: 1}
 WIDE_BUFS = 3
 MIXED_BUFS = 4
 MIXED_S_BUFS = 2
 V_MIXED_BUFS = 3
-PLANE_STEP = W + 32
-PAIR_STEP = 2 * W + 32
-GROUP_STEP = T * PLANE_STEP + 8
-AHEAD = 4
+PAD = 32
+AHEAD = 5
 
 
 def tile_two_sweep_policy_evaluation_d3_kernel(tc, P_bytes, P_scale, V, R, discount, out):
@@ -49,8 +46,8 @@ def tile_two_sweep_policy_evaluation_d3_kernel(tc, P_bytes, P_scale, V, R, disco
         scale_rest = keep.tile([P, G - 1, T], F32, name="scale_rest")
         disc = keep.tile([P, G, T], BF16, name="disc")
         disc32 = keep.tile([P, G, T], F32, name="disc32")
-        first_bytes = [keep.tile([P, T, W], U8, name=f"first_bytes_{q}", align_bytes=64) for q in range(2)]
-        pair_bytes = keep.tile([P, G - 1, T, 2 * W], U8, name="bytes_01", align_bytes=64)
+        head_bytes = [keep.tile([P, 2, 2 * W], U8, name=f"head_bytes_{h}", align_bytes=64) for h in range(4)]
+        pair_bytes = keep.tile([P, 2, T, 2 * W], U8, name="bytes_01", align_bytes=64)
         late_bytes = keep.tile([P, G, T, 2 * W], U8, name="bytes_23", align_bytes=64)
         v_raw = keep.tile([P, G, T, C], BF16, name="v_raw", align_bytes=64)
         r_sb = keep.tile([P, G, T, C], BF16, name="r_sb", align_bytes=64)
@@ -68,11 +65,11 @@ def tile_two_sweep_policy_evaluation_d3_kernel(tc, P_bytes, P_scale, V, R, disco
         r_view = R.rearrange("(g p t) c -> g p t c", p=P, t=T)
         out_view = out.rearrange("(g p t) c -> g p t c", p=P, t=T)
 
-        def load_first(q):
-            nc.sync.dma_start(out=first_bytes[q][:], in_=p_view[0][:, :, q * W : (q + 1) * W])
+        def load_first(h):
+            nc.sync.dma_start(out=head_bytes[h][:], in_=p_view[h // 2][:, h % 2 * 2 : h % 2 * 2 + 2, : 2 * W])
 
         def load_pair(g):
-            nc.sync.dma_start(out=pair_bytes[:, g - 1], in_=p_view[g][:, :, : 2 * W])
+            nc.sync.dma_start(out=pair_bytes[:, g - 2], in_=p_view[g][:, :, : 2 * W])
 
         def load_late(g):
             nc.sync.dma_start(out=late_bytes[:, g], in_=p_view[g][:, :, 2 * W :])
@@ -91,7 +88,8 @@ def tile_two_sweep_policy_evaluation_d3_kernel(tc, P_bytes, P_scale, V, R, disco
         nc.vector.memset(warm_in[:], 0.0)
         nc.scalar.activation(out=warm_out[:], in_=warm_in[:], func=COPY)
         load_first(1)
-        load_pair(1)
+        load_first(2)
+        load_first(3)
         load_pair(2)
         load_v(0)
         load_v(1)
@@ -107,7 +105,6 @@ def tile_two_sweep_policy_evaluation_d3_kernel(tc, P_bytes, P_scale, V, R, disco
         for q in range(1, G):
             load_r(q)
 
-        first_planes = [stream.tile([P, T, PLANE_STEP], BF16, name=f"first_planes_{q}", tag="small", bufs=2, align_bytes=64) for q in range(2)]
         wide = {}
         slots = {}
         mixed = {}
@@ -136,47 +133,41 @@ def tile_two_sweep_policy_evaluation_d3_kernel(tc, P_bytes, P_scale, V, R, disco
             waits[tag].append(set(freed_by))
             return stream.tile(shape, dtype, name=name, tag=tag, bufs=depth, align_bytes=64)
 
-        def readers(n):
-            return [("turned", "p", n, h) for h in range(2)] if n in TURN_P else [("mixed", n, k) for k in range(T)]
+        def readers(q, g):
+            return [("turned", "p", G * q + g, h) for h in range(2)] if G * q + g in TURN_P else [("mixed",) + place(q, g, b) for b in range(T)]
 
-        def wide_slot(key):
+        def wide_slot(q, g):
+            key = g // 2 if q < 2 else q
             if key not in slots:
                 if not slot_free("wide", WIDE_BUFS):
                     return False
-                units = [n for n in (2 * key, 2 * key + 1, 2 * key + G, 2 * key + G + 1) if n % G] if key < 2 else range(T * key, T * key + T)
-                slots[key] = take([P, G * GROUP_STEP], BF16, f"wide_{key}", "wide", WIDE_BUFS, [fact for n in units for fact in readers(n)])
+                chunks = [(k, r) for k in range(2) for r in (2 * key, 2 * key + 1)] if q < 2 else [(q, r) for r in range(G)]
+                shape = [P, 2, T, 2 * W + PAD] if q < 2 else [P, G, T, W + PAD]
+                slots[key] = take(shape, BF16, f"wide_{key}", "wide", WIDE_BUFS, [fact for chunk in chunks for fact in readers(*chunk)])
             return True
 
-        def late_planes(q):
-            rows = slots[q][:].rearrange("p (g x) -> p g x", g=G)[:, :, : T * PLANE_STEP]
-            return rows.rearrange("p g (t i) -> p g t i", t=T)[:, :, :, :W]
-
-        def pair_planes(g):
-            first = (g % 2) * 2 * T * PLANE_STEP
-            return slots[g // 2][:, first : first + T * PAIR_STEP].rearrange("p (t i) -> p t i", t=T)[:, :, : 2 * W]
-
         def planes_of(q, g):
-            if q >= 2:
-                return late_planes(q)[:, g]
-            if g == 0:
-                return first_planes[q][:, :, :W]
-            return pair_planes(g)[:, :, q * W : (q + 1) * W]
+            return slots[g // 2][:, g % 2, :, q * W : (q + 1) * W] if q < 2 else slots[q][:, g, :, :W]
 
-        def widen(engine, q, g, t, count=1):
-            if not ((q < 2 and g == 0) or wide_slot(q if q >= 2 else g // 2)):
+        def widen(engine, q, g, t):
+            if not wide_slot(q, g):
                 return False
-            if count == 2:
-                src, dst = pair_bytes[:, g - 1, t], pair_planes(g)[:, t]
+            if q < 2:
+                src, dst = (head_bytes[2 * g + t // 2][:, t % 2] if g < 2 else pair_bytes[:, g - 2, t]), slots[g // 2][:, g % 2, t, : 2 * W]
             else:
-                src = first_bytes[q][:, t] if q < 2 else late_bytes[:, g, t, (q - 2) * W : (q - 1) * W]
-                dst = planes_of(q, g)[:, t]
+                src, dst = late_bytes[:, g, t, (q - 2) * W : (q - 1) * W], planes_of(q, g)[:, t]
             scale = scale_0[:, t : t + 1] if g == 0 else scale_rest[:, g - 1, t : t + 1]
             if engine == "S":
                 nc.scalar.activation(out=dst, in_=src.bitcast(FP8), func=COPY, scale=scale)
             else:
                 nc.vector.tensor_scalar(out=dst, in0=src.bitcast(FP8), scalar1=scale, scalar2=None, op0=MULT)
-            note(("wide", q + k, g, t) for k in range(count))
+            note(("wide", k, g, t) for k in ((0, 1) if q < 2 else (q,)))
             return True
+
+        def place(q, g, b):
+            if q < G - 1:
+                return G * q + g, b
+            return (G * q + g // 2, 2 * (g % 2) + b) if b < 2 else (G * q + b, g)
 
         def mixed_tile(n):
             tag, depth = ("mixed_s", MIXED_S_BUFS) if n in TURN_P + SCALAR_TILES else ("mixed", MIXED_BUFS)
@@ -190,19 +181,26 @@ def tile_two_sweep_policy_evaluation_d3_kernel(tc, P_bytes, P_scale, V, R, disco
                 v_mixed[sweep, g] = take([P, C, T], BF16, f"v_mixed_{sweep}_{g}", tag, depth, [("v_codes", sweep, g, k) for k in range(T)])
             return (sweep, g) in v_mixed
 
-        def interleave(engine, n, k0, k1):
-            q, r = divmod(n, G)
-            groups = [r] if q < TILED else range(k0, k1)
-            if not ({("wide", q, g, t) for g in groups for t in range(T)} <= done and mixed_tile(n)):
+        def interleave(engine, q, g, b0, b1):
+            n, k = place(q, g, b0)
+            if not ({("wide", q, g, t) for t in range(T)} <= done and mixed_tile(n)):
                 return False
-            if q < TILED:
-                dst = mixed[n][:].rearrange("p (b m e t) -> p m b t e", b=T, e=2, t=T)[:, :, k0:k1]
-                src = planes_of(q, r).rearrange("p t (m e b) -> p m b t e", e=2, b=T)[:, :, k0:k1]
-            else:
-                dst = mixed[n][:].rearrange("p (g m e t) -> p g m t e", g=G, e=2, t=T)[:, k0:k1]
-                src = late_planes(q).rearrange("p g t (m e b) -> p b g m t e", e=2, b=T)[:, r, k0:k1]
-            copier[engine](out=dst, in_=src)
-            note(("mixed", n, k) for k in range(k0, k1))
+            copier[engine](
+                out=mixed[n][:].rearrange("p (k m e t) -> p m k t e", k=T, e=2, t=T)[:, :, k : k + b1 - b0],
+                in_=planes_of(q, g).rearrange("p t (m e b) -> p m b t e", e=2, b=T)[:, :, b0:b1],
+            )
+            note(("mixed", n, j) for j in range(k, k + b1 - b0))
+            return True
+
+        def interleave_tile(engine, b, half):
+            q, n = G - 1, G * (G - 1) + b
+            if not ({("wide", q, g, t) for g in (2 * half, 2 * half + 1) for t in range(T)} <= done and mixed_tile(n)):
+                return False
+            copier[engine](
+                out=mixed[n][:].rearrange("p (g m e t) -> p g m t e", g=G, e=2, t=T)[:, 2 * half : 2 * half + 2],
+                in_=slots[q][:, 2 * half : 2 * half + 2, :, :W].rearrange("p g t (m e b) -> p b g m t e", e=2, b=T)[:, b],
+            )
+            note(("mixed", n, g) for g in (2 * half, 2 * half + 1))
             return True
 
         def turn(engine, kind, n, h, bank):
@@ -296,7 +294,7 @@ def tile_two_sweep_policy_evaluation_d3_kernel(tc, P_bytes, P_scale, V, R, disco
 
         def multiply(engine, sweep, tile, g, bank=None, close=False, c0=0, c1=C):
             q, b = divmod(tile, T)
-            n, k = (G * q + g, b) if q < TILED else (tile, g)
+            n, k = place(q, g, b)
             needs = {("codes", n, k)} | {("v_codes", sweep, g, j) for j in quarters(c0, c1)}
             if not (needs <= done and (bank is None or slot_free(f"bank_{bank}", 1))):
                 return False
@@ -337,7 +335,7 @@ def tile_two_sweep_policy_evaluation_d3_kernel(tc, P_bytes, P_scale, V, R, disco
             return True
 
         def widen_discount(engine):
-            nc.vector.tensor_copy(out=disc32[:], in_=disc[:])
+            nc.scalar.copy(out=disc32[:], in_=disc[:])
             done.add(("disc32",))
             return True
 
@@ -345,9 +343,7 @@ def tile_two_sweep_policy_evaluation_d3_kernel(tc, P_bytes, P_scale, V, R, disco
             if not {("sum", 1, tile, EXITS[tile], 0), ("disc32",)} <= done:
                 return False
             q, b = divmod(tile, T)
-            if tile % 2 == 0:
-                parked["pair"] = stream.tile([P, 2, C], F32, name=f"parked_{tile}", tag="small", bufs=2, align_bytes=64)
-            parked[tile] = parked["pair"][:, tile % 2]
+            parked[tile] = stream.tile([P, C], F32, name=f"parked_{tile}", tag="parked", bufs=len(EXITS))[:]
             if engine == "V":
                 update(parked[tile], acc[1, tile, 0][:], q, b, r_sb[:, q, b])
                 done.add(("rewarded", tile))
@@ -391,17 +387,17 @@ def tile_two_sweep_policy_evaluation_d3_kernel(tc, P_bytes, P_scale, V, R, disco
             done.add(("result", tile, c0))
             return True
 
-        def w1(q, g, ts=range(T)):
+        def wd(q, g, ts=range(T)):
             return [(widen, q, g, t) for t in ts]
-
-        def w2(g, ts):
-            return [(widen, 0, g, t, 2) for t in ts]
 
         def ev(kind, n, hs=range(2)):
             return [(empty, kind, n, h) for h in hs]
 
-        def il(n, k0=0, k1=T):
-            return [(interleave, n, k0, k1)]
+        def il(n, b0=0, b1=T):
+            return [(interleave, n // G, n % G, b0, b1)]
+
+        def ilt(b, half):
+            return [(interleave_tile, b, half)]
 
         def qp(n, k0=0, k1=T):
             return [(quantise, n, k0, k1)]
@@ -424,15 +420,14 @@ def tile_two_sweep_policy_evaluation_d3_kernel(tc, P_bytes, P_scale, V, R, disco
         def mx2(tile, gs, bank=None, c0=0, c1=C):
             return [(multiply, 1, tile, g, bank if g == gs[0] else None, g == G - 1 or g == EXITS.get(tile), c0, c1) for g in gs]
 
-        scalar = w1(0, 0, [0]) + w1(1, 0, [0, 1]) + w2(1, [0, 1]) + w2(2, [0]) + ev("p", 4) + w2(2, [1]) + ev("v", 0) + w2(3, [0]) + ev("v", 1) + w2(3, [1]) + w1(2, 0, [0]) + ev("v", 2) + w1(2, 0, [1, 2]) + ev("v", 3)
-        scalar = scalar + w1(2, 0, [3]) + w1(2, 1, [0]) + ev("p", 7) + w1(2, 1, [1, 2, 3]) + w1(2, 2) + w1(2, 3) + w1(3, 0) + w1(3, 1) + w1(3, 2, [0]) + ev("u", 1) + w1(3, 2, [1, 2, 3]) + w1(3, 3, [0]) + [(park, 0), (park, 1), (park, 2)] + il(12, 2, 3) + [(park, 3)]
-        scalar = scalar + [step for n in range(13, 16) for step in il(n, 2, 3)] + [step for n in range(12, 16) for step in il(n, 3)] + ilv(2) + ilv(3, 3 * P, C)
+        scalar = wd(0, 0, [1]) + wd(0, 1, [1, 2]) + wd(0, 2, [0]) + ev("p", 4, [0]) + wd(0, 2, [1]) + ev("p", 4, [1]) + ev("v", 0, [0]) + wd(0, 3, [0]) + ev("v", 0, [1]) + ev("v", 1) + wd(0, 3, [1]) + wd(2, 0, [0]) + ev("v", 2) + wd(2, 0, [1, 2]) + ev("v", 3)
+        scalar = scalar + wd(2, 0, [3]) + wd(2, 1, [0]) + ev("p", 7) + wd(2, 1, [1, 2, 3]) + wd(2, 2) + wd(2, 3) + wd(3, 0) + wd(3, 1) + wd(3, 2, [0]) + ev("u", 1, [0]) + [(widen_discount,)] + wd(3, 2, [1]) + ev("u", 1, [1]) + wd(3, 2, [2, 3]) + wd(3, 3, [0])
+        scalar = scalar + [(park, 0), (park, 1), (park, 2)] + ilt(2, 0) + [(park, 3)] + ilt(2, 1) + ilt(3, 0) + ilt(3, 1) + ilv(2) + ilv(3, 3 * P, C)
 
-        vector = w1(0, 0, [1, 2, 3]) + w1(1, 0, [2, 3]) + il(0) + w2(1, [2, 3]) + qp(0) + w2(2, [2]) + il(1) + w2(2, [3]) + il(5) + qp(1) + qp(4) + w2(3, [3]) + qv(0, 0) + il(2) + qp(5) + w2(3, [2]) + qv(0, 1)
-        vector = vector + il(3) + qp(2) + qv(0, 2) + il(6) + qp(3) + qv(0, 3) + il(8) + qp(6) + qp(7) + [(widen_discount,)] + upd(range(2))
-        vector = vector + il(9) + qp(8) + upd([2]) + qp(9) + upd(range(3, 8)) + ilv(0, HALF, C) + il(10) + qv(1, 0) + qp(10) + il(11) + qv(1, 1) + w1(3, 3, [2]) + qp(11) + w1(3, 3, [1, 3]) + il(12, 0, 2)
-        vector = vector + upd([8, 9]) + qp(12, 0, 2) + il(13, 0, 2) + il(14, 0, 2) + qp(13, 0, 2) + qp(12, 2, 3) + upd([10]) + qp(14, 0, 2) + il(15, 0, 2) + qp(13, 2, 3) + upd([11])
-        vector = vector + qp(15, 0, 2) + qp(14, 2, 3) + qp(15, 2, 3) + qp(12, 3) + qp(13, 3) + qp(14, 3) + upd([12]) + qp(15, 3) + upd([13, 14])
+        vector = wd(0, 0, [0, 2, 3]) + wd(0, 1, [0]) + il(0) + wd(0, 1, [3]) + qp(0) + wd(0, 2, [2]) + il(1) + wd(0, 2, [3]) + il(5) + qp(1) + qp(4) + wd(0, 3, [3]) + qv(0, 0) + il(2) + qp(5) + wd(0, 3, [2]) + qv(0, 1)
+        vector = vector + il(3) + qp(2) + qv(0, 2) + il(6) + qp(3) + qv(0, 3) + il(8) + qp(6) + qp(7) + upd(range(2))
+        vector = vector + il(9) + qp(8) + upd([2]) + qp(9) + upd(range(3, 8)) + ilv(0, HALF, C) + il(10) + qv(1, 0) + qp(10) + il(11) + qv(1, 1) + wd(3, 3, [2]) + qp(11) + wd(3, 3, [1, 3]) + il(12, 0, 2)
+        vector = vector + upd([8, 9]) + il(13, 0, 2) + qp(12, 0, 2) + il(14, 0, 2) + qp(12, 2, 4) + il(15, 0, 2) + qp(13, 0, 2) + upd([10]) + qp(13, 2, 4) + qp(14) + upd([11]) + qp(15, 0, 2) + upd([12]) + qp(15, 2, 4) + upd([13, 14])
         vector = vector + upd([15], 0, HALF) + upd([15], HALF, C) + qv(1, 2) + ilv(3, 0, HALF) + ilv(3, HALF, 3 * P) + qv(1, 3, 0, HALF) + qv(1, 3, HALF, C)
         order = [8, 9, 10, 11, 4, 5, 6, 7, 0, 12, 1, 13, 2, 14, 3]
         vector = vector + [(finish, tile) for tile in order] + [(finish, 15, 0, HALF), (finish, 15, HALF, C)]
@@ -444,8 +439,8 @@ def tile_two_sweep_policy_evaluation_d3_kernel(tc, P_bytes, P_scale, V, R, disco
         tensor = tensor + mx1(range(4, 8), every, 4) + mx1(range(8, 12), [0, 1], 0) + tn("u", 1, 4) + mx2(0, [0], 6) + mx2(1, [0], 7) + mx1(range(8, 12), [2])
         tensor = tensor + mx2(2, [0], 4) + mx2(3, [0], 5) + mx2(0, [1]) + mx2(1, [1]) + mx2(2, [1]) + mx1([8, 9], [3]) + mx2(3, [1]) + mx1([10, 11], [3])
         tensor = tensor + mx2(8, [0, 1], 6) + mx2(9, [0, 1], 7) + mx2(10, [0, 1], 4) + mx1([12, 13], [0], 0) + mx2(11, [0, 1], 5)
-        tensor = tensor + mx1([12, 13], [1, 2]) + mx1([14], [0, 1], 2) + mx1([12, 13], [3]) + mx1([14], [2, 3]) + mx1([15], every, 3) + mx2(4, [0, 1], 0) + mx2(5, [0, 1], 1) + mx2(6, [0, 1], 2) + mx2(8, [2]) + mx2(7, [0, 1], 3)
-        for tile in order[1:AHEAD]:
+        tensor = tensor + mx1([12, 13], [1, 2, 3]) + mx1([14], every, 2) + mx1([15], every, 3) + mx2(4, [0, 1], 0) + mx2(5, [0, 1], 1) + mx2(6, [0, 1], 2) + mx2(7, [0, 1], 3)
+        for tile in order[:AHEAD]:
             tensor = tensor + mx2(tile, [2])
         for k, tile in enumerate(order[:8]):
             tensor = tensor + mx2(tile, [3]) + [step for later in order[AHEAD + k : 8][:1] for step in mx2(later, [2])]

@@ -26,11 +26,12 @@ TURN_P = (4, 7)
 SCALAR_TILES = (14, 15)
 EXITS = {0: 1, 1: 1, 2: 1, 3: 1}
 WIDE_BUFS = 3
-MIXED_BUFS = 4
+MIXED_BUFS = 3
+HANDED_ON = (6, 9)
 MIXED_S_BUFS = 2
 V_MIXED_BUFS = 3
 PAD = 32
-AHEAD = 5
+JOINED = ()
 
 
 def tile_two_sweep_policy_evaluation_d3_kernel(tc, P_bytes, P_scale, V, R, discount, out):
@@ -90,13 +91,13 @@ def tile_two_sweep_policy_evaluation_d3_kernel(tc, P_bytes, P_scale, V, R, disco
         load_first(1)
         load_first(2)
         load_first(3)
-        load_pair(2)
         load_v(0)
+        load_pair(2)
         load_v(1)
-        load_pair(3)
         load_v(2)
-        load_late(0)
+        load_pair(3)
         load_v(3)
+        load_late(0)
         load_late(1)
         nc.sync.dma_start(out=disc[:], in_=discount.rearrange("(g p t) o -> p g (t o)", p=P, t=T))
         load_late(2)
@@ -149,11 +150,12 @@ def tile_two_sweep_policy_evaluation_d3_kernel(tc, P_bytes, P_scale, V, R, disco
         def planes_of(q, g):
             return slots[g // 2][:, g % 2, :, q * W : (q + 1) * W] if q < 2 else slots[q][:, g, :, :W]
 
-        def widen(engine, q, g, t):
+        def widen(engine, q, g, t, paired):
             if not wide_slot(q, g):
                 return False
             if q < 2:
-                src, dst = (head_bytes[2 * g + t // 2][:, t % 2] if g < 2 else pair_bytes[:, g - 2, t]), slots[g // 2][:, g % 2, t, : 2 * W]
+                cols = slice(0, 2 * W) if paired else slice(q * W, (q + 1) * W)
+                src, dst = (head_bytes[2 * g + t // 2][:, t % 2, cols] if g < 2 else pair_bytes[:, g - 2, t, cols]), slots[g // 2][:, g % 2, t, cols]
             else:
                 src, dst = late_bytes[:, g, t, (q - 2) * W : (q - 1) * W], planes_of(q, g)[:, t]
             scale = scale_0[:, t : t + 1] if g == 0 else scale_rest[:, g - 1, t : t + 1]
@@ -161,7 +163,7 @@ def tile_two_sweep_policy_evaluation_d3_kernel(tc, P_bytes, P_scale, V, R, disco
                 nc.scalar.activation(out=dst, in_=src.bitcast(FP8), func=COPY, scale=scale)
             else:
                 nc.vector.tensor_scalar(out=dst, in0=src.bitcast(FP8), scalar1=scale, scalar2=None, op0=MULT)
-            note(("wide", k, g, t) for k in ((0, 1) if q < 2 else (q,)))
+            note(("wide", k, g, t) for k in ((0, 1) if paired else (q,)))
             return True
 
         def place(q, g, b):
@@ -170,13 +172,13 @@ def tile_two_sweep_policy_evaluation_d3_kernel(tc, P_bytes, P_scale, V, R, disco
             return (G * q + g // 2, 2 * (g % 2) + b) if b < 2 else (G * q + b, g)
 
         def mixed_tile(n):
-            tag, depth = ("mixed_s", MIXED_S_BUFS) if n in TURN_P + SCALAR_TILES else ("mixed", MIXED_BUFS)
+            tag, depth = ("mixed_s", MIXED_S_BUFS) if n in TURN_P + SCALAR_TILES else ("mixed_g", 1) if n in HANDED_ON else ("mixed", MIXED_BUFS)
             if n not in mixed and slot_free(tag, depth):
                 mixed[n] = take([P, W * T], BF16, f"mixed_{n}", tag, depth, [("codes", n, k) for k in range(T)])
             return n in mixed
 
         def v_mixed_tile(sweep, g):
-            tag, depth = ("last", 1) if (sweep, g) == (1, G - 1) else ("v_mixed", V_MIXED_BUFS)
+            tag, depth = ("last", 1) if (sweep, g) == (1, G - 1) else ("mixed_g", 1) if (sweep, g) == (1, 0) else ("v_mixed", V_MIXED_BUFS)
             if (sweep, g) not in v_mixed and slot_free(tag, depth):
                 v_mixed[sweep, g] = take([P, C, T], BF16, f"v_mixed_{sweep}_{g}", tag, depth, [("v_codes", sweep, g, k) for k in range(T)])
             return (sweep, g) in v_mixed
@@ -185,11 +187,44 @@ def tile_two_sweep_policy_evaluation_d3_kernel(tc, P_bytes, P_scale, V, R, disco
             n, k = place(q, g, b0)
             if not ({("wide", q, g, t) for t in range(T)} <= done and mixed_tile(n)):
                 return False
-            copier[engine](
-                out=mixed[n][:].rearrange("p (k m e t) -> p m k t e", k=T, e=2, t=T)[:, :, k : k + b1 - b0],
-                in_=planes_of(q, g).rearrange("p t (m e b) -> p m b t e", e=2, b=T)[:, :, b0:b1],
-            )
+            if engine == "G":
+                nc.gpsimd.tensor_scalar(
+                    out=mixed[n][:].rearrange("p (k m t) -> p m k t", k=T, t=T)[:, :, k : k + b1 - b0],
+                    in0=planes_of(q, g).rearrange("p t (m b) -> p m b t", b=T)[:, :, b0:b1],
+                    scalar1=1.0,
+                    scalar2=0.0,
+                    op0=MULT,
+                    op1=ADD,
+                )
+            else:
+                copier[engine](
+                    out=mixed[n][:].rearrange("p (k m e t) -> p m k t e", k=T, e=2, t=T)[:, :, k : k + b1 - b0],
+                    in_=planes_of(q, g).rearrange("p t (m e b) -> p m b t e", e=2, b=T)[:, :, b0:b1],
+                )
             note(("mixed", n, j) for j in range(k, k + b1 - b0))
+            return True
+
+        def interleave_half(engine, n, half):
+            q, g = divmod(n, G)
+            if not ({("wide", q, g, t) for t in range(T)} <= done and mixed_tile(n)):
+                return False
+            if engine == "G":
+                nc.gpsimd.tensor_scalar(
+                    out=mixed[n][:].rearrange("p (b h m t) -> p h m b t", b=T, h=2, t=T)[:, half],
+                    in0=planes_of(q, g).rearrange("p t (h m b) -> p h m b t", h=2, b=T)[:, half],
+                    scalar1=1.0,
+                    scalar2=0.0,
+                    op0=MULT,
+                    op1=ADD,
+                )
+            else:
+                copier[engine](
+                    out=mixed[n][:].rearrange("p (b h m e t) -> p h m b t e", b=T, h=2, e=2, t=T)[:, half],
+                    in_=planes_of(q, g).rearrange("p t (h m e b) -> p h m b t e", h=2, e=2, b=T)[:, half],
+                )
+            done.add(("half", n, half))
+            if ("half", n, 1 - half) in done:
+                note(("mixed", n, j) for j in range(T))
             return True
 
         def interleave_tile(engine, b, half):
@@ -359,8 +394,8 @@ def tile_two_sweep_policy_evaluation_d3_kernel(tc, P_bytes, P_scale, V, R, disco
             if "late" not in turned:
                 if not ((1, G - 1) in v_mixed and slot_free("last", 1)):
                     return False
-                turned["late"] = take([P, len(EXITS), C], F32, "late", "last", 1, [])
-            dst = turned["late"][:, list(EXITS).index(tile)]
+                turned["late"] = take([P, C], F32, "late", "last", 1, [])
+            dst = turned["late"][:] if tile == 0 else parked[tile]
             nc.gpsimd.tensor_tensor(out=dst, in0=parked[tile], in1=r_sb[:, q, b], op=ADD)
             parked[tile] = dst
             done.add(("rewarded", tile))
@@ -383,12 +418,21 @@ def tile_two_sweep_policy_evaluation_d3_kernel(tc, P_bytes, P_scale, V, R, disco
             dst = results[half][:, place, c0:c1]
             addend = parked[tile][:, c0:c1] if tile in EXITS else r_sb[:, q, b, c0:c1]
             update(dst, acc[1, tile, c0][:], q, b, addend)
-            nc.sync.dma_start(out=out_view[q][:, b, c0:c1], in_=dst)
+            if tile in JOINED:
+                nc.sync.dma_start(out=out_view[q][:, b - 1 : b + 1], in_=results[half][:, place - 1 : place + 1])
+            elif tile + 1 not in JOINED:
+                nc.sync.dma_start(out=out_view[q][:, b, c0:c1], in_=dst)
             done.add(("result", tile, c0))
             return True
 
         def wd(q, g, ts=range(T)):
-            return [(widen, q, g, t) for t in ts]
+            return [(widen, q, g, t, q < 2) for t in ts]
+
+        def wd1(q, g, ts):
+            return [(widen, q, g, t, False) for t in ts]
+
+        def ilh(n, half):
+            return [(interleave_half, n, half)]
 
         def ev(kind, n, hs=range(2)):
             return [(empty, kind, n, h) for h in hs]
@@ -420,33 +464,34 @@ def tile_two_sweep_policy_evaluation_d3_kernel(tc, P_bytes, P_scale, V, R, disco
         def mx2(tile, gs, bank=None, c0=0, c1=C):
             return [(multiply, 1, tile, g, bank if g == gs[0] else None, g == G - 1 or g == EXITS.get(tile), c0, c1) for g in gs]
 
-        scalar = wd(0, 0, [1]) + wd(0, 1, [1, 2]) + wd(0, 2, [0]) + ev("p", 4, [0]) + wd(0, 2, [1]) + ev("p", 4, [1]) + ev("v", 0, [0]) + wd(0, 3, [0]) + ev("v", 0, [1]) + ev("v", 1) + wd(0, 3, [1]) + wd(2, 0, [0]) + ev("v", 2) + wd(2, 0, [1, 2]) + ev("v", 3)
-        scalar = scalar + wd(2, 0, [3]) + wd(2, 1, [0]) + ev("p", 7) + wd(2, 1, [1, 2, 3]) + wd(2, 2) + wd(2, 3) + wd(3, 0) + wd(3, 1) + wd(3, 2, [0]) + ev("u", 1, [0]) + [(widen_discount,)] + wd(3, 2, [1]) + ev("u", 1, [1]) + wd(3, 2, [2, 3]) + wd(3, 3, [0])
-        scalar = scalar + [(park, 0), (park, 1), (park, 2)] + ilt(2, 0) + [(park, 3)] + ilt(2, 1) + ilt(3, 0) + ilt(3, 1) + ilv(2) + ilv(3, 3 * P, C)
+        scalar = wd1(1, 0, [1]) + wd1(0, 0, [1]) + wd(0, 1, [1, 2]) + ev("p", 4) + wd(0, 2, [0]) + ev("v", 0, [0]) + wd(0, 2, [1]) + ev("v", 0, [1]) + wd(0, 3, [0]) + ev("v", 1) + wd(0, 3, [1]) + ev("v", 2) + wd(2, 0, [0, 1]) + ev("v", 3) + wd(2, 0, [2, 3]) + ev("p", 7)
+        scalar = scalar + wd(2, 1) + wd(2, 2) + wd(2, 3) + wd(3, 0) + wd(3, 1, [0, 1, 2]) + ev("u", 1, [0]) + [(widen_discount,)] + wd(3, 1, [3]) + ev("u", 1, [1]) + wd(3, 2) + [(park, 0), (park, 1)] + wd(3, 3, [0])
+        scalar = scalar + [(park, 2), (park, 3)] + ilt(2, 0) + ilt(2, 1) + ilt(3, 0) + ilt(3, 1) + ilv(2) + ilv(3, 3 * P, C)
 
-        vector = wd(0, 0, [0, 2, 3]) + wd(0, 1, [0]) + il(0) + wd(0, 1, [3]) + qp(0) + wd(0, 2, [2]) + il(1) + wd(0, 2, [3]) + il(5) + qp(1) + qp(4) + wd(0, 3, [3]) + qv(0, 0) + il(2) + qp(5) + wd(0, 3, [2]) + qv(0, 1)
-        vector = vector + il(3) + qp(2) + qv(0, 2) + il(6) + qp(3) + qv(0, 3) + il(8) + qp(6) + qp(7) + upd(range(2))
-        vector = vector + il(9) + qp(8) + upd([2]) + qp(9) + upd(range(3, 8)) + ilv(0, HALF, C) + il(10) + qv(1, 0) + qp(10) + il(11) + qv(1, 1) + wd(3, 3, [2]) + qp(11) + wd(3, 3, [1, 3]) + il(12, 0, 2)
-        vector = vector + upd([8, 9]) + il(13, 0, 2) + qp(12, 0, 2) + il(14, 0, 2) + qp(12, 2, 4) + il(15, 0, 2) + qp(13, 0, 2) + upd([10]) + qp(13, 2, 4) + qp(14) + upd([11]) + qp(15, 0, 2) + upd([12]) + qp(15, 2, 4) + upd([13, 14])
+        vector = wd1(1, 0, [0]) + wd1(0, 0, [0]) + wd1(1, 0, [2, 3]) + wd1(0, 0, [2, 3]) + wd(0, 1, [0]) + il(0) + wd(0, 1, [3]) + qp(0) + il(1) + wd(0, 2, [2, 3]) + qp(1) + il(5) + qp(4) + wd(0, 3, [3]) + qv(0, 0) + il(2) + wd(0, 3, [2]) + qv(0, 1) + qp(2)
+        vector = vector + il(3) + qp(5) + qv(0, 2) + qp(3) + il(6) + qv(0, 3) + il(8) + qp(7) + qp(6) + upd(range(4)) + ilh(9, 1) + qp(8) + qp(9) + upd(range(4, 8))
+        vector = vector + ilv(0, HALF, C) + il(10) + qv(1, 0) + qp(10) + il(11) + qv(1, 1) + qp(11) + wd(3, 3, [1, 2, 3]) + il(12, 0, 2)
+        vector = vector + upd([8, 9]) + il(13, 0, 2) + qp(12, 0, 2) + il(14, 0, 2) + qp(12, 2, 4) + il(15, 0, 2) + qp(13, 0, 2) + qp(14, 0, 2) + qp(13, 2, 4) + upd([10]) + qp(14, 2, 4) + upd([11]) + qp(15, 0, 2) + upd([12]) + qp(15, 2, 4) + upd([13, 14])
         vector = vector + upd([15], 0, HALF) + upd([15], HALF, C) + qv(1, 2) + ilv(3, 0, HALF) + ilv(3, HALF, 3 * P) + qv(1, 3, 0, HALF) + qv(1, 3, HALF, C)
         order = [8, 9, 10, 11, 4, 5, 6, 7, 0, 12, 1, 13, 2, 14, 3]
         vector = vector + [(finish, tile) for tile in order] + [(finish, 15, 0, HALF), (finish, 15, HALF, C)]
 
-        gpsimd = ilv(0, 0, HALF) + [(add_reward, tile) for tile in EXITS]
+        gpsimd = ilh(9, 0) + ilv(0, 0, HALF) + [(add_reward, tile) for tile in EXITS]
 
         every = list(range(G))
         tensor = tn("p", 4, 4) + tn("v", 0, 6) + tn("v", 1, 4) + tn("v", 2, 6) + tn("v", 3, 4) + tn("p", 7, 6) + mx1(range(4), every, 0)
-        tensor = tensor + mx1(range(4, 8), every, 4) + mx1(range(8, 12), [0, 1], 0) + tn("u", 1, 4) + mx2(0, [0], 6) + mx2(1, [0], 7) + mx1(range(8, 12), [2])
-        tensor = tensor + mx2(2, [0], 4) + mx2(3, [0], 5) + mx2(0, [1]) + mx2(1, [1]) + mx2(2, [1]) + mx1([8, 9], [3]) + mx2(3, [1]) + mx1([10, 11], [3])
+        tensor = tensor + mx1(range(4, 8), every, 4) + mx1(range(8, 12), [0, 1], 0) + tn("u", 1, 4) + mx2(0, [0], 6) + mx2(1, [0], 7) + mx1(range(8, 12), [2]) + mx2(2, [0], 4) + mx2(3, [0], 5)
+        tensor = tensor + mx2(0, [1]) + mx2(1, [1]) + mx1([8, 9], [3]) + mx2(2, [1]) + mx2(3, [1]) + mx1([10, 11], [3])
         tensor = tensor + mx2(8, [0, 1], 6) + mx2(9, [0, 1], 7) + mx2(10, [0, 1], 4) + mx1([12, 13], [0], 0) + mx2(11, [0, 1], 5)
-        tensor = tensor + mx1([12, 13], [1, 2, 3]) + mx1([14], every, 2) + mx1([15], every, 3) + mx2(4, [0, 1], 0) + mx2(5, [0, 1], 1) + mx2(6, [0, 1], 2) + mx2(7, [0, 1], 3)
-        for tile in order[:AHEAD]:
+        tensor = tensor + mx1([12, 13], [1, 2, 3]) + mx1([14], every, 2) + mx1([15], [0, 1], 3) + mx2(4, [0], 0) + mx1([15], [2, 3]) + mx2(4, [1]) + mx2(5, [0, 1], 1) + mx2(6, [0, 1], 2) + mx2(7, [0, 1], 3)
+        for tile in order[:5]:
             tensor = tensor + mx2(tile, [2])
         for k, tile in enumerate(order[:8]):
-            tensor = tensor + mx2(tile, [3]) + [step for later in order[AHEAD + k : 8][:1] for step in mx2(later, [2])]
+            tensor = tensor + mx2(tile, [3]) + [step for later in order[5 + k : 8][:1] for step in mx2(later, [2])]
         for tile, bank in zip(order[8:], [6, 7, 4, 5, 0, 1, 2]):
             tensor = tensor + mx2(tile, [2, 3] if tile in EXITS else every, bank)
         tensor = tensor + mx2(15, every, 3, 0, HALF) + mx2(15, every, 6, HALF, C)
+
 
         queues = {"S": scalar, "V": vector, "T": tensor, "G": gpsimd}
         at = {engine: 0 for engine in queues}

@@ -22,12 +22,12 @@ COPY = mybir.ActivationFunctionType.Copy
 
 FLOPS = 2 * 2 * S * S * C
 
-TURN_P = (4, 7)
-SCALAR_TILES = (14, 15)
-EXITS = {0: 1, 1: 1, 2: 1, 3: 1}
+TURN_P = (4, 5)
+SCALAR_UNIT = 13
+EXITS = {0: 1, 1: 1, 2: 1, 3: 1, 12: 1}
 WIDE_BUFS = 3
 MIXED_BUFS = 3
-HANDED_ON = (6, 9)
+HANDED_ON = (8, 9, 14)
 MIXED_S_BUFS = 2
 V_MIXED_BUFS = 3
 PAD = 32
@@ -47,7 +47,8 @@ def tile_two_sweep_policy_evaluation_d3_kernel(tc, P_bytes, P_scale, V, R, disco
         scale_rest = keep.tile([P, G - 1, T], F32, name="scale_rest")
         disc = keep.tile([P, G, T], BF16, name="disc")
         disc32 = keep.tile([P, G, T], F32, name="disc32")
-        head_bytes = [keep.tile([P, 2, 2 * W], U8, name=f"head_bytes_{h}", align_bytes=64) for h in range(4)]
+        first_bytes = [keep.tile([P, 2 * W], U8, name=f"first_bytes_{t}", align_bytes=64) for t in range(T)]
+        head_bytes = [keep.tile([P, 2, 2 * W], U8, name=f"head_bytes_{h}", align_bytes=64) for h in range(2)]
         pair_bytes = keep.tile([P, 2, T, 2 * W], U8, name="bytes_01", align_bytes=64)
         late_bytes = keep.tile([P, G, T, 2 * W], U8, name="bytes_23", align_bytes=64)
         v_raw = keep.tile([P, G, T, C], BF16, name="v_raw", align_bytes=64)
@@ -66,8 +67,11 @@ def tile_two_sweep_policy_evaluation_d3_kernel(tc, P_bytes, P_scale, V, R, disco
         r_view = R.rearrange("(g p t) c -> g p t c", p=P, t=T)
         out_view = out.rearrange("(g p t) c -> g p t c", p=P, t=T)
 
-        def load_first(h):
-            nc.sync.dma_start(out=head_bytes[h][:], in_=p_view[h // 2][:, h % 2 * 2 : h % 2 * 2 + 2, : 2 * W])
+        def load_first(t):
+            nc.sync.dma_start(out=first_bytes[t][:], in_=p_view[0][:, t, : 2 * W])
+
+        def load_head(h):
+            nc.sync.dma_start(out=head_bytes[h][:], in_=p_view[1][:, 2 * h : 2 * h + 2, : 2 * W])
 
         def load_pair(g):
             nc.sync.dma_start(out=pair_bytes[:, g - 2], in_=p_view[g][:, :, : 2 * W])
@@ -83,7 +87,6 @@ def tile_two_sweep_policy_evaluation_d3_kernel(tc, P_bytes, P_scale, V, R, disco
 
         nc.scalar.dma_start(out=scale_0[:], in_=scale_view[:, 0])
         load_first(0)
-        nc.scalar.dma_start(out=scale_rest[:], in_=scale_view[:, 1:])
         warm_in = keep.tile([P, 1], F32, name="warm_in")
         warm_out = keep.tile([P, 1], F32, name="warm_out")
         nc.vector.memset(warm_in[:], 0.0)
@@ -91,11 +94,14 @@ def tile_two_sweep_policy_evaluation_d3_kernel(tc, P_bytes, P_scale, V, R, disco
         load_first(1)
         load_first(2)
         load_first(3)
-        load_v(0)
+        nc.sync.dma_start(out=scale_rest[:], in_=scale_view[:, 1:])
+        load_head(0)
+        load_head(1)
         load_pair(2)
+        load_v(0)
         load_v(1)
-        load_v(2)
         load_pair(3)
+        load_v(2)
         load_v(3)
         load_late(0)
         load_late(1)
@@ -103,8 +109,9 @@ def tile_two_sweep_policy_evaluation_d3_kernel(tc, P_bytes, P_scale, V, R, disco
         load_late(2)
         load_r(0)
         load_late(3)
-        for q in range(1, G):
-            load_r(q)
+        load_r(1)
+        load_r(2)
+        load_r(3)
 
         wide = {}
         slots = {}
@@ -155,7 +162,7 @@ def tile_two_sweep_policy_evaluation_d3_kernel(tc, P_bytes, P_scale, V, R, disco
                 return False
             if q < 2:
                 cols = slice(0, 2 * W) if paired else slice(q * W, (q + 1) * W)
-                src, dst = (head_bytes[2 * g + t // 2][:, t % 2, cols] if g < 2 else pair_bytes[:, g - 2, t, cols]), slots[g // 2][:, g % 2, t, cols]
+                src, dst = (first_bytes[t][:, cols] if g == 0 else head_bytes[t // 2][:, t % 2, cols] if g == 1 else pair_bytes[:, g - 2, t, cols]), slots[g // 2][:, g % 2, t, cols]
             else:
                 src, dst = late_bytes[:, g, t, (q - 2) * W : (q - 1) * W], planes_of(q, g)[:, t]
             scale = scale_0[:, t : t + 1] if g == 0 else scale_rest[:, g - 1, t : t + 1]
@@ -167,14 +174,14 @@ def tile_two_sweep_policy_evaluation_d3_kernel(tc, P_bytes, P_scale, V, R, disco
             return True
 
         def place(q, g, b):
-            if q < G - 1:
+            if q < G - 1 or g >= 2:
                 return G * q + g, b
-            return (G * q + g // 2, 2 * (g % 2) + b) if b < 2 else (G * q + b, g)
+            return (G * q, 2 * g + b) if b < 2 else (G * q + 1, 2 * (b - 2) + g)
 
         def mixed_tile(n):
-            tag, depth = ("mixed_s", MIXED_S_BUFS) if n in TURN_P + SCALAR_TILES else ("mixed_g", 1) if n in HANDED_ON else ("mixed", MIXED_BUFS)
+            tag, depth = ("mixed_s", MIXED_S_BUFS) if n in TURN_P + (SCALAR_UNIT,) else ("mixed_g", 1) if n in HANDED_ON else ("mixed", MIXED_BUFS)
             if n not in mixed and slot_free(tag, depth):
-                mixed[n] = take([P, W * T], BF16, f"mixed_{n}", tag, depth, [("codes", n, k) for k in range(T)])
+                mixed[n] = take([P, W * T], BF16, f"mixed_{n}", tag, depth, [("codes", n, k) for k in range(T)])[:]
             return n in mixed
 
         def v_mixed_tile(sweep, g):
@@ -187,21 +194,11 @@ def tile_two_sweep_policy_evaluation_d3_kernel(tc, P_bytes, P_scale, V, R, disco
             n, k = place(q, g, b0)
             if not ({("wide", q, g, t) for t in range(T)} <= done and mixed_tile(n)):
                 return False
-            if engine == "G":
-                nc.gpsimd.tensor_scalar(
-                    out=mixed[n][:].rearrange("p (k m t) -> p m k t", k=T, t=T)[:, :, k : k + b1 - b0],
-                    in0=planes_of(q, g).rearrange("p t (m b) -> p m b t", b=T)[:, :, b0:b1],
-                    scalar1=1.0,
-                    scalar2=0.0,
-                    op0=MULT,
-                    op1=ADD,
-                )
-            else:
-                copier[engine](
-                    out=mixed[n][:].rearrange("p (k m e t) -> p m k t e", k=T, e=2, t=T)[:, :, k : k + b1 - b0],
-                    in_=planes_of(q, g).rearrange("p t (m e b) -> p m b t e", e=2, b=T)[:, :, b0:b1],
-                )
-            note(("mixed", n, j) for j in range(k, k + b1 - b0))
+            copier[engine](
+                out=mixed[n].rearrange("p (k m e t) -> p m k t e", k=T, e=2, t=T)[:, :, k : k + b1 - b0],
+                in_=planes_of(q, g).rearrange("p t (m e b) -> p m b t e", e=2, b=T)[:, :, b0:b1],
+            )
+            note(("mixed",) + place(q, g, b) for b in range(b0, b1))
             return True
 
         def interleave_half(engine, n, half):
@@ -210,7 +207,7 @@ def tile_two_sweep_policy_evaluation_d3_kernel(tc, P_bytes, P_scale, V, R, disco
                 return False
             if engine == "G":
                 nc.gpsimd.tensor_scalar(
-                    out=mixed[n][:].rearrange("p (b h m t) -> p h m b t", b=T, h=2, t=T)[:, half],
+                    out=mixed[n].rearrange("p (b h m t) -> p h m b t", b=T, h=2, t=T)[:, half],
                     in0=planes_of(q, g).rearrange("p t (h m b) -> p h m b t", h=2, b=T)[:, half],
                     scalar1=1.0,
                     scalar2=0.0,
@@ -219,45 +216,49 @@ def tile_two_sweep_policy_evaluation_d3_kernel(tc, P_bytes, P_scale, V, R, disco
                 )
             else:
                 copier[engine](
-                    out=mixed[n][:].rearrange("p (b h m e t) -> p h m b t e", b=T, h=2, e=2, t=T)[:, half],
+                    out=mixed[n].rearrange("p (b h m e t) -> p h m b t e", b=T, h=2, e=2, t=T)[:, half],
                     in_=planes_of(q, g).rearrange("p t (h m e b) -> p h m b t e", h=2, e=2, b=T)[:, half],
                 )
             done.add(("half", n, half))
             if ("half", n, 1 - half) in done:
-                note(("mixed", n, j) for j in range(T))
+                note(("mixed",) + place(q, g, b) for b in range(T))
             return True
 
-        def interleave_tile(engine, b, half):
-            q, n = G - 1, G * (G - 1) + b
-            if not ({("wide", q, g, t) for g in (2 * half, 2 * half + 1) for t in range(T)} <= done and mixed_tile(n)):
+        def interleave_tile(engine, b):
+            q = G - 1
+            n, k = place(q, 0, b)
+            if not ({("wide", q, g, t) for g in range(2) for t in range(T)} <= done and mixed_tile(n)):
                 return False
             copier[engine](
-                out=mixed[n][:].rearrange("p (g m e t) -> p g m t e", g=G, e=2, t=T)[:, 2 * half : 2 * half + 2],
-                in_=slots[q][:, 2 * half : 2 * half + 2, :, :W].rearrange("p g t (m e b) -> p b g m t e", e=2, b=T)[:, b],
+                out=mixed[n].rearrange("p (k m e t) -> p k m t e", k=T, e=2, t=T)[:, k : k + 2],
+                in_=slots[q][:, :2, :, :W].rearrange("p g t (m e b) -> p b g m t e", e=2, b=T)[:, b],
             )
-            note(("mixed", n, g) for g in (2 * half, 2 * half + 1))
+            note(("mixed", n, k + g) for g in range(2))
             return True
 
-        def turn(engine, kind, n, h, bank):
+        def turn(engine, kind, n, h, u, bank):
             q, g = divmod(n, G)
-            needs = {"p": {("wide", q, g, t) for t in range(T)}, "v": set(), "u": {("row", n, b, k) for b in range(T) for k in (2 * h, 2 * h + 1)}}[kind]
-            if not (needs <= done and slot_free(f"bank_{bank}", 1)):
+            pair = (2 * u, 2 * u + 1)
+            needs = {"p": {("wide", q, g, t) for t in pair}, "v": set(), "u": {("row", n, b, k) for b in pair for k in (2 * h, 2 * h + 1)}}[kind]
+            if not needs <= done:
                 return False
+            if (kind, n, h) not in turned:
+                if not slot_free(f"bank_{bank}", 1):
+                    return False
+                waits[f"bank_{bank}"].append({("emptied", kind, n, h)})
+                turned[kind, n, h] = psum.tile([P, 2 * W], BF16, name=f"turn_{kind}{n}_{h}", tag=f"bank_{bank}")
             planes = planes_of(q, g) if kind == "p" else v_raw[:, n] if kind == "v" else v1_rows[n][:]
             tiles = T if kind == "p" else 1
-            waits[f"bank_{bank}"].append({("emptied", kind, n, h)})
-            tile = psum.tile([P, 2 * W], BF16, name=f"turn_{kind}{n}_{h}", tag=f"bank_{bank}")
-            turned[kind, n, h] = tile
-            for j in range(2):
-                first = (2 * h + j) * P
-                nc.tensor.matmul(
-                    out=tile[:].rearrange("p (j b m t) -> p j t m b", j=2, b=tiles, t=T)[:, j],
-                    lhsT=identity[:],
-                    rhs=planes[:, :, first : first + P].rearrange("p t (m b) -> p t m b", b=tiles),
-                    start=True,
-                    stop=True,
-                )
-            done.add(("turned", kind, n, h))
+            nc.tensor.matmul(
+                out=turned[kind, n, h][:].rearrange("p (b m u t) -> p u t m b", b=tiles, u=2, t=2)[:, u],
+                lhsT=identity[:],
+                rhs=planes[:, 2 * u : 2 * u + 2, h * HALF : (h + 1) * HALF].rearrange("p t (m b) -> p t m b", b=tiles),
+                start=True,
+                stop=True,
+            )
+            done.add(("pair", kind, n, h, u))
+            if ("pair", kind, n, h, 1 - u) in done:
+                done.add(("turned", kind, n, h))
             return True
 
         def empty(engine, kind, n, h):
@@ -268,8 +269,8 @@ def tile_two_sweep_policy_evaluation_d3_kernel(tc, P_bytes, P_scale, V, R, disco
                 if not mixed_tile(n):
                     return False
                 copier[engine](
-                    out=mixed[n][:].bitcast(F32).rearrange("p (b h j x) -> p h b j x", b=T, h=2, j=2)[:, h],
-                    in_=words.rearrange("p (j b x) -> p b j x", j=2, b=T),
+                    out=mixed[n].bitcast(F32).rearrange("p (b h x) -> p h b x", b=T, h=2)[:, h],
+                    in_=words.rearrange("p (b x) -> p b x", b=T),
                 )
                 if ("emptied", kind, n, 1 - h) in done:
                     note(("mixed", n, b) for b in range(T))
@@ -403,8 +404,8 @@ def tile_two_sweep_policy_evaluation_d3_kernel(tc, P_bytes, P_scale, V, R, disco
 
         finished = []
 
-        def finish(engine, tile, c0=0, c1=C):
-            needs = {("sum", 1, tile, G - 1, c0)} | ({("rewarded", tile)} if tile in EXITS else set())
+        def finish(engine, tile, c0=0, c1=C, first=0):
+            needs = {("sum", 1, tile, G - 1, first)} | ({("rewarded", tile)} if tile in EXITS else set())
             if not needs <= done:
                 return False
             q, b = divmod(tile, T)
@@ -417,7 +418,7 @@ def tile_two_sweep_policy_evaluation_d3_kernel(tc, P_bytes, P_scale, V, R, disco
                 results[half] = take([P, 2 * T, C], F32, f"results_{half}", "wide", WIDE_BUFS, [])
             dst = results[half][:, place, c0:c1]
             addend = parked[tile][:, c0:c1] if tile in EXITS else r_sb[:, q, b, c0:c1]
-            update(dst, acc[1, tile, c0][:], q, b, addend)
+            update(dst, acc[1, tile, first][:, c0 - first : c1 - first], q, b, addend)
             if tile in JOINED:
                 nc.sync.dma_start(out=out_view[q][:, b - 1 : b + 1], in_=results[half][:, place - 1 : place + 1])
             elif tile + 1 not in JOINED:
@@ -440,8 +441,8 @@ def tile_two_sweep_policy_evaluation_d3_kernel(tc, P_bytes, P_scale, V, R, disco
         def il(n, b0=0, b1=T):
             return [(interleave, n // G, n % G, b0, b1)]
 
-        def ilt(b, half):
-            return [(interleave_tile, b, half)]
+        def ilt(b):
+            return [(interleave_tile, b)]
 
         def qp(n, k0=0, k1=T):
             return [(quantise, n, k0, k1)]
@@ -456,7 +457,10 @@ def tile_two_sweep_policy_evaluation_d3_kernel(tc, P_bytes, P_scale, V, R, disco
             return [(quantise_v, sweep, g, c0, c1)]
 
         def tn(kind, n, bank):
-            return [(turn, kind, n, h, bank + h) for h in range(2)]
+            return [(turn, kind, n, h, u, bank + h) for h in range(2) for u in range(2)]
+
+        def tn_pairs(kind, n, bank, us=range(2)):
+            return [(turn, kind, n, h, u, bank + h) for u in us for h in range(2)]
 
         def mx1(tiles, gs, bank=None):
             return [(multiply, 0, tile, g, bank + j if g == 0 else None, g == G - 1) for g in gs for j, tile in enumerate(tiles)]
@@ -464,33 +468,35 @@ def tile_two_sweep_policy_evaluation_d3_kernel(tc, P_bytes, P_scale, V, R, disco
         def mx2(tile, gs, bank=None, c0=0, c1=C):
             return [(multiply, 1, tile, g, bank if g == gs[0] else None, g == G - 1 or g == EXITS.get(tile), c0, c1) for g in gs]
 
-        scalar = wd1(1, 0, [1]) + wd1(0, 0, [1]) + wd(0, 1, [1, 2]) + ev("p", 4) + wd(0, 2, [0]) + ev("v", 0, [0]) + wd(0, 2, [1]) + ev("v", 0, [1]) + wd(0, 3, [0]) + ev("v", 1) + wd(0, 3, [1]) + ev("v", 2) + wd(2, 0, [0, 1]) + ev("v", 3) + wd(2, 0, [2, 3]) + ev("p", 7)
-        scalar = scalar + wd(2, 1) + wd(2, 2) + wd(2, 3) + wd(3, 0) + wd(3, 1, [0, 1, 2]) + ev("u", 1, [0]) + [(widen_discount,)] + wd(3, 1, [3]) + ev("u", 1, [1]) + wd(3, 2) + [(park, 0), (park, 1)] + wd(3, 3, [0])
-        scalar = scalar + [(park, 2), (park, 3)] + ilt(2, 0) + ilt(2, 1) + ilt(3, 0) + ilt(3, 1) + ilv(2) + ilv(3, 3 * P, C)
+        scalar = wd1(1, 0, [1]) + wd1(0, 0, [1, 3]) + wd(0, 1, [1, 2]) + ev("p", 4) + wd(0, 2, [0]) + ev("p", 5) + ev("v", 0) + wd(0, 2, [1]) + ev("v", 1) + wd(0, 3, [0]) + ev("v", 2) + wd(0, 3, [1]) + ev("v", 3) + wd(2, 0)
+        scalar = scalar + wd(2, 1) + wd(2, 2) + wd(2, 3) + wd(3, 0, [0]) + ilv(0, HALF, C) + wd(3, 0, [1, 2, 3]) + wd(3, 1, [0]) + ev("u", 1, [0]) + [(widen_discount,)] + ev("u", 1, [1]) + wd(3, 1, [1, 2, 3]) + [(park, 0), (park, 1)] + wd(3, 2, [0]) + [(park, 2), (park, 3)]
+        scalar = scalar + ilt(2) + wd(3, 3, [0, 1, 2]) + ilt(3) + [(park, 12)] + il(15, 3, 4) + ilv(2) + ilv(3, HALF, C)
 
-        vector = wd1(1, 0, [0]) + wd1(0, 0, [0]) + wd1(1, 0, [2, 3]) + wd1(0, 0, [2, 3]) + wd(0, 1, [0]) + il(0) + wd(0, 1, [3]) + qp(0) + il(1) + wd(0, 2, [2, 3]) + qp(1) + il(5) + qp(4) + wd(0, 3, [3]) + qv(0, 0) + il(2) + wd(0, 3, [2]) + qv(0, 1) + qp(2)
-        vector = vector + il(3) + qp(5) + qv(0, 2) + qp(3) + il(6) + qv(0, 3) + il(8) + qp(7) + qp(6) + upd(range(4)) + ilh(9, 1) + qp(8) + qp(9) + upd(range(4, 8))
-        vector = vector + ilv(0, HALF, C) + il(10) + qv(1, 0) + qp(10) + il(11) + qv(1, 1) + qp(11) + wd(3, 3, [1, 2, 3]) + il(12, 0, 2)
-        vector = vector + upd([8, 9]) + il(13, 0, 2) + qp(12, 0, 2) + il(14, 0, 2) + qp(12, 2, 4) + il(15, 0, 2) + qp(13, 0, 2) + qp(14, 0, 2) + qp(13, 2, 4) + upd([10]) + qp(14, 2, 4) + upd([11]) + qp(15, 0, 2) + upd([12]) + qp(15, 2, 4) + upd([13, 14])
-        vector = vector + upd([15], 0, HALF) + upd([15], HALF, C) + qv(1, 2) + ilv(3, 0, HALF) + ilv(3, HALF, 3 * P) + qv(1, 3, 0, HALF) + qv(1, 3, HALF, C)
-        order = [8, 9, 10, 11, 4, 5, 6, 7, 0, 12, 1, 13, 2, 14, 3]
-        vector = vector + [(finish, tile) for tile in order] + [(finish, 15, 0, HALF), (finish, 15, HALF, C)]
+        vector = wd1(1, 0, [0]) + wd1(0, 0, [0]) + wd1(1, 0, [2, 3]) + wd1(0, 0, [2]) + wd(0, 1, [0]) + il(0) + wd(0, 1, [3]) + qp(0) + il(1) + wd(0, 2, [2, 3]) + qp(1) + qp(4) + wd(0, 3, [3, 2]) + qp(5) + qv(0, 0) + il(2) + qv(0, 1) + il(6) + qp(2) + qv(0, 2)
+        vector = vector + il(3) + qp(6) + il(7) + qv(0, 3) + qp(3) + il(8) + qp(7) + qp(8) + upd(range(4)) + ilh(9, 1) + il(10, 0, 2) + qp(9) + upd(range(4, 8))
+        vector = vector + il(10, 2, 4) + qv(1, 0) + qp(10) + il(11) + qv(1, 1) + qp(11) + il(12, 0, 2) + il(13, 0, 2) + wd(3, 2, [1]) + qp(12, 0, 2) + qp(12, 2, 4) + wd(3, 2, [2, 3]) + upd(range(8, 12))
+        vector = vector + qp(13, 0, 2) + ilh(14, 1) + wd(3, 3, [3]) + qp(14, 0, 2) + il(15, 0, 3) + qp(14, 2, 3) + qp(15, 0, 2) + qp(13, 2, 4) + qp(15, 2, 3) + qp(14, 3, 4) + upd([12]) + qp(15, 3, 4) + upd([13, 14])
+        vector = vector + upd([15], 0, HALF) + upd([15], HALF, C) + qv(1, 2) + ilv(3, 0, HALF) + qv(1, 3, HALF, C) + qv(1, 3, 0, HALF)
+        order = [8, 9, 10, 11, 4, 5, 6, 7, 0, 1, 13, 2, 3, 12, 14]
+        pieces = [(0, HALF), (HALF, C)]
+        vector = vector + [(finish, tile) for tile in order] + [(finish, 15, c0, c1, c0) for c0, c1 in pieces]
 
-        gpsimd = ilh(9, 0) + ilv(0, 0, HALF) + [(add_reward, tile) for tile in EXITS]
+        gpsimd = ilh(9, 0) + ilv(0, 0, HALF) + ilh(14, 0) + [(add_reward, tile) for tile in EXITS]
 
         every = list(range(G))
-        tensor = tn("p", 4, 4) + tn("v", 0, 6) + tn("v", 1, 4) + tn("v", 2, 6) + tn("v", 3, 4) + tn("p", 7, 6) + mx1(range(4), every, 0)
-        tensor = tensor + mx1(range(4, 8), every, 4) + mx1(range(8, 12), [0, 1], 0) + tn("u", 1, 4) + mx2(0, [0], 6) + mx2(1, [0], 7) + mx1(range(8, 12), [2]) + mx2(2, [0], 4) + mx2(3, [0], 5)
-        tensor = tensor + mx2(0, [1]) + mx2(1, [1]) + mx1([8, 9], [3]) + mx2(2, [1]) + mx2(3, [1]) + mx1([10, 11], [3])
-        tensor = tensor + mx2(8, [0, 1], 6) + mx2(9, [0, 1], 7) + mx2(10, [0, 1], 4) + mx1([12, 13], [0], 0) + mx2(11, [0, 1], 5)
-        tensor = tensor + mx1([12, 13], [1, 2, 3]) + mx1([14], every, 2) + mx1([15], [0, 1], 3) + mx2(4, [0], 0) + mx1([15], [2, 3]) + mx2(4, [1]) + mx2(5, [0, 1], 1) + mx2(6, [0, 1], 2) + mx2(7, [0, 1], 3)
-        for tile in order[:5]:
+        tensor = tn_pairs("p", 4, 4) + tn_pairs("p", 5, 6) + tn("v", 0, 0) + tn("v", 1, 2) + tn("v", 2, 4) + tn("v", 3, 6) + mx1(range(4), [0, 1], 0) + mx1(range(4, 8), [0, 1], 4) + mx1(range(4), [2, 3])
+        tensor = tensor + mx1(range(4, 8), [2, 3]) + mx1(range(8, 12), [0, 1], 0) + tn_pairs("u", 1, 4) + mx2(0, [0], 6) + mx2(1, [0], 7) + mx1(range(8, 12), [2]) + mx2(2, [0], 4) + mx2(3, [0], 5)
+        tensor = tensor + mx2(0, [1]) + mx2(1, [1]) + mx2(2, [1]) + mx2(3, [1]) + mx1(range(8, 12), [3])
+        tensor = tensor + mx2(8, [0, 1], 6) + mx2(9, [0, 1], 7) + mx2(10, [0, 1], 4) + mx2(11, [0, 1], 5)
+        tensor = tensor + mx1([12, 13], [0, 1], 0) + mx1([14], [0, 1], 2) + mx2(12, [0, 1], 3) + mx1([12, 13, 14], [2]) + mx1([12, 13], [3]) + mx1([15], [0], 3) + mx1([14], [3]) + mx1([15], [1, 2, 3]) + mx2(4, [0, 1], 0) + mx2(5, [0, 1], 1) + mx2(6, [0, 1], 2) + mx2(7, [0, 1], 3)
+        for tile in order[:3]:
             tensor = tensor + mx2(tile, [2])
         for k, tile in enumerate(order[:8]):
-            tensor = tensor + mx2(tile, [3]) + [step for later in order[5 + k : 8][:1] for step in mx2(later, [2])]
+            tensor = tensor + mx2(tile, [3]) + [step for later in order[3 + k : 8][:1] for step in mx2(later, [2])]
         for tile, bank in zip(order[8:], [6, 7, 4, 5, 0, 1, 2]):
             tensor = tensor + mx2(tile, [2, 3] if tile in EXITS else every, bank)
-        tensor = tensor + mx2(15, every, 3, 0, HALF) + mx2(15, every, 6, HALF, C)
+        for (c0, c1), bank in zip(pieces, [3, 6, 7]):
+            tensor = tensor + mx2(15, every, bank, c0, c1)
 
 
         queues = {"S": scalar, "V": vector, "T": tensor, "G": gpsimd}

@@ -87,6 +87,7 @@ def tile_two_sweep_policy_evaluation_d3_kernel(tc, P_bytes, P_scale, V, R, disco
 
         nc.scalar.dma_start(out=scale_0[:], in_=scale_view[:, 0])
         load_first(0)
+        nc.scalar.dma_start(out=scale_rest[:], in_=scale_view[:, 1:])
         warm_in = keep.tile([P, 1], F32, name="warm_in")
         warm_out = keep.tile([P, 1], F32, name="warm_out")
         nc.vector.memset(warm_in[:], 0.0)
@@ -94,7 +95,6 @@ def tile_two_sweep_policy_evaluation_d3_kernel(tc, P_bytes, P_scale, V, R, disco
         load_first(1)
         load_first(2)
         load_first(3)
-        nc.sync.dma_start(out=scale_rest[:], in_=scale_view[:, 1:])
         load_head(0)
         load_head(1)
         load_pair(2)
@@ -392,12 +392,17 @@ def tile_two_sweep_policy_evaluation_d3_kernel(tc, P_bytes, P_scale, V, R, disco
             if ("parked", tile) not in done:
                 return False
             q, b = divmod(tile, T)
-            if "late" not in turned:
-                if not ((1, G - 1) in v_mixed and slot_free("last", 1)):
+            if engine == "V":
+                if not slot_free("last", 1):
                     return False
-                turned["late"] = take([P, C], F32, "late", "last", 1, [])
-            dst = turned["late"][:] if tile == 0 else parked[tile]
-            nc.gpsimd.tensor_tensor(out=dst, in0=parked[tile], in1=r_sb[:, q, b], op=ADD)
+                dst = take([P, C], F32, "late", "last", 1, [])[:]
+                nc.vector.tensor_tensor(out=dst, in0=parked[tile], in1=r_sb[:, q, b], op=ADD)
+                parked["spare"] = parked[tile]
+            else:
+                if "spare" not in parked:
+                    return False
+                dst = parked["spare"] if tile == 0 else parked[tile]
+                nc.gpsimd.tensor_tensor(out=dst, in0=parked[tile], in1=r_sb[:, q, b], op=ADD)
             parked[tile] = dst
             done.add(("rewarded", tile))
             return True
@@ -476,12 +481,12 @@ def tile_two_sweep_policy_evaluation_d3_kernel(tc, P_bytes, P_scale, V, R, disco
         vector = vector + il(3) + qp(6) + il(7) + qv(0, 3) + qp(3) + il(8) + qp(7) + qp(8) + upd(range(4)) + ilh(9, 1) + il(10, 0, 2) + qp(9) + upd(range(4, 8))
         vector = vector + il(10, 2, 4) + qv(1, 0) + qp(10) + il(11) + qv(1, 1) + qp(11) + il(12, 0, 2) + il(13, 0, 2) + wd(3, 2, [1]) + qp(12, 0, 2) + qp(12, 2, 4) + wd(3, 2, [2, 3]) + upd(range(8, 12))
         vector = vector + qp(13, 0, 2) + ilh(14, 1) + wd(3, 3, [3]) + qp(14, 0, 2) + il(15, 0, 3) + qp(14, 2, 3) + qp(15, 0, 2) + qp(13, 2, 4) + qp(15, 2, 3) + qp(14, 3, 4) + upd([12]) + qp(15, 3, 4) + upd([13, 14])
-        vector = vector + upd([15], 0, HALF) + upd([15], HALF, C) + qv(1, 2) + ilv(3, 0, HALF) + qv(1, 3, HALF, C) + qv(1, 3, 0, HALF)
-        order = [8, 9, 10, 11, 4, 5, 6, 7, 0, 1, 13, 2, 3, 12, 14]
+        vector = vector + upd([15], 0, HALF) + upd([15], HALF, C) + qv(1, 2) + ilv(3, 0, HALF) + qv(1, 3, HALF, C) + qv(1, 3, 0, HALF) + [(add_reward, 12)]
+        order = [8, 9, 10, 11, 4, 5, 6, 7, 12, 0, 13, 1, 2, 14, 3]
         pieces = [(0, HALF), (HALF, C)]
         vector = vector + [(finish, tile) for tile in order] + [(finish, 15, c0, c1, c0) for c0, c1 in pieces]
 
-        gpsimd = ilh(9, 0) + ilv(0, 0, HALF) + ilh(14, 0) + [(add_reward, tile) for tile in EXITS]
+        gpsimd = ilh(9, 0) + ilv(0, 0, HALF) + ilh(14, 0) + [(add_reward, tile) for tile in range(4)]
 
         every = list(range(G))
         tensor = tn_pairs("p", 4, 4) + tn_pairs("p", 5, 6) + tn("v", 0, 0) + tn("v", 1, 2) + tn("v", 2, 4) + tn("v", 3, 6) + mx1(range(4), [0, 1], 0) + mx1(range(4, 8), [0, 1], 4) + mx1(range(4), [2, 3])

@@ -248,14 +248,14 @@ def tile_two_sweep_policy_evaluation_d3_kernel(tc, P_bytes, P_scale, V, R, disco
                 waits[f"bank_{bank}"].append({("emptied", kind, n, h)})
                 turned[kind, n, h] = psum.tile([P, 2 * W], BF16, name=f"turn_{kind}{n}_{h}", tag=f"bank_{bank}")
             planes = planes_of(q, g) if kind == "p" else v_raw[:, n] if kind == "v" else v1_rows[n][:]
-            tiles = T if kind == "p" else 1
-            nc.tensor.matmul(
-                out=turned[kind, n, h][:].rearrange("p (b m u t) -> p u t m b", b=tiles, u=2, t=2)[:, u],
-                lhsT=identity[:],
-                rhs=planes[:, 2 * u : 2 * u + 2, h * HALF : (h + 1) * HALF].rearrange("p t (m b) -> p t m b", b=tiles),
-                start=True,
-                stop=True,
-            )
+            if kind == "v":
+                first = (2 * h + u) * P
+                dst, src = turned[kind, n, h][:].rearrange("p (u c t) -> p u t c", u=2, t=T)[:, u], planes[:, :, first : first + P]
+            else:
+                tiles = T if kind == "p" else 1
+                dst = turned[kind, n, h][:].rearrange("p (b m u t) -> p u t m b", b=tiles, u=2, t=2)[:, u]
+                src = planes[:, 2 * u : 2 * u + 2, h * HALF : (h + 1) * HALF].rearrange("p t (m b) -> p t m b", b=tiles)
+            nc.tensor.matmul(out=dst, lhsT=identity[:], rhs=src, start=True, stop=True)
             done.add(("pair", kind, n, h, u))
             if ("pair", kind, n, h, 1 - u) in done:
                 done.add(("turned", kind, n, h))
@@ -272,7 +272,8 @@ def tile_two_sweep_policy_evaluation_d3_kernel(tc, P_bytes, P_scale, V, R, disco
                     out=mixed[n].bitcast(F32).rearrange("p (b h x) -> p h b x", b=T, h=2)[:, h],
                     in_=words.rearrange("p (b x) -> p b x", b=T),
                 )
-                if ("emptied", kind, n, 1 - h) in done:
+                done.add(("half", n, h))
+                if ("half", n, 1 - h) in done:
                     note(("mixed", n, b) for b in range(T))
             else:
                 sweep = 0 if kind == "v" else 1
@@ -461,8 +462,8 @@ def tile_two_sweep_policy_evaluation_d3_kernel(tc, P_bytes, P_scale, V, R, disco
         def qv(sweep, g, c0=0, c1=C):
             return [(quantise_v, sweep, g, c0, c1)]
 
-        def tn(kind, n, bank):
-            return [(turn, kind, n, h, u, bank + h) for h in range(2) for u in range(2)]
+        def tn(kind, n, bank, hs=range(2)):
+            return [(turn, kind, n, h, u, bank + k) for k, h in enumerate(hs) for u in range(2)]
 
         def tn_pairs(kind, n, bank, us=range(2)):
             return [(turn, kind, n, h, u, bank + h) for u in us for h in range(2)]
@@ -473,15 +474,15 @@ def tile_two_sweep_policy_evaluation_d3_kernel(tc, P_bytes, P_scale, V, R, disco
         def mx2(tile, gs, bank=None, c0=0, c1=C):
             return [(multiply, 1, tile, g, bank if g == gs[0] else None, g == G - 1 or g == EXITS.get(tile), c0, c1) for g in gs]
 
-        scalar = wd1(1, 0, [1]) + wd1(0, 0, [1, 3]) + wd(0, 1, [1, 2]) + ev("p", 4) + wd(0, 2, [0]) + ev("p", 5) + ev("v", 0) + wd(0, 2, [1]) + ev("v", 1) + wd(0, 3, [0]) + ev("v", 2) + wd(0, 3, [1]) + ev("v", 3) + wd(2, 0)
-        scalar = scalar + wd(2, 1) + wd(2, 2) + wd(2, 3) + wd(3, 0, [0]) + ilv(0, HALF, C) + wd(3, 0, [1, 2, 3]) + wd(3, 1, [0]) + ev("u", 1, [0]) + [(widen_discount,)] + ev("u", 1, [1]) + wd(3, 1, [1, 2, 3]) + [(park, 0), (park, 1)] + wd(3, 2, [0]) + [(park, 2), (park, 3)]
+        scalar = wd1(1, 0, [1]) + wd1(0, 0, [1, 3]) + wd(0, 1, [1, 2]) + ev("p", 4) + wd(0, 2, [0]) + ev("p", 5) + wd(0, 2, [1]) + ev("v", 0) + wd(0, 3, [0]) + ev("v", 1) + wd(0, 3, [1]) + ev("v", 2) + wd(2, 0, [0]) + ev("v", 3) + wd(2, 0, [1, 2, 3])
+        scalar = scalar + wd(2, 1) + wd(2, 2) + wd(2, 3) + wd(3, 0, [0]) + ilv(0, HALF, C) + wd(3, 0, [1]) + [(widen_discount,)] + ilv(1, HALF, C) + ev("u", 1, [0]) + wd(3, 0, [2, 3]) + wd(3, 1, [0, 1, 2]) + [(park, 0), (park, 1)] + wd(3, 2, [0]) + [(park, 2), (park, 3)]
         scalar = scalar + ilt(2) + wd(3, 3, [0, 1, 2]) + ilt(3) + [(park, 12)] + il(15, 3, 4) + ilv(2) + ilv(3, HALF, C)
 
-        vector = wd1(1, 0, [0]) + wd1(0, 0, [0]) + wd1(1, 0, [2, 3]) + wd1(0, 0, [2]) + wd(0, 1, [0]) + il(0) + wd(0, 1, [3]) + qp(0) + il(1) + wd(0, 2, [2, 3]) + qp(1) + qp(4) + wd(0, 3, [3, 2]) + qp(5) + qv(0, 0) + il(2) + qv(0, 1) + il(6) + qp(2) + qv(0, 2)
-        vector = vector + il(3) + qp(6) + il(7) + qv(0, 3) + qp(3) + il(8) + qp(7) + qp(8) + upd(range(4)) + ilh(9, 1) + il(10, 0, 2) + qp(9) + upd(range(4, 8))
-        vector = vector + il(10, 2, 4) + qv(1, 0) + qp(10) + il(11) + qv(1, 1) + qp(11) + il(12, 0, 2) + il(13, 0, 2) + wd(3, 2, [1]) + qp(12, 0, 2) + qp(12, 2, 4) + wd(3, 2, [2, 3]) + upd(range(8, 12))
+        vector = wd1(1, 0, [0]) + wd1(0, 0, [0]) + wd1(1, 0, [2, 3]) + wd1(0, 0, [2]) + wd(0, 1, [0]) + il(0) + wd(0, 1, [3]) + qp(0) + il(1) + wd(0, 2, [2, 3]) + qp(1) + qp(4) + wd(0, 3, [3, 2]) + qp(5) + il(2) + qv(0, 0) + il(6) + qv(0, 1) + qp(2)
+        vector = vector + il(3) + qv(0, 2) + qp(3) + il(7) + qv(0, 3) + qp(6) + il(8) + qp(7) + qp(8) + upd(range(4)) + ilh(9, 1) + il(10, 0, 2) + qp(9) + upd(range(4, 8))
+        vector = vector + qv(1, 0) + il(10, 2, 4) + wd(3, 1, [3]) + qp(10) + il(11) + qv(1, 1) + qp(11) + il(12, 0, 2) + il(13, 0, 2) + wd(3, 2, [1]) + qp(12) + wd(3, 2, [2, 3]) + upd(range(8, 12))
         vector = vector + qp(13, 0, 2) + ilh(14, 1) + wd(3, 3, [3]) + qp(14, 0, 2) + il(15, 0, 3) + qp(14, 2, 3) + qp(15, 0, 2) + qp(13, 2, 4) + qp(15, 2, 3) + qp(14, 3, 4) + upd([12]) + qp(15, 3, 4) + upd([13, 14])
-        vector = vector + upd([15], 0, HALF) + upd([15], HALF, C) + qv(1, 2) + ilv(3, 0, HALF) + qv(1, 3, HALF, C) + qv(1, 3, 0, HALF) + [(add_reward, 12)]
+        vector = vector + upd([15], HALF, C) + upd([15], 0, HALF) + qv(1, 2) + ilv(3, 0, HALF) + qv(1, 3, HALF, C) + qv(1, 3, 0, HALF) + [(add_reward, 12)]
         order = [8, 9, 10, 11, 4, 5, 6, 7, 12, 0, 13, 1, 2, 14, 3]
         pieces = [(0, HALF), (HALF, C)]
         vector = vector + [(finish, tile) for tile in order] + [(finish, 15, c0, c1, c0) for c0, c1 in pieces]
@@ -489,18 +490,18 @@ def tile_two_sweep_policy_evaluation_d3_kernel(tc, P_bytes, P_scale, V, R, disco
         gpsimd = ilh(9, 0) + ilv(0, 0, HALF) + ilh(14, 0) + [(add_reward, tile) for tile in range(4)]
 
         every = list(range(G))
-        tensor = tn_pairs("p", 4, 4) + tn_pairs("p", 5, 6) + tn("v", 0, 0) + tn("v", 1, 2) + tn("v", 2, 4) + tn("v", 3, 6) + mx1(range(4), [0, 1], 0) + mx1(range(4, 8), [0, 1], 4) + mx1(range(4), [2, 3])
-        tensor = tensor + mx1(range(4, 8), [2, 3]) + mx1(range(8, 12), [0, 1], 0) + tn_pairs("u", 1, 4) + mx2(0, [0], 6) + mx2(1, [0], 7) + mx1(range(8, 12), [2]) + mx2(2, [0], 4) + mx2(3, [0], 5)
+        tensor = tn_pairs("p", 4, 4) + tn_pairs("p", 5, 6) + tn("v", 0, 0) + tn("v", 1, 2) + tn("v", 2, 4) + tn("v", 3, 6) + mx1(range(4), every, 0) + mx1(range(4, 8), [0, 1], 4)
+        tensor = tensor + mx1(range(4, 8), [2, 3]) + mx1(range(8, 12), [0, 1], 0) + tn("u", 1, 4, [0]) + mx2(0, [0], 5) + mx2(1, [0], 6) + mx2(2, [0], 7) + mx1(range(8, 12), [2]) + mx2(3, [0], 4)
         tensor = tensor + mx2(0, [1]) + mx2(1, [1]) + mx2(2, [1]) + mx2(3, [1]) + mx1(range(8, 12), [3])
-        tensor = tensor + mx2(8, [0, 1], 6) + mx2(9, [0, 1], 7) + mx2(10, [0, 1], 4) + mx2(11, [0, 1], 5)
+        tensor = tensor + mx2(8, [0, 1], 5) + mx2(9, [0, 1], 6) + mx2(10, [0, 1], 7) + mx2(11, [0, 1], 4)
         tensor = tensor + mx1([12, 13], [0, 1], 0) + mx1([14], [0, 1], 2) + mx2(12, [0, 1], 3) + mx1([12, 13, 14], [2]) + mx1([12, 13], [3]) + mx1([15], [0], 3) + mx1([14], [3]) + mx1([15], [1, 2, 3]) + mx2(4, [0, 1], 0) + mx2(5, [0, 1], 1) + mx2(6, [0, 1], 2) + mx2(7, [0, 1], 3)
         for tile in order[:3]:
             tensor = tensor + mx2(tile, [2])
         for k, tile in enumerate(order[:8]):
             tensor = tensor + mx2(tile, [3]) + [step for later in order[3 + k : 8][:1] for step in mx2(later, [2])]
-        for tile, bank in zip(order[8:], [6, 7, 4, 5, 0, 1, 2]):
+        for tile, bank in zip(order[8:], [5, 6, 7, 4, 0, 1, 2]):
             tensor = tensor + mx2(tile, [2, 3] if tile in EXITS else every, bank)
-        for (c0, c1), bank in zip(pieces, [3, 6, 7]):
+        for (c0, c1), bank in zip(pieces, [3, 5, 6]):
             tensor = tensor + mx2(15, every, bank, c0, c1)
 
 

@@ -474,14 +474,14 @@ def tile_two_sweep_policy_evaluation_d3_kernel(tc, P_bytes, P_scale, V, R, disco
         def mx2(tile, gs, bank=None, c0=0, c1=C):
             return [(multiply, 1, tile, g, bank if g == gs[0] else None, g == G - 1 or g == EXITS.get(tile), c0, c1) for g in gs]
 
-        scalar = wd1(1, 0, [1]) + wd1(0, 0, [1, 3]) + wd(0, 1, [1, 2]) + ev("p", 4) + wd(0, 2, [0]) + ev("p", 5) + wd(0, 2, [1]) + ev("v", 0) + wd(0, 3, [0]) + ev("v", 1) + wd(0, 3, [1]) + ev("v", 2) + wd(2, 0, [0]) + ev("v", 3) + wd(2, 0, [1, 2, 3])
-        scalar = scalar + wd(2, 1) + wd(2, 2) + wd(2, 3) + wd(3, 0, [0]) + ilv(0, HALF, C) + wd(3, 0, [1]) + [(widen_discount,)] + ilv(1, HALF, C) + ev("u", 1, [0]) + wd(3, 0, [2, 3]) + wd(3, 1, [0, 1, 2]) + [(park, 0), (park, 1)] + wd(3, 2, [0]) + [(park, 2), (park, 3)]
-        scalar = scalar + ilt(2) + wd(3, 3, [0, 1, 2]) + ilt(3) + [(park, 12)] + il(15, 3, 4) + ilv(2) + ilv(3, HALF, C)
+        scalar = wd1(1, 0, [1, 2, 3]) + wd(0, 1, [1, 2]) + ev("p", 4) + wd(0, 2, [0]) + ev("p", 5) + wd(0, 2, [1]) + ev("v", 0) + wd(0, 3, [0]) + ev("v", 1) + wd(0, 3, [1]) + ev("v", 2) + wd(2, 0, [0]) + ev("v", 3) + wd(2, 0, [1, 2, 3])
+        scalar = scalar + wd(2, 1) + wd(2, 2) + wd(2, 3) + wd(3, 0, [0]) + ilv(0, HALF, C) + wd(3, 0, [1, 2, 3]) + [(widen_discount,)] + wd(3, 1, [0]) + ev("u", 1) + wd(3, 1, [1, 2, 3]) + [(park, 0), (park, 1)] + wd(3, 2, [0]) + [(park, 2), (park, 3)]
+        scalar = scalar + ilt(2) + wd(3, 3, [0, 1]) + ilt(3) + il(15, 3, 4) + [(park, 12)] + ilv(2) + ilv(3, HALF, C)
 
-        vector = wd1(1, 0, [0]) + wd1(0, 0, [0]) + wd1(1, 0, [2, 3]) + wd1(0, 0, [2]) + wd(0, 1, [0]) + il(0) + wd(0, 1, [3]) + qp(0) + il(1) + wd(0, 2, [2, 3]) + qp(1) + qp(4) + wd(0, 3, [3, 2]) + qp(5) + il(2) + qv(0, 0) + il(6) + qv(0, 1) + qp(2)
+        vector = wd1(1, 0, [0]) + wd1(0, 0, range(T)) + il(0) + wd(0, 1, [0]) + qp(0) + wd(0, 1, [3]) + wd(0, 2, [2]) + il(1) + wd(0, 2, [3]) + qp(4) + qp(1) + wd(0, 3, [3, 2]) + qp(5) + il(2) + qv(0, 0) + il(6) + qv(0, 1) + qp(2)
         vector = vector + il(3) + qv(0, 2) + qp(3) + il(7) + qv(0, 3) + qp(6) + il(8) + qp(7) + qp(8) + upd(range(4)) + ilh(9, 1) + il(10, 0, 2) + qp(9) + upd(range(4, 8))
-        vector = vector + qv(1, 0) + il(10, 2, 4) + wd(3, 1, [3]) + qp(10) + il(11) + qv(1, 1) + qp(11) + il(12, 0, 2) + il(13, 0, 2) + wd(3, 2, [1]) + qp(12) + wd(3, 2, [2, 3]) + upd(range(8, 12))
-        vector = vector + qp(13, 0, 2) + ilh(14, 1) + wd(3, 3, [3]) + qp(14, 0, 2) + il(15, 0, 3) + qp(14, 2, 3) + qp(15, 0, 2) + qp(13, 2, 4) + qp(15, 2, 3) + qp(14, 3, 4) + upd([12]) + qp(15, 3, 4) + upd([13, 14])
+        vector = vector + il(10, 2, 4) + qv(1, 0) + qp(10) + il(11) + qv(1, 1) + qp(11) + il(12, 0, 2) + il(13, 0, 2) + wd(3, 2, [1]) + qp(12) + wd(3, 2, [2, 3]) + upd(range(8, 12))
+        vector = vector + ilh(14, 1) + qp(13, 0, 2) + wd(3, 3, [2, 3]) + qp(14, 0, 2) + il(15, 0, 3) + qp(14, 2, 4) + qp(15, 0, 2) + qp(13, 2, 4) + qp(15, 2, 4) + upd([12, 13, 14])
         vector = vector + upd([15], HALF, C) + upd([15], 0, HALF) + qv(1, 2) + ilv(3, 0, HALF) + qv(1, 3, HALF, C) + qv(1, 3, 0, HALF) + [(add_reward, 12)]
         order = [8, 9, 10, 11, 4, 5, 6, 7, 12, 0, 13, 1, 2, 14, 3]
         pieces = [(0, HALF), (HALF, C)]
@@ -491,17 +491,17 @@ def tile_two_sweep_policy_evaluation_d3_kernel(tc, P_bytes, P_scale, V, R, disco
 
         every = list(range(G))
         tensor = tn_pairs("p", 4, 4) + tn_pairs("p", 5, 6) + tn("v", 0, 0) + tn("v", 1, 2) + tn("v", 2, 4) + tn("v", 3, 6) + mx1(range(4), every, 0) + mx1(range(4, 8), [0, 1], 4)
-        tensor = tensor + mx1(range(4, 8), [2, 3]) + mx1(range(8, 12), [0, 1], 0) + tn("u", 1, 4, [0]) + mx2(0, [0], 5) + mx2(1, [0], 6) + mx2(2, [0], 7) + mx1(range(8, 12), [2]) + mx2(3, [0], 4)
+        tensor = tensor + mx1(range(4, 8), [2, 3]) + mx1(range(8, 12), [0, 1], 0) + tn_pairs("u", 1, 4) + mx2(0, [0], 6) + mx2(1, [0], 7) + mx1(range(8, 12), [2]) + mx2(2, [0], 4) + mx2(3, [0], 5)
         tensor = tensor + mx2(0, [1]) + mx2(1, [1]) + mx2(2, [1]) + mx2(3, [1]) + mx1(range(8, 12), [3])
-        tensor = tensor + mx2(8, [0, 1], 5) + mx2(9, [0, 1], 6) + mx2(10, [0, 1], 7) + mx2(11, [0, 1], 4)
-        tensor = tensor + mx1([12, 13], [0, 1], 0) + mx1([14], [0, 1], 2) + mx2(12, [0, 1], 3) + mx1([12, 13, 14], [2]) + mx1([12, 13], [3]) + mx1([15], [0], 3) + mx1([14], [3]) + mx1([15], [1, 2, 3]) + mx2(4, [0, 1], 0) + mx2(5, [0, 1], 1) + mx2(6, [0, 1], 2) + mx2(7, [0, 1], 3)
+        tensor = tensor + mx2(8, [0, 1], 6) + mx2(9, [0, 1], 7) + mx2(10, [0, 1], 4) + mx2(11, [0, 1], 5)
+        tensor = tensor + mx1([12, 13], [0, 1], 0) + mx2(12, [0, 1], 3) + mx1([14], [0, 1], 2) + mx1([12, 13, 14], [2]) + mx1([12, 13, 14], [3]) + mx1([15], every, 3) + mx2(4, [0, 1], 0) + mx2(5, [0, 1], 1) + mx2(6, [0, 1], 2) + mx2(7, [0, 1], 3)
         for tile in order[:3]:
             tensor = tensor + mx2(tile, [2])
         for k, tile in enumerate(order[:8]):
             tensor = tensor + mx2(tile, [3]) + [step for later in order[3 + k : 8][:1] for step in mx2(later, [2])]
-        for tile, bank in zip(order[8:], [5, 6, 7, 4, 0, 1, 2]):
+        for tile, bank in zip(order[8:], [6, 7, 4, 5, 0, 1, 2]):
             tensor = tensor + mx2(tile, [2, 3] if tile in EXITS else every, bank)
-        for (c0, c1), bank in zip(pieces, [3, 5, 6]):
+        for (c0, c1), bank in zip(pieces, [3, 6, 7]):
             tensor = tensor + mx2(15, every, bank, c0, c1)
 
 

from contextlib import ExitStack

import concourse.mybir as mybir
from concourse.masks import make_identity

S, C = 2048, 512
P = 128
T = 4
W = P * T
G = S // W
HALF = C // 2

F32 = mybir.dt.float32
BF16 = mybir.dt.bfloat16
U32 = mybir.dt.uint32
U8 = mybir.dt.uint8
FP8 = mybir.dt.float8_e4m3fn
FP8X4 = mybir.dt.float8_e4m3fn_x4
MULT = mybir.AluOpType.mult
ADD = mybir.AluOpType.add
COPY = mybir.ActivationFunctionType.Copy

FLOPS = 2 * 2 * S * S * C

TURN_P = (4, 5)
SCALAR_UNIT = 13
EXITS = {0: 1, 1: 1, 2: 1, 3: 1, 12: 1}
WIDE_BUFS = 3
MIXED_BUFS = 3
HANDED_ON = (8, 9, 14)
MIXED_S_BUFS = 2
V_MIXED_BUFS = 3
PAD = 32
JOINED = ()


def tile_two_sweep_policy_evaluation_d3_kernel(tc, P_bytes, P_scale, V, R, discount, out):
    nc = tc.nc

    with ExitStack() as ctx:
        keep = ctx.enter_context(tc.tile_pool(name="keep", bufs=1))
        stream = ctx.enter_context(tc.tile_pool(name="stream", bufs=1))
        psum = ctx.enter_context(tc.psum_pool(name="psum", bufs=1))
        ctx.enter_context(tc.manual_schedule())

        scale_0 = keep.tile([P, T], F32, name="scale_0")
        scale_rest = keep.tile([P, G - 1, T], F32, name="scale_rest")
        disc = keep.tile([P, G, T], BF16, name="disc")
        disc32 = keep.tile([P, G, T], F32, name="disc32")
        first_bytes = [keep.tile([P, 2 * W], U8, name=f"first_bytes_{t}", align_bytes=64) for t in range(T)]
        head_bytes = [keep.tile([P, 2, 2 * W], U8, name=f"head_bytes_{h}", align_bytes=64) for h in range(2)]
        pair_bytes = keep.tile([P, 2, T, 2 * W], U8, name="bytes_01", align_bytes=64)
        late_bytes = keep.tile([P, G, T, 2 * W], U8, name="bytes_23", align_bytes=64)
        v_raw = keep.tile([P, G, T, C], BF16, name="v_raw", align_bytes=64)
        r_sb = keep.tile([P, G, T, C], BF16, name="r_sb", align_bytes=64)
        p_codes = keep.tile([P, G * G, W], U32, name="p_codes", align_bytes=64)
        p_scales = keep.tile([P, G * G, W], U8, name="p_scales", align_bytes=64)
        v_codes = [keep.tile([P, G, C], U32, name=f"v_codes_{s}", align_bytes=64) for s in range(2)]
        v_scales = [keep.tile([P, G, C], U8, name=f"v_scales_{s}", align_bytes=64) for s in range(2)]

        identity = keep.tile([P, P], BF16, name="identity")
        make_identity(nc, identity[:])

        scale_view = P_scale.rearrange("(g p t) o -> p g (t o)", p=P, t=T)
        p_view = P_bytes.rearrange("(g p t) i -> g p t i", p=P, t=T)
        v_view = V.rearrange("(g p t) c -> g p t c", p=P, t=T)
        r_view = R.rearrange("(g p t) c -> g p t c", p=P, t=T)
        out_view = out.rearrange("(g p t) c -> g p t c", p=P, t=T)

        def load_first(t):
            nc.sync.dma_start(out=first_bytes[t][:], in_=p_view[0][:, t, : 2 * W])

        def load_head(h):
            nc.sync.dma_start(out=head_bytes[h][:], in_=p_view[1][:, 2 * h : 2 * h + 2, : 2 * W])

        def load_pair(g):
            nc.sync.dma_start(out=pair_bytes[:, g - 2], in_=p_view[g][:, :, : 2 * W])

        def load_late(g):
            nc.sync.dma_start(out=late_bytes[:, g], in_=p_view[g][:, :, 2 * W :])

        def load_v(g):
            nc.sync.dma_start(out=v_raw[:, g], in_=v_view[g])

        def load_r(q):
            nc.sync.dma_start(out=r_sb[:, q], in_=r_view[q])

        nc.scalar.dma_start(out=scale_0[:], in_=scale_view[:, 0])
        load_first(0)
        nc.scalar.dma_start(out=scale_rest[:], in_=scale_view[:, 1:])
        warm_in = keep.tile([P, 1], F32, name="warm_in")
        warm_out = keep.tile([P, 1], F32, name="warm_out")
        nc.vector.memset(warm_in[:], 0.0)
        nc.scalar.activation(out=warm_out[:], in_=warm_in[:], func=COPY)
        load_first(1)
        load_first(2)
        load_first(3)
        load_head(0)
        load_head(1)
        load_pair(2)
        load_v(0)
        load_v(1)
        load_pair(3)
        load_v(2)
        load_v(3)
        load_late(0)
        load_late(1)
        nc.sync.dma_start(out=disc[:], in_=discount.rearrange("(g p t) o -> p g (t o)", p=P, t=T))
        load_late(2)
        load_r(0)
        load_late(3)
        load_r(1)
        load_r(2)
        load_r(3)

        wide = {}
        slots = {}
        mixed = {}
        v_mixed = {}
        v1_rows = {}
        turned = {}
        parked = {}
        acc = {}
        results = {}
        copier = {"V": nc.vector.tensor_copy, "S": nc.scalar.copy}
        done = set()
        waits = {}

        def note(facts):
            for fact in facts:
                done.add(fact)

        def quarters(c0, c1):
            return range(c0 // P, c1 // P)

        def slot_free(tag, depth):
            users = waits.setdefault(tag, [])
            return len(users) < depth or users[len(users) - depth] <= done

        def take(shape, dtype, name, tag, depth, freed_by):
            waits[tag].append(set(freed_by))
            return stream.tile(shape, dtype, name=name, tag=tag, bufs=depth, align_bytes=64)

        def readers(q, g):
            return [("turned", "p", G * q + g, h) for h in range(2)] if G * q + g in TURN_P else [("mixed",) + place(q, g, b) for b in range(T)]

        def wide_slot(q, g):
            key = g // 2 if q < 2 else q
            if key not in slots:
                if not slot_free("wide", WIDE_BUFS):
                    return False
                chunks = [(k, r) for k in range(2) for r in (2 * key, 2 * key + 1)] if q < 2 else [(q, r) for r in range(G)]
                shape = [P, 2, T, 2 * W + PAD] if q < 2 else [P, G, T, W + PAD]
                slots[key] = take(shape, BF16, f"wide_{key}", "wide", WIDE_BUFS, [fact for chunk in chunks for fact in readers(*chunk)])
            return True

        def planes_of(q, g):
            return slots[g // 2][:, g % 2, :, q * W : (q + 1) * W] if q < 2 else slots[q][:, g, :, :W]

        def widen(engine, q, g, t, paired):
            if not wide_slot(q, g):
                return False
            if q < 2:
                cols = slice(0, 2 * W) if paired else slice(q * W, (q + 1) * W)
                src, dst = (first_bytes[t][:, cols] if g == 0 else head_bytes[t // 2][:, t % 2, cols] if g == 1 else pair_bytes[:, g - 2, t, cols]), slots[g // 2][:, g % 2, t, cols]
            else:
                src, dst = late_bytes[:, g, t, (q - 2) * W : (q - 1) * W], planes_of(q, g)[:, t]
            scale = scale_0[:, t : t + 1] if g == 0 else scale_rest[:, g - 1, t : t + 1]
            if engine == "S":
                nc.scalar.activation(out=dst, in_=src.bitcast(FP8), func=COPY, scale=scale)
            else:
                nc.vector.tensor_scalar(out=dst, in0=src.bitcast(FP8), scalar1=scale, scalar2=None, op0=MULT)
            note(("wide", k, g, t) for k in ((0, 1) if paired else (q,)))
            return True

        def place(q, g, b):
            if q < G - 1 or g >= 2:
                return G * q + g, b
            return (G * q, 2 * g + b) if b < 2 else (G * q + 1, 2 * (b - 2) + g)

        def mixed_tile(n):
            tag, depth = ("mixed_s", MIXED_S_BUFS) if n in TURN_P + (SCALAR_UNIT,) else ("mixed_g", 1) if n in HANDED_ON else ("mixed", MIXED_BUFS)
            if n not in mixed and slot_free(tag, depth):
                mixed[n] = take([P, W * T], BF16, f"mixed_{n}", tag, depth, [("codes", n, k) for k in range(T)])[:]
            return n in mixed

        def v_mixed_tile(sweep, g):
            tag, depth = ("last", 1) if (sweep, g) == (1, G - 1) else ("mixed_g", 1) if (sweep, g) == (1, 0) else ("v_mixed", V_MIXED_BUFS)
            if (sweep, g) not in v_mixed and slot_free(tag, depth):
                v_mixed[sweep, g] = take([P, C, T], BF16, f"v_mixed_{sweep}_{g}", tag, depth, [("v_codes", sweep, g, k) for k in range(T)])
            return (sweep, g) in v_mixed

        def interleave(engine, q, g, b0, b1):
            n, k = place(q, g, b0)
            if not ({("wide", q, g, t) for t in range(T)} <= done and mixed_tile(n)):
                return False
            copier[engine](
                out=mixed[n].rearrange("p (k m e t) -> p m k t e", k=T, e=2, t=T)[:, :, k : k + b1 - b0],
                in_=planes_of(q, g).rearrange("p t (m e b) -> p m b t e", e=2, b=T)[:, :, b0:b1],
            )
            note(("mixed",) + place(q, g, b) for b in range(b0, b1))
            return True

        def interleave_half(engine, n, half):
            q, g = divmod(n, G)
            if not ({("wide", q, g, t) for t in range(T)} <= done and mixed_tile(n)):
                return False
            if engine == "G":
                nc.gpsimd.tensor_scalar(
                    out=mixed[n].rearrange("p (b h m t) -> p h m b t", b=T, h=2, t=T)[:, half],
                    in0=planes_of(q, g).rearrange("p t (h m b) -> p h m b t", h=2, b=T)[:, half],
                    scalar1=1.0,
                    scalar2=0.0,
                    op0=MULT,
                    op1=ADD,
                )
            else:
                copier[engine](
                    out=mixed[n].rearrange("p (b h m e t) -> p h m b t e", b=T, h=2, e=2, t=T)[:, half],
                    in_=planes_of(q, g).rearrange("p t (h m e b) -> p h m b t e", h=2, e=2, b=T)[:, half],
                )
            done.add(("half", n, half))
            if ("half", n, 1 - half) in done:
                note(("mixed",) + place(q, g, b) for b in range(T))
            return True

        def interleave_tile(engine, b):
            q = G - 1
            n, k = place(q, 0, b)
            if not ({("wide", q, g, t) for g in range(2) for t in range(T)} <= done and mixed_tile(n)):
                return False
            copier[engine](
                out=mixed[n].rearrange("p (k m e t) -> p k m t e", k=T, e=2, t=T)[:, k : k + 2],
                in_=slots[q][:, :2, :, :W].rearrange("p g t (m e b) -> p b g m t e", e=2, b=T)[:, b],
            )
            note(("mixed", n, k + g) for g in range(2))
            return True

        def turn(engine, kind, n, h, u, bank):
            q, g = divmod(n, G)
            pair = (2 * u, 2 * u + 1)
            needs = {"p": {("wide", q, g, t) for t in pair}, "v": set(), "u": {("row", n, b, k) for b in pair for k in (2 * h, 2 * h + 1)}}[kind]
            if not needs <= done:
                return False
            if (kind, n, h) not in turned:
                if not slot_free(f"bank_{bank}", 1):
                    return False
                waits[f"bank_{bank}"].append({("emptied", kind, n, h)})
                turned[kind, n, h] = psum.tile([P, 2 * W], BF16, name=f"turn_{kind}{n}_{h}", tag=f"bank_{bank}")
            planes = planes_of(q, g) if kind == "p" else v_raw[:, n] if kind == "v" else v1_rows[n][:]
            if kind == "v":
                first = (2 * h + u) * P
                dst, src = turned[kind, n, h][:].rearrange("p (u c t) -> p u t c", u=2, t=T)[:, u], planes[:, :, first : first + P]
            else:
                tiles = T if kind == "p" else 1
                dst = turned[kind, n, h][:].rearrange("p (b m u t) -> p u t m b", b=tiles, u=2, t=2)[:, u]
                src = planes[:, 2 * u : 2 * u + 2, h * HALF : (h + 1) * HALF].rearrange("p t (m b) -> p t m b", b=tiles)
            nc.tensor.matmul(out=dst, lhsT=identity[:], rhs=src, start=True, stop=True)
            done.add(("pair", kind, n, h, u))
            if ("pair", kind, n, h, 1 - u) in done:
                done.add(("turned", kind, n, h))
            return True

        def empty(engine, kind, n, h):
            if ("turned", kind, n, h) not in done:
                return False
            words = turned[kind, n, h][:].bitcast(F32)
            if kind == "p":
                if not mixed_tile(n):
                    return False
                copier[engine](
                    out=mixed[n].bitcast(F32).rearrange("p (b h x) -> p h b x", b=T, h=2)[:, h],
                    in_=words.rearrange("p (b x) -> p b x", b=T),
                )
                done.add(("half", n, h))
                if ("half", n, 1 - h) in done:
                    note(("mixed", n, b) for b in range(T))
            else:
                sweep = 0 if kind == "v" else 1
                if not v_mixed_tile(sweep, n):
                    return False
                copier[engine](out=v_mixed[sweep, n][:].rearrange("p c t -> p (c t)").bitcast(F32)[:, h * W : (h + 1) * W], in_=words)
                note(("v_mixed", sweep, n, k) for k in (2 * h, 2 * h + 1))
            done.add(("emptied", kind, n, h))
            return True

        def quantise(engine, n, k0, k1):
            if not {("mixed", n, k) for k in range(k0, k1)} <= done:
                return False
            cols = slice(k0 * P, k1 * P)
            nc.vector.quantize_mx(
                out=p_codes[:, n, cols].bitcast(FP8X4),
                scales=p_scales[:, n, cols],
                in_=mixed[n][:, k0 * P * T : k1 * P * T],
            )
            note(("codes", n, k) for k in range(k0, k1))
            return True

        def interleave_v(engine, g, c0, c1):
            needs = {("row", g, b, k) for b in range(T) for k in quarters(c0, c1)}
            if not (needs <= done and v_mixed_tile(1, g)):
                return False
            src = v1_rows[g][:]
            if engine == "G":
                nc.gpsimd.tensor_scalar(
                    out=v_mixed[1, g][:, c0:c1, :],
                    in0=src[:, :, c0:c1].rearrange("p t c -> p c t"),
                    scalar1=1.0,
                    scalar2=0.0,
                    op0=MULT,
                    op1=ADD,
                )
            else:
                copier[engine](
                    out=v_mixed[1, g][:, c0:c1, :].rearrange("p (c i) t -> p c t i", i=4),
                    in_=src[:, :, c0:c1].rearrange("p t (c i) -> p c t i", i=4),
                )
            note(("v_mixed", 1, g, k) for k in quarters(c0, c1))
            return True

        def quantise_v(engine, sweep, g, c0, c1):
            if not {("v_mixed", sweep, g, k) for k in quarters(c0, c1)} <= done:
                return False
            nc.vector.quantize_mx(
                out=v_codes[sweep][:, g, c0:c1].bitcast(FP8X4),
                scales=v_scales[sweep][:, g, c0:c1],
                in_=v_mixed[sweep, g][:, c0:c1, :].rearrange("p c t -> p (c t)"),
            )
            note(("v_codes", sweep, g, k) for k in quarters(c0, c1))
            return True

        def multiply(engine, sweep, tile, g, bank=None, close=False, c0=0, c1=C):
            q, b = divmod(tile, T)
            n, k = place(q, g, b)
            needs = {("codes", n, k)} | {("v_codes", sweep, g, j) for j in quarters(c0, c1)}
            if not (needs <= done and (bank is None or slot_free(f"bank_{bank}", 1))):
                return False
            if bank is not None:
                if sweep == 0:
                    freed = {("row", q, b, j) for j in range(T)}
                else:
                    freed = {("parked", tile) if g == 0 and tile in EXITS else ("result", tile, c0)}
                waits[f"bank_{bank}"].append(freed)
                acc[sweep, tile, c0] = psum.tile([P, c1 - c0], F32, name=f"acc_{sweep}_{tile}", tag=f"bank_{bank}")
            cols = slice(k * P, (k + 1) * P)
            nc.tensor.matmul_mx(
                out=acc[sweep, tile, c0][:],
                lhsT=p_codes[:, n, cols].bitcast(FP8X4),
                lhsT_scale=p_scales[:, n, cols],
                rhs=v_codes[sweep][:, g, c0:c1].bitcast(FP8X4),
                rhs_scale=v_scales[sweep][:, g, c0:c1],
                start=bank is not None,
                stop=close,
            )
            if close:
                done.add(("sum", sweep, tile, g, c0))
            return True

        def update(dst, sums, q, b, addend):
            nc.vector.scalar_tensor_tensor(out=dst, in0=sums, scalar=disc[:, q, b : b + 1], in1=addend, op0=MULT, op1=ADD)

        def update_v1(engine, tile, c0, c1):
            q, b = divmod(tile, T)
            if ("sum", 0, tile, G - 1, 0) not in done:
                return False
            if q not in v1_rows:
                if not slot_free("v1_rows", 2):
                    return False
                v1_rows[q] = take([P, T, C], BF16, f"v1_rows_{q}", "v1_rows", 2, [("v_mixed", 1, q, k) for k in range(T)])
            update(v1_rows[q][:, b, c0:c1], acc[0, tile, 0][:, c0:c1], q, b, r_sb[:, q, b, c0:c1])
            note(("row", q, b, k) for k in quarters(c0, c1))
            return True

        def widen_discount(engine):
            nc.scalar.copy(out=disc32[:], in_=disc[:])
            done.add(("disc32",))
            return True

        def park(engine, tile):
            if not {("sum", 1, tile, EXITS[tile], 0), ("disc32",)} <= done:
                return False
            q, b = divmod(tile, T)
            parked[tile] = stream.tile([P, C], F32, name=f"parked_{tile}", tag="parked", bufs=len(EXITS))[:]
            if engine == "V":
                update(parked[tile], acc[1, tile, 0][:], q, b, r_sb[:, q, b])
                done.add(("rewarded", tile))
            else:
                nc.scalar.activation(out=parked[tile], in_=acc[1, tile, 0][:], func=COPY, scale=disc32[:, q, b : b + 1])
            done.add(("parked", tile))
            return True

        def add_reward(engine, tile):
            if ("parked", tile) not in done:
                return False
            q, b = divmod(tile, T)
            if engine == "V":
                if not slot_free("last", 1):
                    return False
                dst = take([P, C], F32, "late", "last", 1, [])[:]
                nc.vector.tensor_tensor(out=dst, in0=parked[tile], in1=r_sb[:, q, b], op=ADD)
                parked["spare"] = parked[tile]
            else:
                if "spare" not in parked:
                    return False
                dst = parked["spare"] if tile == 0 else parked[tile]
                nc.gpsimd.tensor_tensor(out=dst, in0=parked[tile], in1=r_sb[:, q, b], op=ADD)
            parked[tile] = dst
            done.add(("rewarded", tile))
            return True

        finished = []

        def finish(engine, tile, c0=0, c1=C, first=0):
            needs = {("sum", 1, tile, G - 1, first)} | ({("rewarded", tile)} if tile in EXITS else set())
            if not needs <= done:
                return False
            q, b = divmod(tile, T)
            if tile not in finished:
                finished.append(tile)
            half, place = divmod(finished.index(tile), 2 * T)
            if half not in results:
                if not slot_free("wide", WIDE_BUFS):
                    return False
                results[half] = take([P, 2 * T, C], F32, f"results_{half}", "wide", WIDE_BUFS, [])
            dst = results[half][:, place, c0:c1]
            addend = parked[tile][:, c0:c1] if tile in EXITS else r_sb[:, q, b, c0:c1]
            update(dst, acc[1, tile, first][:, c0 - first : c1 - first], q, b, addend)
            if tile in JOINED:
                nc.sync.dma_start(out=out_view[q][:, b - 1 : b + 1], in_=results[half][:, place - 1 : place + 1])
            elif tile + 1 not in JOINED:
                nc.sync.dma_start(out=out_view[q][:, b, c0:c1], in_=dst)
            done.add(("result", tile, c0))
            return True

        def wd(q, g, ts=range(T)):
            return [(widen, q, g, t, q < 2) for t in ts]

        def wd1(q, g, ts):
            return [(widen, q, g, t, False) for t in ts]

        def ilh(n, half):
            return [(interleave_half, n, half)]

        def ev(kind, n, hs=range(2)):
            return [(empty, kind, n, h) for h in hs]

        def il(n, b0=0, b1=T):
            return [(interleave, n // G, n % G, b0, b1)]

        def ilt(b):
            return [(interleave_tile, b)]

        def qp(n, k0=0, k1=T):
            return [(quantise, n, k0, k1)]

        def upd(tiles, c0=0, c1=C):
            return [(update_v1, tile, c0, c1) for tile in tiles]

        def ilv(g, c0=0, c1=C):
            return [(interleave_v, g, c0, c1)]

        def qv(sweep, g, c0=0, c1=C):
            return [(quantise_v, sweep, g, c0, c1)]

        def tn(kind, n, bank, hs=range(2)):
            return [(turn, kind, n, h, u, bank + k) for k, h in enumerate(hs) for u in range(2)]

        def tn_pairs(kind, n, bank, us=range(2)):
            return [(turn, kind, n, h, u, bank + h) for u in us for h in range(2)]

        def mx1(tiles, gs, bank=None):
            return [(multiply, 0, tile, g, bank + j if g == 0 else None, g == G - 1) for g in gs for j, tile in enumerate(tiles)]

        def mx2(tile, gs, bank=None, c0=0, c1=C):
            return [(multiply, 1, tile, g, bank if g == gs[0] else None, g == G - 1 or g == EXITS.get(tile), c0, c1) for g in gs]

        scalar = wd1(1, 0, [1, 2, 3]) + wd(0, 1, [1, 2]) + ev("p", 4) + wd(0, 2, [0]) + ev("p", 5) + wd(0, 2, [1]) + ev("v", 0) + wd(0, 3, [0]) + ev("v", 1) + wd(0, 3, [1]) + ev("v", 2) + wd(2, 0, [0]) + ev("v", 3) + wd(2, 0, [1, 2, 3])
        scalar = scalar + wd(2, 1) + wd(2, 2) + wd(2, 3) + wd(3, 0, [0]) + ilv(0, HALF, C) + wd(3, 0, [1, 2, 3]) + [(widen_discount,)] + wd(3, 1, [0]) + ev("u", 1) + wd(3, 1, [1, 2, 3]) + [(park, 0), (park, 1)] + wd(3, 2, [0]) + [(park, 2), (park, 3)]
        scalar = scalar + ilt(2) + wd(3, 3, [0, 1]) + ilt(3) + il(15, 3, 4) + [(park, 12)] + ilv(2) + ilv(3, HALF, C)

        vector = wd1(1, 0, [0]) + wd1(0, 0, range(T)) + il(0) + wd(0, 1, [0]) + qp(0) + wd(0, 1, [3]) + wd(0, 2, [2]) + il(1) + wd(0, 2, [3]) + qp(4) + qp(1) + wd(0, 3, [3, 2]) + qp(5) + il(2) + qv(0, 0) + il(6) + qv(0, 1) + qp(2)
        vector = vector + il(3) + qv(0, 2) + qp(3) + il(7) + qv(0, 3) + qp(6) + il(8) + qp(7) + qp(8) + upd(range(4)) + ilh(9, 1) + il(10, 0, 2) + qp(9) + upd(range(4, 8))
        vector = vector + il(10, 2, 4) + qv(1, 0) + qp(10) + il(11) + qv(1, 1) + qp(11) + il(12, 0, 2) + il(13, 0, 2) + wd(3, 2, [1]) + qp(12) + wd(3, 2, [2, 3]) + upd(range(8, 12))
        vector = vector + ilh(14, 1) + qp(13, 0, 2) + wd(3, 3, [2, 3]) + qp(14, 0, 2) + il(15, 0, 3) + qp(14, 2, 4) + qp(15, 0, 2) + qp(13, 2, 4) + qp(15, 2, 4) + upd([12, 13, 14])
        vector = vector + upd([15], HALF, C) + upd([15], 0, HALF) + qv(1, 2) + ilv(3, 0, HALF) + qv(1, 3, HALF, C) + qv(1, 3, 0, HALF) + [(add_reward, 12)]
        order = [8, 9, 10, 11, 4, 5, 6, 7, 12, 0, 13, 1, 2, 14, 3]
        pieces = [(0, HALF), (HALF, C)]
        vector = vector + [(finish, tile) for tile in order] + [(finish, 15, c0, c1, c0) for c0, c1 in pieces]

        gpsimd = ilh(9, 0) + ilv(0, 0, HALF) + ilh(14, 0) + [(add_reward, tile) for tile in range(4)]

        every = list(range(G))
        tensor = tn_pairs("p", 4, 4) + tn_pairs("p", 5, 6) + tn("v", 0, 0) + tn("v", 1, 2) + tn("v", 2, 4) + tn("v", 3, 6) + mx1(range(4), every, 0) + mx1(range(4, 8), [0, 1], 4)
        tensor = tensor + mx1(range(4, 8), [2, 3]) + mx1(range(8, 12), [0, 1], 0) + tn_pairs("u", 1, 4) + mx2(0, [0], 6) + mx2(1, [0], 7) + mx1(range(8, 12), [2]) + mx2(2, [0], 4) + mx2(3, [0], 5)
        tensor = tensor + mx2(0, [1]) + mx2(1, [1]) + mx2(2, [1]) + mx2(3, [1]) + mx1(range(8, 12), [3])
        tensor = tensor + mx2(8, [0, 1], 6) + mx2(9, [0, 1], 7) + mx2(10, [0, 1], 4) + mx2(11, [0, 1], 5)
        tensor = tensor + mx1([12, 13], [0, 1], 0) + mx2(12, [0, 1], 3) + mx1([14], [0, 1], 2) + mx1([12, 13, 14], [2]) + mx1([12, 13, 14], [3]) + mx1([15], every, 3) + mx2(4, [0, 1], 0) + mx2(5, [0, 1], 1) + mx2(6, [0, 1], 2) + mx2(7, [0, 1], 3)
        for tile in order[:3]:
            tensor = tensor + mx2(tile, [2])
        for k, tile in enumerate(order[:8]):
            tensor = tensor + mx2(tile, [3]) + [step for later in order[3 + k : 8][:1] for step in mx2(later, [2])]
        for tile, bank in zip(order[8:], [6, 7, 4, 5, 0, 1, 2]):
            tensor = tensor + mx2(tile, [2, 3] if tile in EXITS else every, bank)
        for (c0, c1), bank in zip(pieces, [3, 6, 7]):
            tensor = tensor + mx2(15, every, bank, c0, c1)


        queues = {"S": scalar, "V": vector, "T": tensor, "G": gpsimd}
        at = {engine: 0 for engine in queues}
        while any(at[engine] < len(queues[engine]) for engine in queues):
            moved = False
            for engine, steps in queues.items():
                while at[engine] < len(steps) and steps[at[engine]][0](engine, *steps[at[engine]][1:]):
                    at[engine] = at[engine] + 1
                    moved = True
            assert moved, [steps[at[engine]] for engine, steps in queues.items() if at[engine] < len(steps)]
